import numpy as np
import ml_dtypes


def mxq(x, axis, fmt="e4m3"):
    dtype, down = {"e4m3": (ml_dtypes.float8_e4m3fn, 7), "e5m2": (ml_dtypes.float8_e5m2, 14)}[fmt]
    v = np.moveaxis(np.asarray(x, np.float32).astype(ml_dtypes.bfloat16).astype(np.float64), axis, -1)
    blocks = v.reshape(v.shape[:-1] + (-1, 32))
    amax = np.abs(blocks).max(-1, keepdims=True)
    byte = np.maximum(np.where(amax > 0, np.frexp(amax)[1] - 1 + 127, 0) - down, 1)
    scale = np.exp2(byte - 127.0)
    codes = (blocks / scale).astype(np.float32).astype(dtype).astype(np.float64)
    return np.moveaxis((codes * scale).reshape(v.shape), -1, axis)


WIDE = False


def mx_kscale(k):
    if not WIDE:
        return np.ones(k)
    levels = np.array([10, -10, 5, -5, 0])
    if k % 512:
        return np.exp2(np.random.permutation(np.resize(levels, k // 32))).repeat(32)
    a = np.empty((k // 512, 16))
    for p in range(k // 512):
        a[p, :8] = np.random.permutation(np.resize(levels, 8))
        for g in range(8):
            far = levels[np.abs(levels - a[p, g]) >= 10]
            a[p, g + 8] = far[np.random.randint(len(far))]
    return np.exp2(a.ravel()).repeat(32)


def f64(x):
    return np.asarray(x).astype(np.float64)


def striped(idx):
    return np.tile(idx.reshape(-1, 16).T, (8, 1)).astype(np.uint16)


def unstriped(offs):
    return offs[:16].T.reshape(-1).astype(np.int64)


def pack_weight(w):
    k, n = w.shape
    w = f64(np.asarray(w, np.float32).astype(ml_dtypes.bfloat16)).reshape(k // 32, 32, n)
    amax = np.abs(w).max(1)
    byte = np.clip(np.where(amax > 0, np.frexp(amax)[1] - 1 + 127 - 7, 1), 1, 254)
    scaled = (w * np.exp2(127.0 - byte)[:, None, :]).reshape(k, n).astype(np.float32)
    words = np.ascontiguousarray(scaled.reshape(k // 512, 128, 4, n).transpose(0, 1, 3, 2)).astype(ml_dtypes.float8_e4m3fn).view(np.uint8)
    return words, np.ascontiguousarray(byte.astype(np.uint8).reshape(k // 512, 16, n))


def unpack_weight(words, scales):
    g, p, n, _ = words.shape
    vals = np.ascontiguousarray(words).view(ml_dtypes.float8_e4m3fn).astype(np.float64) * np.repeat(np.exp2(scales.astype(np.float64) - 127.0), 8, axis=1)[..., None]
    return vals.transpose(0, 1, 3, 2).reshape(g * 512, n)


def relu(v):
    return np.maximum(v, 0.0)


K, T, H, N = 1024, 512, 512, 128


def setup_inputs():
    n = np.random.standard_normal
    s = mx_kscale(K)[:, None]
    u = mx_kscale(H)
    packed_xT = pack_weight(n((K, T)) * s)
    packed_w3 = pack_weight(n((H, N)) / np.sqrt(H) / u[:, None])
    return {
        "x_words": packed_xT[0],
        "x_scales": packed_xT[1],
        "w1": (n((K, H)) / np.sqrt(2 * K) / s * u).astype(np.float32),
        "w2": (n((K, H)) / np.sqrt(2 * K) / s * u).astype(np.float32),
        "w3_words": packed_w3[0],
        "w3_scales": packed_w3[1],
        "pos1": striped(np.random.permutation(T)),
        "pos2": striped(np.random.permutation(T)),
        "pos3": striped(np.random.permutation(T)),
        "pos4": striped(np.random.permutation(T)),
    }


def reference(x_words, x_scales, w1, w2, w3_words, w3_scales, pos1, pos2, pos3, pos4):
    xq = unpack_weight(x_words, x_scales)
    y = mxq(f64(w1), 0, "e4m3").T @ xq
    e = mxq(f64(w2), 0, "e4m3").T @ xq
    z = np.maximum(np.maximum(np.maximum(relu(y + e[:, unstriped(pos1)]), relu(y + e[:, unstriped(pos2)])), relu(y + e[:, unstriped(pos3)])), relu(y + e[:, unstriped(pos4)]))
    return unpack_weight(w3_words, w3_scales).T @ mxq(z, 0, "e4m3")

@@ -1,0 +1,267 @@
+from contextlib import ExitStack
+
+import concourse.mybir as mybir
+from concourse.masks import make_identity
+
+K, T, H, N = 1024, 512, 512, 128
+FLOPS = 2 * (2 * K * H * T + H * N * T)
+
+F32 = mybir.dt.float32
+BF16 = mybir.dt.bfloat16
+I32 = mybir.dt.int32
+U32 = mybir.dt.uint32
+U16 = mybir.dt.uint16
+U8 = mybir.dt.uint8
+FP8X4 = mybir.dt.float8_e4m3fn_x4
+ALU = mybir.AluOpType
+RELU = mybir.ActivationFunctionType.Relu
+
+P = 128
+PACK = 4
+K_PASS = P * PACK
+PASSES = K // K_PASS
+TILES = H // P
+HALVES = 2
+HALF = T // HALVES
+BLOCKS = HALF // P
+LIST_COLS = HALF // 16
+
+
+def tile_picked_wedgecv_relu_l_kernel(
+    tc, x_words, x_scales, w1, w2, w3_words, w3_scales, pos1, pos2, pos3, pos4, out
+):
+    nc = tc.nc
+    with ExitStack() as ctx:
+        keep = ctx.enter_context(tc.tile_pool(name="keep", bufs=1))
+        psum = ctx.enter_context(tc.psum_pool(name="psum", bufs=2))
+        psum_sums = ctx.enter_context(tc.psum_pool(name="psum_sums", bufs=3))
+
+        raw = {}
+
+        def load_weights(label, w, h):
+            for z in range(PASSES):
+                raw[label, h, z] = keep.tile([P, PACK, P], F32, name=f"raw_{label}_{h}_{z}")
+                rows = w[z * K_PASS : (z + 1) * K_PASS, h * P : (h + 1) * P]
+                nc.sync.dma_start(out=raw[label, h, z][:], in_=rows.rearrange("(p j) c -> p j c", j=PACK))
+
+        def load_scale_rows(queue, plane, scales):
+            passes = scales.shape[0]
+            nc.vector.memset(plane[:].bitcast(I32), 0)
+            for q in range(4):
+                queue.dma_start(
+                    out=plane[32 * q : 32 * q + 4 * passes, :].bitcast(I32),
+                    in_=scales[:, 4 * q : 4 * q + 4, :].bitcast(I32),
+                )
+
+        x_plane = keep.tile([P, T], U8, align_bytes=64)
+        load_scale_rows(nc.scalar, x_plane, x_scales)
+
+        load_weights("e", w2, 0)
+        x_codes = []
+        for z in range(PASSES):
+            x_codes.append(keep.tile([P, T], U32, name=f"x_codes_{z}", align_bytes=64))
+            nc.sync.dma_start(
+                out=x_codes[z][:].bitcast(I32),
+                in_=x_words[z].rearrange("p c r -> p (c r)").bitcast(I32),
+            )
+        lists = {}
+        for d, pos in ((2, pos2), (4, pos4), (1, pos1), (3, pos3)):
+            lists[d] = keep.tile([P, T // 16], U16, name=f"list_{d}")
+            nc.sync.dma_start(lists[d][:], pos)
+        for label, h in (("e", 1), ("y", 0), ("y", 1), ("e", 2), ("y", 2), ("e", 3), ("y", 3)):
+            load_weights(label, w2 if label == "e" else w1, h)
+        w3_codes = keep.tile([P, N], U32, align_bytes=64)
+        nc.sync.dma_start(out=w3_codes[:].bitcast(I32), in_=w3_words[0].rearrange("p c r -> p (c r)").bitcast(I32))
+        w3_plane = keep.tile([P, N], U8, align_bytes=64)
+        load_scale_rows(nc.sync, w3_plane, w3_scales)
+
+        ident = keep.tile([P, P], F32)
+        make_identity(nc, ident[:])
+        warm = keep.tile([P, 1], F32)
+        nc.scalar.activation(warm[:], ident[:, 0:1], RELU)
+
+        grouped, codes, planes, accs, results = {}, {}, {}, {}, {}
+
+        def cast(key, engine_copy):
+            label, h = key
+            grouped[key] = keep.tile([P, PASSES, P, PACK], BF16, name=f"grouped_{label}_{h}", align_bytes=64)
+            for z in range(PASSES):
+                engine_copy(
+                    out=grouped[key][:, z, :, :].rearrange("p (c i) t -> p c t i", i=4),
+                    in_=raw[label, h, z][:].rearrange("p t (c i) -> p c t i", i=4),
+                )
+
+        def quantize(key, pieces):
+            label, h = key
+            codes[key] = keep.tile([P, PASSES * P], U32, name=f"codes_{label}_{h}", align_bytes=64)
+            planes[key] = keep.tile([P, PASSES * P], U8, name=f"plane_{label}_{h}", align_bytes=64)
+            values = grouped[key][:].rearrange("p z c t -> p (z c t)")
+            width = PASSES * P // pieces
+            for i in range(pieces):
+                cols = slice(i * width, (i + 1) * width)
+                nc.vector.quantize_mx(
+                    out=codes[key][:, cols].bitcast(FP8X4),
+                    scales=planes[key][:, cols],
+                    in_=values[:, i * width * PACK : (i + 1) * width * PACK],
+                )
+
+        def multiply(key):
+            accs[key] = psum.tile([P, T], F32, name="acc")
+            for z in range(PASSES):
+                cols = slice(z * P, (z + 1) * P)
+                nc.tensor.matmul_mx(
+                    out=accs[key][:],
+                    lhsT=codes[key][:, cols].bitcast(FP8X4),
+                    lhsT_scale=planes[key][:, cols],
+                    rhs=x_codes[z][:].bitcast(FP8X4),
+                    rhs_scale=x_plane[4 * z :, :],
+                    start=(z == 0),
+                    stop=(z == PASSES - 1),
+                )
+
+        def unload(key):
+            label, h = key
+            results[key] = keep.tile([P, T], F32, name=f"result_{label}_{h}")
+            nc.scalar.copy(out=results[key][:], in_=accs[key][:])
+
+        units = [(h, u * HALF, HALF) for h in range(TILES) for u in range(HALVES)][:-1]
+        units = units + [(TILES - 1, HALF, P), (TILES - 1, HALF + P, P)]
+        before_base = {1: ("e", 1), 3: ("e", 2), 4: ("y", 2), 5: ("e", 3), 6: ("y", 3)}
+        before_diff = {1: ("y", 0), 2: ("y", 1)}
+        base_a, base_b, diff_a, diff_b, gain_a, gain_b, sum_a, sum_b, relu_a = ({} for i in range(9))
+
+        def fresh(name, n):
+            return keep.tile([P, units[n][2]], F32, name=f"{name}_{n}")[:]
+
+        def over_raw(key, n):
+            return raw[key[0], key[1], PASSES - 1][:].rearrange("p t c -> p (t c)")[:, : units[n][2]]
+
+        def offsets(d, n):
+            h, v0, width = units[n]
+            return lists[d][:, v0 // 16 : (v0 + width) // 16]
+
+        def gather_bases(n):
+            h, v0, width = units[n]
+            e = results["e", h]
+            if n in before_base:
+                base_a[n] = over_raw(before_base[n], n)
+            elif n == 7:
+                base_a[n] = base_b[5][:, :width]
+            else:
+                base_a[n] = fresh("base_a", n)
+            base_b[n] = fresh("base_b", n)
+            nc.vector.tensor_copy(base_a[n], e[:].indirect(offsets(2, n)))
+            nc.vector.tensor_copy(base_b[n], e[:].indirect(offsets(4, n)))
+
+        def gather_diffs(n):
+            h, v0, width = units[n]
+            e = results["e", h]
+            if n in before_diff:
+                diff_a[n] = over_raw(before_diff[n], n)
+            elif n == 8:
+                diff_a[n] = base_b[6][:, :width]
+            else:
+                diff_a[n] = fresh("diff_a", n)
+            diff_b[n] = fresh("diff_b", n)
+            nc.vector.tensor_tensor(diff_a[n], e[:].indirect(offsets(1, n)), base_a[n], ALU.subtract)
+            nc.vector.tensor_tensor(diff_b[n], e[:].indirect(offsets(3, n)), base_b[n], ALU.subtract)
+
+        def gain(gains, diffs, name, n):
+            gains[n] = fresh(name, n)
+            nc.scalar.activation(gains[n], diffs[n], RELU)
+
+        def pair_sum(sums, bases, gains, name, n):
+            h, v0, width = units[n]
+            sums[n] = psum_sums.tile([P, width // P, P], F32, name=name)
+            for b in range(width // P):
+                own = slice(b * P, (b + 1) * P)
+                terms = (results["y", h][:, v0 + b * P : v0 + (b + 1) * P], bases[n][:, own], gains[n][:, own])
+                for i, term in enumerate(terms):
+                    nc.tensor.matmul(
+                        sums[n][:, b, :], term, ident[:], start=(i == 0), stop=(i == len(terms) - 1), is_transpose=True
+                    )
+
+        def clip(n):
+            relu_a[n] = fresh("relu_a", n).rearrange("p (b c) -> p b c", c=P)
+            nc.scalar.activation(relu_a[n], sum_a[n][:], RELU)
+
+        z_tile = keep.tile([P, T // P * H], BF16)
+        z_rows = z_tile[:].rearrange("p (b c) -> p b c", c=H)
+
+        def largest(n):
+            h, v0, width = units[n]
+            nc.vector.tensor_tensor(
+                z_rows[:, v0 // P : (v0 + width) // P, h * P : (h + 1) * P], relu_a[n], sum_b[n][:], ALU.max
+            )
+
+        def project(n):
+            h, v0, width = units[n]
+            blocks = width // P
+            turned = psum.tile([P, blocks, 2, P], F32, name="acc")
+            for b in range(blocks):
+                pairs = z_rows[:, v0 // P + b, :].bitcast(F32)
+                for s in range(2):
+                    nc.tensor.transpose(turned[:, b, s, :], pairs[:, s : H // 2 : 2], ident[:])
+            z_grouped = keep.tile([P, width * PACK], BF16, name=f"z_grouped_{n}", align_bytes=64)
+            nc.scalar.copy(
+                out=z_grouped[:].bitcast(F32).rearrange("p (b r s) -> p b r s", b=blocks, s=2),
+                in_=turned[:].rearrange("p b s r -> p b r s"),
+            )
+            z_codes = keep.tile([P, width], U32, name=f"z_codes_{n}", align_bytes=64)
+            z_plane = keep.tile([P, width], U8, name=f"z_plane_{n}", align_bytes=64)
+            nc.vector.quantize_mx(out=z_codes[:].bitcast(FP8X4), scales=z_plane[:], in_=z_grouped[:])
+            projected = psum.tile([P, width], F32, name="acc")
+            nc.tensor.matmul_mx(
+                out=projected[:],
+                lhsT=w3_codes[:].bitcast(FP8X4),
+                lhsT_scale=w3_plane[:],
+                rhs=z_codes[:].bitcast(FP8X4),
+                rhs_scale=z_plane[:],
+                start=True,
+                stop=True,
+            )
+            staged = keep.tile([P, width], F32, name=f"staged_{n}")
+            nc.scalar.copy(out=staged[:], in_=projected[:])
+            nc.sync.dma_start(out=out[:, v0 : v0 + width], in_=staged[:])
+
+        cast(("e", 0), nc.vector.tensor_copy)
+        quantize(("e", 0), PASSES)
+        multiply(("e", 0))
+        unload(("e", 0))
+        summed = 0
+        for n in range(len(units)):
+            if n >= 2 and n != 8:
+                largest(n - 2)
+            if n in before_base:
+                quantize(before_base[n], 1)
+            gather_bases(n)
+            if n in before_diff:
+                quantize(before_diff[n], 1)
+            if n == 8:
+                largest(6)
+            gather_diffs(n)
+            if n in before_base:
+                multiply(before_base[n])
+            if n in before_diff:
+                multiply(before_diff[n])
+            if n + 1 in before_base:
+                cast(before_base[n + 1], nc.scalar.copy)
+            if n in before_base:
+                unload(before_base[n])
+            if n + 1 in before_diff:
+                cast(before_diff[n + 1], nc.scalar.copy)
+            gain(gain_a, diff_a, "gain_a", n)
+            if n in before_diff:
+                unload(before_diff[n])
+            gain(gain_b, diff_b, "gain_b", n)
+            if n == 8:
+                project(6)
+            if n >= 1:
+                for m in range(summed, n + 1):
+                    pair_sum(sum_a, base_a, gain_a, "sum_a", m)
+                    pair_sum(sum_b, base_b, gain_b, "sum_b", m)
+                    clip(m)
+                summed = n + 1
+        for n in (7, 8):
+            largest(n)
+            project(n)

@@ -34,7 +34,7 @@ def tile_picked_wedgecv_relu_l_kernel(
     with ExitStack() as ctx:
         keep = ctx.enter_context(tc.tile_pool(name="keep", bufs=1))
         psum = ctx.enter_context(tc.psum_pool(name="psum", bufs=2))
-        psum_sums = ctx.enter_context(tc.psum_pool(name="psum_sums", bufs=3))
+        psum_sums = ctx.enter_context(tc.psum_pool(name="psum_sums", bufs=4))
 
         raw = {}
 
@@ -46,7 +46,7 @@ def tile_picked_wedgecv_relu_l_kernel(
 
         def load_scale_rows(queue, plane, scales):
             passes = scales.shape[0]
-            nc.vector.memset(plane[:].bitcast(I32), 0)
+            nc.gpsimd.memset(plane[:].bitcast(I32), 0)
             for q in range(4):
                 queue.dma_start(
                     out=plane[32 * q : 32 * q + 4 * passes, :].bitcast(I32),
@@ -65,7 +65,7 @@ def tile_picked_wedgecv_relu_l_kernel(
                 in_=x_words[z].rearrange("p c r -> p (c r)").bitcast(I32),
             )
         lists = {}
-        for d, pos in ((2, pos2), (4, pos4), (1, pos1), (3, pos3)):
+        for d, pos in ((4, pos4), (1, pos1), (2, pos2), (3, pos3)):
             lists[d] = keep.tile([P, T // 16], U16, name=f"list_{d}")
             nc.sync.dma_start(lists[d][:], pos)
         for label, h in (("e", 1), ("y", 0), ("y", 1), ("e", 2), ("y", 2), ("e", 3), ("y", 3)):
@@ -82,13 +82,13 @@ def tile_picked_wedgecv_relu_l_kernel(
 
         grouped, codes, planes, accs, results = {}, {}, {}, {}, {}
 
-        def cast(key, engine_copy):
+        def cast(key, copies):
             label, h = key
             grouped[key] = keep.tile([P, PASSES, P, PACK], BF16, name=f"grouped_{label}_{h}", align_bytes=64)
             for z in range(PASSES):
-                engine_copy(
-                    out=grouped[key][:, z, :, :].rearrange("p (c i) t -> p c t i", i=4),
-                    in_=raw[label, h, z][:].rearrange("p t (c i) -> p c t i", i=4),
+                copies[z](
+                    out=grouped[key][:, z, :, :].rearrange("p (s q e) j -> p q j s e", s=2, e=2),
+                    in_=raw[label, h, z][:].rearrange("p j (q s e) -> p q j s e", s=2, e=2),
                 )
 
         def quantize(key, pieces):
@@ -119,97 +119,111 @@ def tile_picked_wedgecv_relu_l_kernel(
                     stop=(z == PASSES - 1),
                 )
 
+        def first_product(key):
+            halves = [psum.tile([P, HALF], F32, name="acc") for u in range(HALVES)]
+            for z in range(PASSES):
+                cols = slice(z * P, (z + 1) * P)
+                for u in range(HALVES):
+                    points = slice(u * HALF, (u + 1) * HALF)
+                    nc.tensor.matmul_mx(
+                        out=halves[u][:],
+                        lhsT=codes[key][:, cols].bitcast(FP8X4),
+                        lhsT_scale=planes[key][:, cols],
+                        rhs=x_codes[z][:, points].bitcast(FP8X4),
+                        rhs_scale=x_plane[4 * z :, points],
+                        start=(z == 0),
+                        stop=(z == PASSES - 1),
+                    )
+            results[key] = keep.tile([P, T], F32, name="result_first")
+            nc.scalar.copy(out=results[key][:, :HALF], in_=halves[0][:])
+            nc.vector.tensor_copy(out=results[key][:, HALF:], in_=halves[1][:])
+
         def unload(key):
             label, h = key
             results[key] = keep.tile([P, T], F32, name=f"result_{label}_{h}")
             nc.scalar.copy(out=results[key][:], in_=accs[key][:])
 
-        units = [(h, u * HALF, HALF) for h in range(TILES) for u in range(HALVES)][:-1]
-        units = units + [(TILES - 1, HALF, P), (TILES - 1, HALF + P, P)]
-        before_base = {1: ("e", 1), 3: ("e", 2), 4: ("y", 2), 5: ("e", 3), 6: ("y", 3)}
-        before_diff = {1: ("y", 0), 2: ("y", 1)}
-        base_a, base_b, diff_a, diff_b, gain_a, gain_b, sum_a, sum_b, relu_a = ({} for i in range(9))
+        last = TILES - 1
+        units = [(h, u * HALF, HALF) for h in range(last) for u in range(HALVES)]
+        units = units + [(last, b * P, P) for b in range(T // P)]
+        z_rows = [keep.tile([P, H], BF16, name=f"z_rows_{b}") for b in range(T // P)]
+        base, diffs, gain, totals = {}, {}, {}, {}
 
-        def fresh(name, n):
-            return keep.tile([P, units[n][2]], F32, name=f"{name}_{n}")[:]
+        def raw_bytes(label, h):
+            return raw[label, h, PASSES - 1][:].rearrange("p t c -> p (t c)")
 
-        def over_raw(key, n):
-            return raw[key[0], key[1], PASSES - 1][:].rearrange("p t c -> p (t c)")[:, : units[n][2]]
+        reused = {("base", 2 * h): raw_bytes("y", h) for h in range(1, TILES)}
+        reused.update({("diff1", 2 * h - 1): raw_bytes("e", h) for h in range(1, TILES)})
+        reused["diff3", 8] = z_rows[0][:].bitcast(F32)
+        reused["base", 9] = z_rows[0][:].bitcast(F32)[:, P:]
+        reused["diff3", 9] = z_rows[1][:].bitcast(F32)
 
-        def offsets(d, n):
+        def buffer(name, n):
+            width = units[n][2]
+            if (name, n) in reused:
+                return reused[name, n][:, :width]
+            return keep.tile([P, width], F32, name=f"{name}_{n}")[:]
+
+        def looked_up(d, n):
             h, v0, width = units[n]
-            return lists[d][:, v0 // 16 : (v0 + width) // 16]
+            return results["e", h][:].indirect(lists[d][:, v0 // 16 : (v0 + width) // 16])
 
-        def gather_bases(n):
-            h, v0, width = units[n]
-            e = results["e", h]
-            if n in before_base:
-                base_a[n] = over_raw(before_base[n], n)
-            elif n == 7:
-                base_a[n] = base_b[5][:, :width]
-            else:
-                base_a[n] = fresh("base_a", n)
-            base_b[n] = fresh("base_b", n)
-            nc.vector.tensor_copy(base_a[n], e[:].indirect(offsets(2, n)))
-            nc.vector.tensor_copy(base_b[n], e[:].indirect(offsets(4, n)))
+        def gather_base(n):
+            base[n] = buffer("base", n)
+            nc.vector.tensor_copy(base[n], looked_up(4, n))
 
         def gather_diffs(n):
-            h, v0, width = units[n]
-            e = results["e", h]
-            if n in before_diff:
-                diff_a[n] = over_raw(before_diff[n], n)
-            elif n == 8:
-                diff_a[n] = base_b[6][:, :width]
-            else:
-                diff_a[n] = fresh("diff_a", n)
-            diff_b[n] = fresh("diff_b", n)
-            nc.vector.tensor_tensor(diff_a[n], e[:].indirect(offsets(1, n)), base_a[n], ALU.subtract)
-            nc.vector.tensor_tensor(diff_b[n], e[:].indirect(offsets(3, n)), base_b[n], ALU.subtract)
-
-        def gain(gains, diffs, name, n):
-            gains[n] = fresh(name, n)
-            nc.scalar.activation(gains[n], diffs[n], RELU)
-
-        def pair_sum(sums, bases, gains, name, n):
-            h, v0, width = units[n]
-            sums[n] = psum_sums.tile([P, width // P, P], F32, name=name)
-            for b in range(width // P):
-                own = slice(b * P, (b + 1) * P)
-                terms = (results["y", h][:, v0 + b * P : v0 + (b + 1) * P], bases[n][:, own], gains[n][:, own])
-                for i, term in enumerate(terms):
-                    nc.tensor.matmul(
-                        sums[n][:, b, :], term, ident[:], start=(i == 0), stop=(i == len(terms) - 1), is_transpose=True
-                    )
-
-        def clip(n):
-            relu_a[n] = fresh("relu_a", n).rearrange("p (b c) -> p b c", c=P)
-            nc.scalar.activation(relu_a[n], sum_a[n][:], RELU)
-
-        z_tile = keep.tile([P, T // P * H], BF16)
-        z_rows = z_tile[:].rearrange("p (b c) -> p b c", c=H)
+            for d in (1, 2, 3):
+                diffs[n, d] = buffer(f"diff{d}", n)
+                nc.vector.tensor_tensor(diffs[n, d], looked_up(d, n), base[n], ALU.subtract)
 
         def largest(n):
+            partial = buffer("partial", n)
+            gain[n] = buffer("gain", n)
+            nc.vector.scalar_tensor_tensor(partial, diffs[n, 1], 0.0, diffs[n, 2], ALU.max, ALU.max)
+            nc.vector.tensor_tensor(gain[n], partial, diffs[n, 3], ALU.max)
+
+        def add_turned(total, term, start, stop):
+            nc.tensor.matmul(total[:], term, ident[:], start=start, stop=stop, is_transpose=True)
+
+        def open_sum(n, b):
             h, v0, width = units[n]
-            nc.vector.tensor_tensor(
-                z_rows[:, v0 // P : (v0 + width) // P, h * P : (h + 1) * P], relu_a[n], sum_b[n][:], ALU.max
+            totals[n, b] = psum_sums.tile([P, P], F32, name="total")
+            add_turned(totals[n, b], results["y", h][:, v0 + b * P : v0 + (b + 1) * P], True, False)
+            add_turned(totals[n, b], base[n][:, b * P : (b + 1) * P], False, False)
+
+        def close_sum(n, b):
+            h, v0, width = units[n]
+            add_turned(totals[n, b], gain[n][:, b * P : (b + 1) * P], False, True)
+            nc.scalar.activation(
+                z_rows[v0 // P + b][:].rearrange("p (s g c) -> p s g c", s=2, g=TILES)[:, :, h, :],
+                totals[n, b][:].rearrange("p (s c) -> p s c", s=2),
+                RELU,
             )
 
-        def project(n):
-            h, v0, width = units[n]
-            blocks = width // P
-            turned = psum.tile([P, blocks, 2, P], F32, name="acc")
-            for b in range(blocks):
-                pairs = z_rows[:, v0 // P + b, :].bitcast(F32)
-                for s in range(2):
-                    nc.tensor.transpose(turned[:, b, s, :], pairs[:, s : H // 2 : 2], ident[:])
-            z_grouped = keep.tile([P, width * PACK], BF16, name=f"z_grouped_{n}", align_bytes=64)
+        def edge_sum(n):
+            for b in range(units[n][2] // P):
+                open_sum(n, b)
+                close_sum(n, b)
+
+        z_grouped = keep.tile([P, T * PACK], BF16, align_bytes=64)
+
+        def turn_back(b):
+            turned = psum.tile([P, 2, P], F32)
+            pairs = z_rows[b][:].bitcast(F32)
+            for s in range(2):
+                nc.tensor.transpose(turned[:, s, :], pairs[:, s * P : (s + 1) * P], ident[:])
             nc.scalar.copy(
-                out=z_grouped[:].bitcast(F32).rearrange("p (b r s) -> p b r s", b=blocks, s=2),
-                in_=turned[:].rearrange("p b s r -> p b r s"),
+                out=z_grouped[:, b * P * PACK : (b + 1) * P * PACK].bitcast(F32).rearrange("p (r s) -> p r s", s=2),
+                in_=turned[:].rearrange("p s r -> p r s"),
             )
-            z_codes = keep.tile([P, width], U32, name=f"z_codes_{n}", align_bytes=64)
-            z_plane = keep.tile([P, width], U8, name=f"z_plane_{n}", align_bytes=64)
-            nc.vector.quantize_mx(out=z_codes[:].bitcast(FP8X4), scales=z_plane[:], in_=z_grouped[:])
+
+        def project(v0, width):
+            z_codes = keep.tile([P, width], U32, name=f"z_codes_{v0}", align_bytes=64)
+            z_plane = keep.tile([P, width], U8, name=f"z_plane_{v0}", align_bytes=64)
+            nc.vector.quantize_mx(
+                out=z_codes[:].bitcast(FP8X4), scales=z_plane[:], in_=z_grouped[:, v0 * PACK : (v0 + width) * PACK]
+            )
             projected = psum.tile([P, width], F32, name="acc")
             nc.tensor.matmul_mx(
                 out=projected[:],
@@ -220,48 +234,59 @@ def tile_picked_wedgecv_relu_l_kernel(
                 start=True,
                 stop=True,
             )
-            staged = keep.tile([P, width], F32, name=f"staged_{n}")
+            staged = keep.tile([P, width], F32, name=f"staged_{v0}")
             nc.scalar.copy(out=staged[:], in_=projected[:])
             nc.sync.dma_start(out=out[:, v0 : v0 + width], in_=staged[:])
 
-        cast(("e", 0), nc.vector.tensor_copy)
+        on_scalar = (nc.scalar.copy, nc.scalar.copy)
+        cast(("e", 0), (nc.vector.tensor_copy, nc.scalar.copy))
         quantize(("e", 0), PASSES)
-        multiply(("e", 0))
-        unload(("e", 0))
-        summed = 0
-        for n in range(len(units)):
-            if n >= 2 and n != 8:
-                largest(n - 2)
-            if n in before_base:
-                quantize(before_base[n], 1)
-            gather_bases(n)
-            if n in before_diff:
-                quantize(before_diff[n], 1)
-            if n == 8:
-                largest(6)
+        first_product(("e", 0))
+        for h in range(TILES):
+            first, second = 2 * h, 2 * h + 1
+            if h > 0:
+                quantize(("y", h), 1)
+                multiply(("y", h))
+            if h < last:
+                cast(("e", h + 1), on_scalar)
+            if h == 0:
+                cast(("y", 0), on_scalar)
+            else:
+                unload(("y", h))
+                edge_sum(first - 1)
+            if h == last:
+                break
+            gather_base(first)
+            gather_base(second)
+            gather_diffs(first)
+            largest(first)
+            quantize(("e", h + 1), 1)
+            multiply(("e", h + 1))
+            cast(("y", h + 1), on_scalar)
+            unload(("e", h + 1))
+            gather_diffs(second)
+            largest(second)
+            if h == 0:
+                quantize(("y", 0), 1)
+                multiply(("y", 0))
+                unload(("y", 0))
+            edge_sum(first)
+        for b in range(T // P):
+            n = 2 * last + b
+            if b == 0:
+                gather_base(n)
+                open_sum(n, 0)
+            if b < 2:
+                gather_base(n + 1)
+                open_sum(n + 1, 0)
             gather_diffs(n)
-            if n in before_base:
-                multiply(before_base[n])
-            if n in before_diff:
-                multiply(before_diff[n])
-            if n + 1 in before_base:
-                cast(before_base[n + 1], nc.scalar.copy)
-            if n in before_base:
-                unload(before_base[n])
-            if n + 1 in before_diff:
-                cast(before_diff[n + 1], nc.scalar.copy)
-            gain(gain_a, diff_a, "gain_a", n)
-            if n in before_diff:
-                unload(before_diff[n])
-            gain(gain_b, diff_b, "gain_b", n)
-            if n == 8:
-                project(6)
-            if n >= 1:
-                for m in range(summed, n + 1):
-                    pair_sum(sum_a, base_a, gain_a, "sum_a", m)
-                    pair_sum(sum_b, base_b, gain_b, "sum_b", m)
-                    clip(m)
-                summed = n + 1
-        for n in (7, 8):
+            if b == 2:
+                gather_base(n + 1)
+                open_sum(n + 1, 0)
             largest(n)
-            project(n)
+            close_sum(n, 0)
+            turn_back(b)
+            if b == 1:
+                project(0, HALF)
+            if b > 1:
+                project(b * P, P)

@@ -36,17 +36,22 @@ def tile_picked_wedgecv_relu_l_kernel(
         psum = ctx.enter_context(tc.psum_pool(name="psum", bufs=2))
         psum_sums = ctx.enter_context(tc.psum_pool(name="psum_sums", bufs=4))
 
-        raw = {}
+        raw, staging, windows = {}, {}, {}
 
-        def load_weights(label, w, h):
-            for z in range(PASSES):
-                raw[label, h, z] = keep.tile([P, PACK, P], F32, name=f"raw_{label}_{h}_{z}")
+        def load_weights(label, w, h, passes=range(PASSES)):
+            for z in passes:
+                if label == "e" and z == 0 and h < TILES - 1:
+                    windows[h] = keep.tile([P, 2 * T], F32, name=f"window_{h}")
+                    raw[label, h, z] = windows[h][:, T:].rearrange("p (j c) -> p j c", j=PACK)
+                else:
+                    staging[label, h, z] = keep.tile([P, PACK * P], F32, name=f"raw_{label}_{h}_{z}")
+                    raw[label, h, z] = staging[label, h, z][:].rearrange("p (j c) -> p j c", j=PACK)
                 rows = w[z * K_PASS : (z + 1) * K_PASS, h * P : (h + 1) * P]
-                nc.sync.dma_start(out=raw[label, h, z][:], in_=rows.rearrange("(p j) c -> p j c", j=PACK))
+                nc.sync.dma_start(out=raw[label, h, z], in_=rows.rearrange("(p j) c -> p j c", j=PACK))
 
         def load_scale_rows(queue, plane, scales):
             passes = scales.shape[0]
-            nc.gpsimd.memset(plane[:].bitcast(I32), 0)
+            nc.vector.memset(plane[:].bitcast(I32), 0)
             for q in range(4):
                 queue.dma_start(
                     out=plane[32 * q : 32 * q + 4 * passes, :].bitcast(I32),
@@ -54,21 +59,21 @@ def tile_picked_wedgecv_relu_l_kernel(
                 )
 
         x_plane = keep.tile([P, T], U8, align_bytes=64)
-        load_scale_rows(nc.scalar, x_plane, x_scales)
-
-        load_weights("e", w2, 0)
+        load_weights("e", w2, 0, [0])
+        load_scale_rows(nc.sync, x_plane, x_scales)
+        load_weights("e", w2, 0, [1])
         x_codes = []
         for z in range(PASSES):
             x_codes.append(keep.tile([P, T], U32, name=f"x_codes_{z}", align_bytes=64))
-            nc.sync.dma_start(
-                out=x_codes[z][:].bitcast(I32),
-                in_=x_words[z].rearrange("p c r -> p (c r)").bitcast(I32),
-            )
+            words = x_words[z].rearrange("p c r -> p (c r)").bitcast(I32)
+            for points in ((slice(0, T),), (slice(0, HALF), slice(HALF, T)))[z]:
+                nc.sync.dma_start(out=x_codes[z][:, points].bitcast(I32), in_=words[:, points])
+        load_weights("e", w2, 1)
         lists = {}
         for d, pos in ((4, pos4), (1, pos1), (2, pos2), (3, pos3)):
             lists[d] = keep.tile([P, T // 16], U16, name=f"list_{d}")
             nc.sync.dma_start(lists[d][:], pos)
-        for label, h in (("e", 1), ("y", 0), ("y", 1), ("e", 2), ("y", 2), ("e", 3), ("y", 3)):
+        for label, h in (("y", 0), ("y", 1), ("e", 2), ("y", 2), ("e", 3), ("y", 3)):
             load_weights(label, w2 if label == "e" else w1, h)
         w3_codes = keep.tile([P, N], U32, align_bytes=64)
         nc.sync.dma_start(out=w3_codes[:].bitcast(I32), in_=w3_words[0].rearrange("p c r -> p (c r)").bitcast(I32))
@@ -88,7 +93,7 @@ def tile_picked_wedgecv_relu_l_kernel(
             for z in range(PASSES):
                 copies[z](
                     out=grouped[key][:, z, :, :].rearrange("p (s q e) j -> p q j s e", s=2, e=2),
-                    in_=raw[label, h, z][:].rearrange("p j (q s e) -> p q j s e", s=2, e=2),
+                    in_=raw[label, h, z].rearrange("p j (q s e) -> p q j s e", s=2, e=2),
                 )
 
         def quantize(key, pieces):
@@ -134,54 +139,66 @@ def tile_picked_wedgecv_relu_l_kernel(
                         start=(z == 0),
                         stop=(z == PASSES - 1),
                     )
-            results[key] = keep.tile([P, T], F32, name="result_first")
-            nc.scalar.copy(out=results[key][:, :HALF], in_=halves[0][:])
-            nc.vector.tensor_copy(out=results[key][:, HALF:], in_=halves[1][:])
+            nc.scalar.copy(out=windows[0][:, :HALF], in_=halves[0][:])
+            nc.vector.tensor_copy(out=windows[0][:, HALF:T], in_=halves[1][:])
 
         def unload(key):
             label, h = key
-            results[key] = keep.tile([P, T], F32, name=f"result_{label}_{h}")
-            nc.scalar.copy(out=results[key][:], in_=accs[key][:])
+            if label == "e" and h < TILES - 1:
+                nc.scalar.copy(out=windows[h][:, :T], in_=accs[key][:])
+            else:
+                results[key] = keep.tile([P, T], F32, name=f"result_{label}_{h}")
+                nc.scalar.copy(out=results[key][:], in_=accs[key][:])
+                if label == "e":
+                    windows[h] = results[key]
 
         last = TILES - 1
-        units = [(h, u * HALF, HALF) for h in range(last) for u in range(HALVES)]
-        units = units + [(last, b * P, P) for b in range(T // P)]
-        z_rows = [keep.tile([P, H], BF16, name=f"z_rows_{b}") for b in range(T // P)]
-        base, diffs, gain, totals = {}, {}, {}, {}
+        units = [(h, 0, T) for h in range(last)] + [(last, b * P, P) for b in range(T // P)]
+        z_words = [staging["y", 2, 1 - b // 2][:, b % 2 * HALF : (b % 2 + 1) * HALF] for b in range(T // P)]
+        base, diffs, partial, gain, totals = {}, {}, {}, {}, {}
 
-        def raw_bytes(label, h):
-            return raw[label, h, PASSES - 1][:].rearrange("p t c -> p (t c)")
-
-        reused = {("base", 2 * h): raw_bytes("y", h) for h in range(1, TILES)}
-        reused.update({("diff1", 2 * h - 1): raw_bytes("e", h) for h in range(1, TILES)})
-        reused["diff3", 8] = z_rows[0][:].bitcast(F32)
-        reused["base", 9] = z_rows[0][:].bitcast(F32)[:, P:]
-        reused["diff3", 9] = z_rows[1][:].bitcast(F32)
+        reused = {("diff3", h): staging["e", h + 1, 1][:] for h in range(last)}
+        reused["diff3", 5] = z_words[0]
+        reused["base", 6] = z_words[0][:, P:]
+        reused["diff3", 6] = z_words[1]
 
         def buffer(name, n):
-            width = units[n][2]
+            h, v0, width = units[n]
+            if name == "base" and h > 0 and (name, n) not in reused:
+                return diffs[h - 1, 1][:, v0 : v0 + width]
             if (name, n) in reused:
                 return reused[name, n][:, :width]
             return keep.tile([P, width], F32, name=f"{name}_{n}")[:]
 
-        def looked_up(d, n):
+        def looked_up(d, n, part):
             h, v0, width = units[n]
-            return results["e", h][:].indirect(lists[d][:, v0 // 16 : (v0 + width) // 16])
+            return windows[h][:].indirect(lists[d][:, (v0 + part.start) // 16 : (v0 + part.stop) // 16])
 
-        def gather_base(n):
+        def parts(n, pieces):
+            width = units[n][2] // pieces
+            return [slice(i * width, (i + 1) * width) for i in range(pieces)]
+
+        def gather_base(n, pieces=1):
             base[n] = buffer("base", n)
-            nc.vector.tensor_copy(base[n], looked_up(4, n))
+            for part in parts(n, pieces):
+                nc.vector.tensor_copy(base[n][:, part], looked_up(4, n, part))
+
+        def gather_diff(n, d, pieces=1):
+            diffs[n, d] = buffer(f"diff{d}", n)
+            for part in parts(n, pieces):
+                nc.vector.tensor_tensor(diffs[n, d][:, part], looked_up(d, n, part), base[n][:, part], ALU.subtract)
 
         def gather_diffs(n):
             for d in (1, 2, 3):
-                diffs[n, d] = buffer(f"diff{d}", n)
-                nc.vector.tensor_tensor(diffs[n, d], looked_up(d, n), base[n], ALU.subtract)
+                gather_diff(n, d)
+
+        def larger(n):
+            partial[n] = buffer("partial", n)
+            nc.vector.scalar_tensor_tensor(partial[n], diffs[n, 1], 0.0, diffs[n, 2], ALU.max, ALU.max)
 
         def largest(n):
-            partial = buffer("partial", n)
             gain[n] = buffer("gain", n)
-            nc.vector.scalar_tensor_tensor(partial, diffs[n, 1], 0.0, diffs[n, 2], ALU.max, ALU.max)
-            nc.vector.tensor_tensor(gain[n], partial, diffs[n, 3], ALU.max)
+            nc.vector.tensor_tensor(gain[n], partial[n], diffs[n, 3], ALU.max)
 
         def add_turned(total, term, start, stop):
             nc.tensor.matmul(total[:], term, ident[:], start=start, stop=stop, is_transpose=True)
@@ -196,21 +213,16 @@ def tile_picked_wedgecv_relu_l_kernel(
             h, v0, width = units[n]
             add_turned(totals[n, b], gain[n][:, b * P : (b + 1) * P], False, True)
             nc.scalar.activation(
-                z_rows[v0 // P + b][:].rearrange("p (s g c) -> p s g c", s=2, g=TILES)[:, :, h, :],
+                z_words[v0 // P + b].bitcast(BF16).rearrange("p (s g c) -> p s g c", s=2, g=TILES)[:, :, h, :],
                 totals[n, b][:].rearrange("p (s c) -> p s c", s=2),
                 RELU,
             )
-
-        def edge_sum(n):
-            for b in range(units[n][2] // P):
-                open_sum(n, b)
-                close_sum(n, b)
 
         z_grouped = keep.tile([P, T * PACK], BF16, align_bytes=64)
 
         def turn_back(b):
             turned = psum.tile([P, 2, P], F32)
-            pairs = z_rows[b][:].bitcast(F32)
+            pairs = z_words[b]
             for s in range(2):
                 nc.tensor.transpose(turned[:, s, :], pairs[:, s * P : (s + 1) * P], ident[:])
             nc.scalar.copy(
@@ -242,37 +254,39 @@ def tile_picked_wedgecv_relu_l_kernel(
         cast(("e", 0), (nc.vector.tensor_copy, nc.scalar.copy))
         quantize(("e", 0), PASSES)
         first_product(("e", 0))
-        for h in range(TILES):
-            first, second = 2 * h, 2 * h + 1
-            if h > 0:
-                quantize(("y", h), 1)
-                multiply(("y", h))
-            if h < last:
-                cast(("e", h + 1), on_scalar)
+        for h in range(last):
+            cast(("e", h + 1), on_scalar)
             if h == 0:
                 cast(("y", 0), on_scalar)
-            else:
+            cast(("y", h + 1), on_scalar)
+            gather_base(h, 2)
+            if h > 0:
+                for b in range(T // P):
+                    close_sum(h - 1, b)
                 unload(("y", h))
-                edge_sum(first - 1)
-            if h == last:
-                break
-            gather_base(first)
-            gather_base(second)
-            gather_diffs(first)
-            largest(first)
+                for b in range(T // P):
+                    open_sum(h, b)
+            gather_diff(h, 1, 2)
+            gather_diff(h, 2)
             quantize(("e", h + 1), 1)
             multiply(("e", h + 1))
-            cast(("y", h + 1), on_scalar)
             unload(("e", h + 1))
-            gather_diffs(second)
-            largest(second)
+            gather_diff(h, 3)
             if h == 0:
                 quantize(("y", 0), 1)
                 multiply(("y", 0))
                 unload(("y", 0))
-            edge_sum(first)
+                for b in range(T // P):
+                    open_sum(h, b)
+            larger(h)
+            quantize(("y", h + 1), 1)
+            multiply(("y", h + 1))
+            largest(h)
         for b in range(T // P):
-            n = 2 * last + b
+            close_sum(last - 1, b)
+        unload(("y", last))
+        for b in range(T // P):
+            n = last + b
             if b == 0:
                 gather_base(n)
                 open_sum(n, 0)
@@ -283,6 +297,7 @@ def tile_picked_wedgecv_relu_l_kernel(
             if b == 2:
                 gather_base(n + 1)
                 open_sum(n + 1, 0)
+            larger(n)
             largest(n)
             close_sum(n, 0)
             turn_back(b)

@@ -40,12 +40,13 @@ def tile_picked_wedgecv_relu_l_kernel(
 
         def load_weights(label, w, h, passes=range(PASSES)):
             for z in passes:
-                if label == "e" and z == 0 and h < TILES - 1:
+                if label == "e" and z == 0:
                     windows[h] = keep.tile([P, 2 * T], F32, name=f"window_{h}")
                     raw[label, h, z] = windows[h][:, T:].rearrange("p (j c) -> p j c", j=PACK)
                 else:
-                    staging[label, h, z] = keep.tile([P, PACK * P], F32, name=f"raw_{label}_{h}_{z}")
-                    raw[label, h, z] = staging[label, h, z][:].rearrange("p (j c) -> p j c", j=PACK)
+                    margin = HALF if label == "e" else 0
+                    staging[label, h, z] = keep.tile([P, T + 2 * margin], F32, name=f"raw_{label}_{h}_{z}")
+                    raw[label, h, z] = staging[label, h, z][:, margin : margin + T].rearrange("p (j c) -> p j c", j=PACK)
                 rows = w[z * K_PASS : (z + 1) * K_PASS, h * P : (h + 1) * P]
                 nc.sync.dma_start(out=raw[label, h, z], in_=rows.rearrange("(p j) c -> p j c", j=PACK))
 
@@ -73,7 +74,7 @@ def tile_picked_wedgecv_relu_l_kernel(
         for d, pos in ((4, pos4), (1, pos1), (2, pos2), (3, pos3)):
             lists[d] = keep.tile([P, T // 16], U16, name=f"list_{d}")
             nc.sync.dma_start(lists[d][:], pos)
-        for label, h in (("y", 0), ("y", 1), ("e", 2), ("y", 2), ("e", 3), ("y", 3)):
+        for label, h in (("y", 0), ("y", 1), ("e", 2), ("y", 3), ("e", 3), ("y", 2)):
             load_weights(label, w2 if label == "e" else w1, h)
         w3_codes = keep.tile([P, N], U32, align_bytes=64)
         nc.sync.dma_start(out=w3_codes[:].bitcast(I32), in_=w3_words[0].rearrange("p c r -> p (c r)").bitcast(I32))
@@ -82,6 +83,8 @@ def tile_picked_wedgecv_relu_l_kernel(
 
         ident = keep.tile([P, P], F32)
         make_identity(nc, ident[:])
+        ident_bf16 = keep.tile([P, P], BF16)
+        make_identity(nc, ident_bf16[:])
         warm = keep.tile([P, 1], F32)
         nc.scalar.activation(warm[:], ident[:, 0:1], RELU)
 
@@ -111,7 +114,7 @@ def tile_picked_wedgecv_relu_l_kernel(
                 )
 
         def multiply(key):
-            accs[key] = psum.tile([P, T], F32, name="acc")
+            accs[key] = psum.tile([P, T], F32, name=f"acc_{key[0]}")
             for z in range(PASSES):
                 cols = slice(z * P, (z + 1) * P)
                 nc.tensor.matmul_mx(
@@ -125,7 +128,7 @@ def tile_picked_wedgecv_relu_l_kernel(
                 )
 
         def first_product(key):
-            halves = [psum.tile([P, HALF], F32, name="acc") for u in range(HALVES)]
+            halves = [psum.tile([P, HALF], F32, name="acc_e") for u in range(HALVES)]
             for z in range(PASSES):
                 cols = slice(z * P, (z + 1) * P)
                 for u in range(HALVES):
@@ -144,90 +147,105 @@ def tile_picked_wedgecv_relu_l_kernel(
 
         def unload(key):
             label, h = key
-            if label == "e" and h < TILES - 1:
+            if label == "e":
                 nc.scalar.copy(out=windows[h][:, :T], in_=accs[key][:])
             else:
-                results[key] = keep.tile([P, T], F32, name=f"result_{label}_{h}")
-                nc.scalar.copy(out=results[key][:], in_=accs[key][:])
-                if label == "e":
-                    windows[h] = results[key]
+                results[key] = staging["e", h + 2, 1][:, :T] if h < 2 else keep.tile([P, T], F32, name=f"result_{label}_{h}")[:]
+                nc.scalar.copy(out=results[key], in_=accs[key][:])
 
         last = TILES - 1
-        units = [(h, 0, T) for h in range(last)] + [(last, b * P, P) for b in range(T // P)]
-        z_words = [staging["y", 2, 1 - b // 2][:, b % 2 * HALF : (b % 2 + 1) * HALF] for b in range(T // P)]
+        z_words = [staging["y", 2, b // 2][:, b % 2 * HALF : (b % 2 + 1) * HALF] for b in range(T // P)]
         base, diffs, partial, gain, totals = {}, {}, {}, {}, {}
+        everything = slice(0, T)
 
-        reused = {("diff3", h): staging["e", h + 1, 1][:] for h in range(last)}
-        reused["diff3", 5] = z_words[0]
-        reused["base", 6] = z_words[0][:, P:]
-        reused["diff3", 6] = z_words[1]
+        def fresh(name):
+            return keep.tile([P, T], F32, name=name)[:]
 
-        def buffer(name, n):
-            h, v0, width = units[n]
-            if name == "base" and h > 0 and (name, n) not in reused:
-                return diffs[h - 1, 1][:, v0 : v0 + width]
-            if (name, n) in reused:
-                return reused[name, n][:, :width]
-            return keep.tile([P, width], F32, name=f"{name}_{n}")[:]
+        def spent(key):
+            return grouped[key][:].rearrange("p z c t -> p (z c t)").bitcast(F32)
 
-        def looked_up(d, n, part):
-            h, v0, width = units[n]
-            return windows[h][:].indirect(lists[d][:, (v0 + part.start) // 16 : (v0 + part.stop) // 16])
+        def lay_out(h):
+            base[h] = windows[h - 1][:, T:] if h > 0 else fresh("base_first")
+            partial[h] = spent(("y", 2)) if h == 2 else fresh(f"partial_{h}")
+            gain[h] = fresh(f"gain_{h}")
+            if h == 0:
+                places = staging["e", 1, 1][:, :T], windows[1][:, T:], spent(("e", 1))
+            elif h < last:
+                places = staging["e", h + 1, 1][:, T:], windows[h + 1][:, T:], spent(("e", h + 1))
+            else:
+                places = fresh("sum_2"), fresh("sum_4"), fresh("sum_3")
+            diffs[h, 1], diffs[h, 2], diffs[h, 3] = places
 
-        def parts(n, pieces):
-            width = units[n][2] // pieces
-            return [slice(i * width, (i + 1) * width) for i in range(pieces)]
+        def looked_up(d, h, part):
+            return windows[h][:].indirect(lists[d][:, part.start // 16 : part.stop // 16])
 
-        def gather_base(n, pieces=1):
-            base[n] = buffer("base", n)
-            for part in parts(n, pieces):
-                nc.vector.tensor_copy(base[n][:, part], looked_up(4, n, part))
+        def gather_base(h, part=everything):
+            nc.vector.tensor_copy(base[h][:, part], looked_up(4, h, part))
 
-        def gather_diff(n, d, pieces=1):
-            diffs[n, d] = buffer(f"diff{d}", n)
-            for part in parts(n, pieces):
-                nc.vector.tensor_tensor(diffs[n, d][:, part], looked_up(d, n, part), base[n][:, part], ALU.subtract)
+        def gather_diff(h, d, part=everything):
+            nc.vector.tensor_tensor(diffs[h, d][:, part], looked_up(d, h, part), base[h][:, part], ALU.subtract)
 
-        def gather_diffs(n):
-            for d in (1, 2, 3):
-                gather_diff(n, d)
+        def larger(h, part=everything):
+            nc.vector.scalar_tensor_tensor(
+                partial[h][:, part], diffs[h, 1][:, part], 0.0, diffs[h, 2][:, part], ALU.max, ALU.max
+            )
 
-        def larger(n):
-            partial[n] = buffer("partial", n)
-            nc.vector.scalar_tensor_tensor(partial[n], diffs[n, 1], 0.0, diffs[n, 2], ALU.max, ALU.max)
+        def largest(h, part=everything):
+            nc.vector.tensor_tensor(gain[h][:, part], partial[h][:, part], diffs[h, 3][:, part], ALU.max)
 
-        def largest(n):
-            gain[n] = buffer("gain", n)
-            nc.vector.tensor_tensor(gain[n], partial[n], diffs[n, 3], ALU.max)
+        z_last = keep.tile([P, T], BF16)
+
+        def gather_sum(d, part, target):
+            nc.vector.tensor_tensor(target, looked_up(d, last, part), results["y", last][:, part], ALU.add)
+
+        def turn_last(first, count, turned_z):
+            for i in range(count):
+                nc.tensor.transpose(turned_z[:, i, :], z_last[:, (first + i) * P : (first + i + 1) * P], ident_bf16[:])
+
+        def place_last(first, count, turned_z):
+            rows = staging["y", 2, first // 2][:, first % 2 * HALF : (first % 2 + count) * HALF]
+            nc.scalar.copy(
+                out=rows.bitcast(BF16).rearrange("p (b s g c) -> p b s g c", b=count, s=2, g=TILES)[:, :, :, last, :],
+                in_=turned_z.rearrange("p b (s c) -> p b s c", s=2),
+            )
 
         def add_turned(total, term, start, stop):
             nc.tensor.matmul(total[:], term, ident[:], start=start, stop=stop, is_transpose=True)
 
-        def open_sum(n, b):
-            h, v0, width = units[n]
-            totals[n, b] = psum_sums.tile([P, P], F32, name="total")
-            add_turned(totals[n, b], results["y", h][:, v0 + b * P : v0 + (b + 1) * P], True, False)
-            add_turned(totals[n, b], base[n][:, b * P : (b + 1) * P], False, False)
+        def add_term(h, b, term, start, stop):
+            if start:
+                totals[h, b] = psum_sums.tile([P, P], F32, name="total")
+            add_turned(totals[h, b], term[:, b * P : (b + 1) * P], start, stop)
 
-        def close_sum(n, b):
-            h, v0, width = units[n]
-            add_turned(totals[n, b], gain[n][:, b * P : (b + 1) * P], False, True)
+        def clip(h, b):
             nc.scalar.activation(
-                z_words[v0 // P + b].bitcast(BF16).rearrange("p (s g c) -> p s g c", s=2, g=TILES)[:, :, h, :],
-                totals[n, b][:].rearrange("p (s c) -> p s c", s=2),
+                z_words[b].bitcast(BF16).rearrange("p (s g c) -> p s g c", s=2, g=TILES)[:, :, h, :],
+                totals[h, b][:].rearrange("p (s c) -> p s c", s=2),
                 RELU,
             )
 
+        def open_sum(h, b):
+            add_term(h, b, results["y", h], True, False)
+            add_term(h, b, base[h], False, False)
+
+        def close_sum(h, b):
+            add_term(h, b, gain[h], False, True)
+            clip(h, b)
+
         z_grouped = keep.tile([P, T * PACK], BF16, align_bytes=64)
 
+        banks = {}
+
         def turn_back(b):
-            turned = psum.tile([P, 2, P], F32)
-            pairs = z_words[b]
+            banks[b] = psum.tile([P, 2, P], F32, name="acc_y")
             for s in range(2):
-                nc.tensor.transpose(turned[:, s, :], pairs[:, s * P : (s + 1) * P], ident[:])
+                nc.tensor.transpose(banks[b][:, s, :], z_words[b][:, s * P : (s + 1) * P], ident[:])
+
+        def group(b):
+            turned = banks[b][:, :2, :]
             nc.scalar.copy(
                 out=z_grouped[:, b * P * PACK : (b + 1) * P * PACK].bitcast(F32).rearrange("p (r s) -> p r s", s=2),
-                in_=turned[:].rearrange("p s r -> p r s"),
+                in_=turned.rearrange("p s r -> p r s"),
             )
 
         def project(v0, width):
@@ -236,7 +254,7 @@ def tile_picked_wedgecv_relu_l_kernel(
             nc.vector.quantize_mx(
                 out=z_codes[:].bitcast(FP8X4), scales=z_plane[:], in_=z_grouped[:, v0 * PACK : (v0 + width) * PACK]
             )
-            projected = psum.tile([P, width], F32, name="acc")
+            projected = psum.tile([P, width], F32, name="acc_e")
             nc.tensor.matmul_mx(
                 out=projected[:],
                 lhsT=w3_codes[:].bitcast(FP8X4),
@@ -251,57 +269,104 @@ def tile_picked_wedgecv_relu_l_kernel(
             nc.sync.dma_start(out=out[:, v0 : v0 + width], in_=staged[:])
 
         on_scalar = (nc.scalar.copy, nc.scalar.copy)
+        halves = (slice(0, HALF), slice(HALF, T))
+        strips = [slice(b * P, (b + 1) * P) for b in range(T // P)]
         cast(("e", 0), (nc.vector.tensor_copy, nc.scalar.copy))
         quantize(("e", 0), PASSES)
         first_product(("e", 0))
+        y_after = (1, 3, 2)
         for h in range(last):
-            cast(("e", h + 1), on_scalar)
             if h == 0:
-                cast(("y", 0), on_scalar)
-            cast(("y", h + 1), on_scalar)
-            gather_base(h, 2)
-            if h > 0:
+                for key in (("e", 1), ("y", 0), ("y", 1), ("e", 2), ("y", 3), ("e", 3), ("y", 2)):
+                    cast(key, on_scalar)
+            lay_out(h)
+            if h == 0:
+                for part in halves:
+                    gather_base(h, part)
+                for part in halves:
+                    gather_diff(h, 1, part)
+            else:
+                gather_base(h)
+                largest(h - 1)
                 for b in range(T // P):
                     close_sum(h - 1, b)
-                unload(("y", h))
+                unload(("y", y_after[h - 1]))
                 for b in range(T // P):
-                    open_sum(h, b)
-            gather_diff(h, 1, 2)
-            gather_diff(h, 2)
+                    if h == 1:
+                        open_sum(h, b)
+                    else:
+                        add_term(h, b, base[h], True, False)
+                gather_diff(h, 1)
             quantize(("e", h + 1), 1)
             multiply(("e", h + 1))
             unload(("e", h + 1))
-            gather_diff(h, 3)
+            gather_diff(h, 2)
             if h == 0:
                 quantize(("y", 0), 1)
                 multiply(("y", 0))
                 unload(("y", 0))
                 for b in range(T // P):
                     open_sum(h, b)
+            if h == 2:
+                quantize(("y", 2), 1)
+                multiply(("y", 2))
+            gather_diff(h, 3)
             larger(h)
-            quantize(("y", h + 1), 1)
-            multiply(("y", h + 1))
-            largest(h)
+            if h < 2:
+                quantize(("y", y_after[h]), 1)
+                multiply(("y", y_after[h]))
+        lay_out(last)
+        gather_sum(1, everything, base[last])
+        largest(last - 1)
+        unload(("y", 2))
         for b in range(T // P):
-            close_sum(last - 1, b)
-        unload(("y", last))
+            add_term(2, b, gain[2], False, False)
         for b in range(T // P):
-            n = last + b
-            if b == 0:
-                gather_base(n)
-                open_sum(n, 0)
-            if b < 2:
-                gather_base(n + 1)
-                open_sum(n + 1, 0)
-            gather_diffs(n)
-            if b == 2:
-                gather_base(n + 1)
-                open_sum(n + 1, 0)
-            larger(n)
-            largest(n)
-            close_sum(n, 0)
-            turn_back(b)
-            if b == 1:
-                project(0, HALF)
-            if b > 1:
-                project(b * P, P)
+            add_term(2, b, results["y", 2], False, True)
+            clip(2, b)
+        sum1, sum2, two, three = base[last], diffs[last, 1], partial[last], gain[last]
+        pieces = (halves[0], strips[2], strips[3])
+        sum3 = [diffs[last, 3][:, :HALF], sum1[:, :P], three[:, :P]]
+        sum4 = [diffs[last, 2][:, :HALF], sum3[0][:, :P], three[:, strips[2]]]
+        three_of = [three[:, :HALF], three[:, strips[2]], three[:, strips[3]]]
+
+        def third(i):
+            nc.vector.tensor_tensor(three_of[i], two[:, pieces[i]], sum3[i], ALU.max)
+
+        def fourth(i):
+            nc.vector.tensor_tensor(z_last[:, pieces[i]], three_of[i], sum4[i], ALU.max)
+
+        gather_sum(2, everything, sum2)
+        gather_sum(3, pieces[0], sum3[0])
+        nc.vector.scalar_tensor_tensor(two, sum1, 0.0, sum2, ALU.max, ALU.max)
+        gather_sum(4, pieces[0], sum4[0])
+        third(0)
+        gather_sum(3, pieces[1], sum3[1])
+        fourth(0)
+        first_half = psum_sums.tile([P, 2, P], BF16, name="total")
+        turn_last(0, 2, first_half[:])
+        place_last(0, 2, first_half[:])
+        turn_back(0)
+        group(0)
+        turn_back(1)
+        group(1)
+        third(1)
+        gather_sum(4, pieces[1], sum4[1])
+        gather_sum(3, pieces[2], sum3[2])
+        fourth(1)
+        third_strip = psum_sums.tile([P, 1, P], BF16, name="total")
+        turn_last(2, 1, third_strip[:])
+        place_last(2, 1, third_strip[:])
+        third(2)
+        gather_sum(4, pieces[2], sum4[2])
+        fourth(2)
+        project(0, HALF)
+        turn_back(2)
+        group(2)
+        fourth_strip = psum_sums.tile([P, 1, P], BF16, name="total")
+        turn_last(3, 1, fourth_strip[:])
+        place_last(3, 1, fourth_strip[:])
+        project(2 * P, P)
+        turn_back(3)
+        group(3)
+        project(3 * P, P)

@@ -21,10 +21,10 @@ PACK = 4
 K_PASS = P * PACK
 PASSES = K // K_PASS
 TILES = H // P
-HALVES = 2
-HALF = T // HALVES
-BLOCKS = HALF // P
-LIST_COLS = HALF // 16
+LAST = TILES - 1
+HALF = T // 2
+STRIPS = T // P
+RANGES = ((0, 44), (44, 88), (88, 128))
 
 
 def tile_picked_wedgecv_relu_l_kernel(
@@ -36,50 +36,62 @@ def tile_picked_wedgecv_relu_l_kernel(
         psum = ctx.enter_context(tc.psum_pool(name="psum", bufs=2))
         psum_sums = ctx.enter_context(tc.psum_pool(name="psum_sums", bufs=4))
 
-        raw, staging, windows = {}, {}, {}
+        def size(r):
+            return PACK * PACK * (RANGES[r][1] - RANGES[r][0])
 
-        def load_weights(label, w, h, passes=range(PASSES)):
+        windows = [keep.tile([P, T + size(h % LAST)], F32, name=f"window_{h}") for h in range(TILES)]
+        margined = {r: keep.tile([P, 2 * T], F32, name=f"margined_{r}") for r in (1, 2)}
+        late = keep.tile([P, 4 * T], F32)
+        staged = {}
+        for r in range(len(RANGES)):
+            staged["e", r, 0] = windows[r][:, T:]
+            if r > 0:
+                staged["e", r, 1] = margined[r][:, HALF : HALF + size(r)]
+        staged["y", 0, 0] = windows[LAST][:, T:]
+        staged["y", 2, 0] = late[:, T - 16 : T - 16 + size(2)]
+        staged["y", 2, 1] = late[:, T - 16 + size(2) : T - 16 + 2 * size(2)]
+        for key in (("e", 0, 1), ("y", 0, 1), ("y", 1, 0), ("y", 1, 1)):
+            staged[key] = keep.tile([P, size(key[1])], F32, name="staged_%s_%d_%d" % key)[:]
+
+        def load_weights(label, r, passes=range(PASSES)):
+            w = w2 if label == "e" else w1
             for z in passes:
-                if label == "e" and z == 0:
-                    windows[h] = keep.tile([P, 2 * T], F32, name=f"window_{h}")
-                    raw[label, h, z] = windows[h][:, T:].rearrange("p (j c) -> p j c", j=PACK)
-                else:
-                    margin = HALF if label == "e" else 0
-                    staging[label, h, z] = keep.tile([P, T + 2 * margin], F32, name=f"raw_{label}_{h}_{z}")
-                    raw[label, h, z] = staging[label, h, z][:, margin : margin + T].rearrange("p (j c) -> p j c", j=PACK)
-                rows = w[z * K_PASS : (z + 1) * K_PASS, h * P : (h + 1) * P]
-                nc.sync.dma_start(out=raw[label, h, z], in_=rows.rearrange("(p j) c -> p j c", j=PACK))
+                rows = w[z * K_PASS : (z + 1) * K_PASS, PACK * RANGES[r][0] : PACK * RANGES[r][1]]
+                nc.sync.dma_start(
+                    out=staged[label, r, z].rearrange("p (j c) -> p j c", j=PACK),
+                    in_=rows.rearrange("(p j) c -> p j c", j=PACK),
+                )
 
-        def load_scale_rows(queue, plane, scales):
+        def load_scale_rows(plane, scales):
             passes = scales.shape[0]
             nc.vector.memset(plane[:].bitcast(I32), 0)
             for q in range(4):
-                queue.dma_start(
+                nc.sync.dma_start(
                     out=plane[32 * q : 32 * q + 4 * passes, :].bitcast(I32),
                     in_=scales[:, 4 * q : 4 * q + 4, :].bitcast(I32),
                 )
 
         x_plane = keep.tile([P, T], U8, align_bytes=64)
-        load_weights("e", w2, 0, [0])
-        load_scale_rows(nc.sync, x_plane, x_scales)
-        load_weights("e", w2, 0, [1])
+        load_weights("e", 0, [0])
+        load_scale_rows(x_plane, x_scales)
+        load_weights("e", 0, [1])
         x_codes = []
         for z in range(PASSES):
             x_codes.append(keep.tile([P, T], U32, name=f"x_codes_{z}", align_bytes=64))
             words = x_words[z].rearrange("p c r -> p (c r)").bitcast(I32)
             for points in ((slice(0, T),), (slice(0, HALF), slice(HALF, T)))[z]:
                 nc.sync.dma_start(out=x_codes[z][:, points].bitcast(I32), in_=words[:, points])
-        load_weights("e", w2, 1)
+        load_weights("e", 1)
         lists = {}
         for d, pos in ((4, pos4), (1, pos1), (2, pos2), (3, pos3)):
             lists[d] = keep.tile([P, T // 16], U16, name=f"list_{d}")
             nc.sync.dma_start(lists[d][:], pos)
-        for label, h in (("y", 0), ("y", 1), ("e", 2), ("y", 3), ("e", 3), ("y", 2)):
-            load_weights(label, w2 if label == "e" else w1, h)
+        for label, r in (("y", 0), ("y", 1), ("e", 2), ("y", 2)):
+            load_weights(label, r)
         w3_codes = keep.tile([P, N], U32, align_bytes=64)
         nc.sync.dma_start(out=w3_codes[:].bitcast(I32), in_=w3_words[0].rearrange("p c r -> p (c r)").bitcast(I32))
         w3_plane = keep.tile([P, N], U8, align_bytes=64)
-        load_scale_rows(nc.sync, w3_plane, w3_scales)
+        load_scale_rows(w3_plane, w3_scales)
 
         ident = keep.tile([P, P], F32)
         make_identity(nc, ident[:])
@@ -88,93 +100,102 @@ def tile_picked_wedgecv_relu_l_kernel(
         warm = keep.tile([P, 1], F32)
         nc.scalar.activation(warm[:], ident[:, 0:1], RELU)
 
-        grouped, codes, planes, accs, results = {}, {}, {}, {}, {}
-
-        def cast(key, copies):
-            label, h = key
-            grouped[key] = keep.tile([P, PASSES, P, PACK], BF16, name=f"grouped_{label}_{h}", align_bytes=64)
+        front, back, codes, planes, accs, results = {}, {}, {}, {}, {}, {}
+        for label in "ey":
+            back[label] = keep.tile([P, PASSES * P * PACK], BF16, name=f"back_{label}", align_bytes=64)
             for z in range(PASSES):
-                copies[z](
-                    out=grouped[key][:, z, :, :].rearrange("p (s q e) j -> p q j s e", s=2, e=2),
-                    in_=raw[label, h, z].rearrange("p j (q s e) -> p q j s e", s=2, e=2),
-                )
+                front[label, z] = keep.tile([P, LAST * P * PACK], BF16, name=f"front_{label}_{z}", align_bytes=64)
 
-        def quantize(key, pieces):
+        def by_word(label, r, z):
+            return staged[label, r, z].rearrange("p (j w t) -> p w j t", j=PACK, t=PACK)
+
+        def cast_front(label, r, z, copy=nc.scalar.copy):
+            lo, hi = (LAST * PACK * w for w in RANGES[r])
+            copy(
+                out=front[label, z][:, lo:hi].rearrange("p (w t j) -> p w j t", t=LAST, j=PACK),
+                in_=by_word(label, r, z)[:, :, :, :LAST],
+            )
+
+        def cast_back(label, r, z):
+            lo, hi = (PACK * (z * P + w) for w in RANGES[r])
+            nc.scalar.copy(
+                out=back[label][:, lo:hi].rearrange("p (w j) -> p w j", j=PACK), in_=by_word(label, r, z)[:, :, :, LAST]
+            )
+
+        def cast(label, r):
+            for z in range(PASSES):
+                cast_front(label, r, z)
+            for z in range(PASSES):
+                cast_back(label, r, z)
+
+        def quantize(key):
             label, h = key
             codes[key] = keep.tile([P, PASSES * P], U32, name=f"codes_{label}_{h}", align_bytes=64)
             planes[key] = keep.tile([P, PASSES * P], U8, name=f"plane_{label}_{h}", align_bytes=64)
-            values = grouped[key][:].rearrange("p z c t -> p (z c t)")
-            width = PASSES * P // pieces
-            for i in range(pieces):
-                cols = slice(i * width, (i + 1) * width)
+            if h == LAST:
+                nc.vector.quantize_mx(out=codes[key][:].bitcast(FP8X4), scales=planes[key][:], in_=back[label][:])
+                return
+            for z in range(PASSES):
+                cols = slice(z * P, (z + 1) * P)
                 nc.vector.quantize_mx(
                     out=codes[key][:, cols].bitcast(FP8X4),
                     scales=planes[key][:, cols],
-                    in_=values[:, i * width * PACK : (i + 1) * width * PACK],
+                    in_=front[label, z][:, h * P * PACK : (h + 1) * P * PACK],
                 )
+
+        def one_pass(acc, key, z, points):
+            cols = slice(z * P, (z + 1) * P)
+            nc.tensor.matmul_mx(
+                out=acc[:],
+                lhsT=codes[key][:, cols].bitcast(FP8X4),
+                lhsT_scale=planes[key][:, cols],
+                rhs=x_codes[z][:, points].bitcast(FP8X4),
+                rhs_scale=x_plane[4 * z :, points],
+                start=(z == 0),
+                stop=(z == PASSES - 1),
+            )
+
+        everything = slice(0, T)
+        halves = (slice(0, HALF), slice(HALF, T))
+        strips = [slice(b * P, (b + 1) * P) for b in range(STRIPS)]
 
         def multiply(key):
             accs[key] = psum.tile([P, T], F32, name=f"acc_{key[0]}")
             for z in range(PASSES):
-                cols = slice(z * P, (z + 1) * P)
-                nc.tensor.matmul_mx(
-                    out=accs[key][:],
-                    lhsT=codes[key][:, cols].bitcast(FP8X4),
-                    lhsT_scale=planes[key][:, cols],
-                    rhs=x_codes[z][:].bitcast(FP8X4),
-                    rhs_scale=x_plane[4 * z :, :],
-                    start=(z == 0),
-                    stop=(z == PASSES - 1),
-                )
+                one_pass(accs[key], key, z, everything)
 
-        def first_product(key):
-            halves = [psum.tile([P, HALF], F32, name="acc_e") for u in range(HALVES)]
+        def first_product():
+            parts = [psum.tile([P, HALF], F32, name="acc_e") for points in halves]
             for z in range(PASSES):
-                cols = slice(z * P, (z + 1) * P)
-                for u in range(HALVES):
-                    points = slice(u * HALF, (u + 1) * HALF)
-                    nc.tensor.matmul_mx(
-                        out=halves[u][:],
-                        lhsT=codes[key][:, cols].bitcast(FP8X4),
-                        lhsT_scale=planes[key][:, cols],
-                        rhs=x_codes[z][:, points].bitcast(FP8X4),
-                        rhs_scale=x_plane[4 * z :, points],
-                        start=(z == 0),
-                        stop=(z == PASSES - 1),
-                    )
-            nc.scalar.copy(out=windows[0][:, :HALF], in_=halves[0][:])
-            nc.vector.tensor_copy(out=windows[0][:, HALF:T], in_=halves[1][:])
-
-        def unload(key):
-            label, h = key
-            if label == "e":
-                nc.scalar.copy(out=windows[h][:, :T], in_=accs[key][:])
-            else:
-                results[key] = staging["e", h + 2, 1][:, :T] if h < 2 else keep.tile([P, T], F32, name=f"result_{label}_{h}")[:]
-                nc.scalar.copy(out=results[key], in_=accs[key][:])
-
-        last = TILES - 1
-        z_words = [staging["y", 2, b // 2][:, b % 2 * HALF : (b % 2 + 1) * HALF] for b in range(T // P)]
-        base, diffs, partial, gain, totals = {}, {}, {}, {}, {}
-        everything = slice(0, T)
+                for acc, points in zip(parts, halves):
+                    one_pass(acc, ("e", 0), z, points)
+            nc.scalar.copy(out=windows[0][:, halves[0]], in_=parts[0][:])
+            nc.vector.tensor_copy(out=windows[0][:, halves[1]], in_=parts[1][:])
 
         def fresh(name):
             return keep.tile([P, T], F32, name=name)[:]
 
-        def spent(key):
-            return grouped[key][:].rearrange("p z c t -> p (z c t)").bitcast(F32)
+        y_places = [margined[2][:, :T], late[:, :T], fresh("y_2"), fresh("y_3")]
 
-        def lay_out(h):
-            base[h] = windows[h - 1][:, T:] if h > 0 else fresh("base_first")
-            partial[h] = spent(("y", 2)) if h == 2 else fresh(f"partial_{h}")
-            gain[h] = fresh(f"gain_{h}")
-            if h == 0:
-                places = staging["e", 1, 1][:, :T], windows[1][:, T:], spent(("e", 1))
-            elif h < last:
-                places = staging["e", h + 1, 1][:, T:], windows[h + 1][:, T:], spent(("e", h + 1))
-            else:
-                places = fresh("sum_2"), fresh("sum_4"), fresh("sum_3")
-            diffs[h, 1], diffs[h, 2], diffs[h, 3] = places
+        def unload(key):
+            label, h = key
+            results[key] = windows[h][:, :T] if label == "e" else y_places[h]
+            nc.scalar.copy(out=results[key], in_=accs[key][:])
+
+        def product(key):
+            quantize(key)
+            multiply(key)
+            unload(key)
+
+        z_rows = late[:, T : T + STRIPS * LAST * P // 2].bitcast(BF16).rearrange("p (b c) -> p b c", b=STRIPS)
+        base = [fresh("base_0")] + [windows[h][:, T : 2 * T] for h in range(LAST)]
+        partial = [fresh(f"partial_{h}") for h in range(TILES)]
+        gain = [fresh(f"gain_{h}") for h in range(TILES)]
+        diffs = [
+            (margined[1][:, :T], margined[1][:, T:], front["e", 1][:].bitcast(F32)[:, :T]),
+            (margined[2][:, T:], front["e", 1][:].bitcast(F32)[:, HALF:], back["e"][:].bitcast(F32)),
+            (late[:, 5 * HALF : 7 * HALF], back["y"][:].bitcast(F32), front["y", 1][:].bitcast(F32)[:, HALF:]),
+        ]
 
         def looked_up(d, h, part):
             return windows[h][:].indirect(lists[d][:, part.start // 16 : part.stop // 16])
@@ -183,78 +204,46 @@ def tile_picked_wedgecv_relu_l_kernel(
             nc.vector.tensor_copy(base[h][:, part], looked_up(4, h, part))
 
         def gather_diff(h, d, part=everything):
-            nc.vector.tensor_tensor(diffs[h, d][:, part], looked_up(d, h, part), base[h][:, part], ALU.subtract)
+            nc.vector.tensor_tensor(diffs[h][d - 1][:, part], looked_up(d, h, part), base[h][:, part], ALU.subtract)
 
-        def larger(h, part=everything):
-            nc.vector.scalar_tensor_tensor(
-                partial[h][:, part], diffs[h, 1][:, part], 0.0, diffs[h, 2][:, part], ALU.max, ALU.max
-            )
+        def larger(h):
+            nc.vector.scalar_tensor_tensor(partial[h], diffs[h][0], 0.0, diffs[h][1], ALU.max, ALU.max)
 
-        def largest(h, part=everything):
-            nc.vector.tensor_tensor(gain[h][:, part], partial[h][:, part], diffs[h, 3][:, part], ALU.max)
-
-        z_last = keep.tile([P, T], BF16)
-
-        def gather_sum(d, part, target):
-            nc.vector.tensor_tensor(target, looked_up(d, last, part), results["y", last][:, part], ALU.add)
-
-        def turn_last(first, count, turned_z):
-            for i in range(count):
-                nc.tensor.transpose(turned_z[:, i, :], z_last[:, (first + i) * P : (first + i + 1) * P], ident_bf16[:])
-
-        def place_last(first, count, turned_z):
-            rows = staging["y", 2, first // 2][:, first % 2 * HALF : (first % 2 + count) * HALF]
-            nc.scalar.copy(
-                out=rows.bitcast(BF16).rearrange("p (b s g c) -> p b s g c", b=count, s=2, g=TILES)[:, :, :, last, :],
-                in_=turned_z.rearrange("p b (s c) -> p b s c", s=2),
-            )
+        def largest(h):
+            nc.vector.tensor_tensor(gain[h], partial[h], diffs[h][2], ALU.max)
 
         def add_turned(total, term, start, stop):
-            nc.tensor.matmul(total[:], term, ident[:], start=start, stop=stop, is_transpose=True)
+            nc.tensor.matmul(total, term, ident[:], start=start, stop=stop, is_transpose=True)
 
-        def add_term(h, b, term, start, stop):
-            if start:
-                totals[h, b] = psum_sums.tile([P, P], F32, name="total")
-            add_turned(totals[h, b], term[:, b * P : (b + 1) * P], start, stop)
+        def sum_tile(h):
+            totals = psum_sums.tile([P, STRIPS, P], F32, name="total")
+            for b in range(STRIPS):
+                for i, term in enumerate((results["y", h], base[h], gain[h])):
+                    add_turned(totals[:, b, :], term[:, strips[b]], i == 0, i == 2)
+            nc.scalar.activation(z_rows[:, :, h * P : (h + 1) * P], totals[:], RELU)
 
-        def clip(h, b):
-            nc.scalar.activation(
-                z_words[b].bitcast(BF16).rearrange("p (s g c) -> p s g c", s=2, g=TILES)[:, :, h, :],
-                totals[h, b][:].rearrange("p (s c) -> p s c", s=2),
-                RELU,
-            )
+        z_grouped = keep.tile([P, T, PACK], BF16, align_bytes=64)
 
-        def open_sum(h, b):
-            add_term(h, b, results["y", h], True, False)
-            add_term(h, b, base[h], False, False)
-
-        def close_sum(h, b):
-            add_term(h, b, gain[h], False, True)
-            clip(h, b)
-
-        z_grouped = keep.tile([P, T * PACK], BF16, align_bytes=64)
-
-        banks = {}
-
-        def turn_back(b):
-            banks[b] = psum.tile([P, 2, P], F32, name="acc_y")
-            for s in range(2):
-                nc.tensor.transpose(banks[b][:, s, :], z_words[b][:, s * P : (s + 1) * P], ident[:])
-
-        def group(b):
-            turned = banks[b][:, :2, :]
+        def turn_back(first):
+            turned = psum.tile([P, 2, LAST, P], BF16, name="acc_y")
+            for b in range(2):
+                for t in range(LAST):
+                    nc.tensor.transpose(turned[:, b, t, :], z_rows[:, first + b, t::LAST], ident_bf16[:])
             nc.scalar.copy(
-                out=z_grouped[:, b * P * PACK : (b + 1) * P * PACK].bitcast(F32).rearrange("p (r s) -> p r s", s=2),
-                in_=turned.rearrange("p s r -> p r s"),
+                out=z_grouped[:, first * P : (first + 2) * P, :LAST].rearrange("p (b v) t -> p b v t", b=2),
+                in_=turned[:].rearrange("p b t v -> p b v t"),
             )
 
-        def project(v0, width):
-            z_codes = keep.tile([P, width], U32, name=f"z_codes_{v0}", align_bytes=64)
-            z_plane = keep.tile([P, width], U8, name=f"z_plane_{v0}", align_bytes=64)
+        def project(part):
+            width = part.stop - part.start
+            z_codes = keep.tile([P, width], U32, name=f"z_codes_{part.start}", align_bytes=64)
+            z_plane = keep.tile([P, width], U8, name=f"z_plane_{part.start}", align_bytes=64)
             nc.vector.quantize_mx(
-                out=z_codes[:].bitcast(FP8X4), scales=z_plane[:], in_=z_grouped[:, v0 * PACK : (v0 + width) * PACK]
+                out=z_codes[:].bitcast(FP8X4),
+                scales=z_plane[:],
+                in_=z_grouped[:, part, :].rearrange("p v t -> p (v t)"),
             )
-            projected = psum.tile([P, width], F32, name="acc_e")
+            projected = psum_sums.tile([P, width], F32, name="total")
             nc.tensor.matmul_mx(
                 out=projected[:],
                 lhsT=w3_codes[:].bitcast(FP8X4),
@@ -264,109 +253,94 @@ def tile_picked_wedgecv_relu_l_kernel(
                 start=True,
                 stop=True,
             )
-            staged = keep.tile([P, width], F32, name=f"staged_{v0}")
-            nc.scalar.copy(out=staged[:], in_=projected[:])
-            nc.sync.dma_start(out=out[:, v0 : v0 + width], in_=staged[:])
+            result = keep.tile([P, width], F32, name=f"result_{part.start}")
+            nc.scalar.copy(out=result[:], in_=projected[:])
+            nc.sync.dma_start(out=out[:, part], in_=result[:])
 
-        on_scalar = (nc.scalar.copy, nc.scalar.copy)
-        halves = (slice(0, HALF), slice(HALF, T))
-        strips = [slice(b * P, (b + 1) * P) for b in range(T // P)]
-        cast(("e", 0), (nc.vector.tensor_copy, nc.scalar.copy))
-        quantize(("e", 0), PASSES)
-        first_product(("e", 0))
-        y_after = (1, 3, 2)
-        for h in range(last):
-            if h == 0:
-                for key in (("e", 1), ("y", 0), ("y", 1), ("e", 2), ("y", 3), ("e", 3), ("y", 2)):
-                    cast(key, on_scalar)
-            lay_out(h)
-            if h == 0:
-                for part in halves:
-                    gather_base(h, part)
-                for part in halves:
-                    gather_diff(h, 1, part)
-            else:
-                gather_base(h)
-                largest(h - 1)
-                for b in range(T // P):
-                    close_sum(h - 1, b)
-                unload(("y", y_after[h - 1]))
-                for b in range(T // P):
-                    if h == 1:
-                        open_sum(h, b)
-                    else:
-                        add_term(h, b, base[h], True, False)
-                gather_diff(h, 1)
-            quantize(("e", h + 1), 1)
-            multiply(("e", h + 1))
-            unload(("e", h + 1))
-            gather_diff(h, 2)
-            if h == 0:
-                quantize(("y", 0), 1)
-                multiply(("y", 0))
-                unload(("y", 0))
-                for b in range(T // P):
-                    open_sum(h, b)
-            if h == 2:
-                quantize(("y", 2), 1)
-                multiply(("y", 2))
-            gather_diff(h, 3)
-            larger(h)
-            if h < 2:
-                quantize(("y", y_after[h]), 1)
-                multiply(("y", y_after[h]))
-        lay_out(last)
-        gather_sum(1, everything, base[last])
-        largest(last - 1)
-        unload(("y", 2))
-        for b in range(T // P):
-            add_term(2, b, gain[2], False, False)
-        for b in range(T // P):
-            add_term(2, b, results["y", 2], False, True)
-            clip(2, b)
-        sum1, sum2, two, three = base[last], diffs[last, 1], partial[last], gain[last]
+        def gather_sum(d, part, target):
+            nc.vector.tensor_tensor(target, looked_up(d, LAST, part), results["y", LAST][:, part], ALU.add)
+
+        cast_front("e", 0, 0, nc.vector.tensor_copy)
+        cast_front("e", 0, 1)
+        quantize(("e", 0))
+        first_product()
+        cast("e", 1)
+        for z in range(PASSES):
+            cast_back("e", 0, z)
+        for label, r in (("y", 0), ("y", 1), ("e", 2), ("y", 2)):
+            cast(label, r)
+
+        for part in halves:
+            gather_base(0, part)
+        for part in halves:
+            gather_diff(0, 1, part)
+        product(("e", 1))
+        gather_diff(0, 2)
+        product(("y", 0))
+        gather_diff(0, 3)
+        larger(0)
+        product(("y", 1))
+
+        gather_base(1)
+        largest(0)
+        gather_diff(1, 1)
+        product(("e", 2))
+        product(("e", 3))
+        sum_tile(0)
+        gather_diff(1, 2)
+        gather_diff(1, 3)
+        larger(1)
+
+        gather_base(2)
+        largest(1)
+        gather_diff(2, 1)
+        product(("y", 3))
+        product(("y", 2))
+        sum_tile(1)
+        totals = [psum_sums.tile([P, P], F32, name="total") for b in range(STRIPS)]
+        for b in range(STRIPS):
+            add_turned(totals[b][:], base[2][:, strips[b]], True, False)
+            add_turned(totals[b][:], results["y", 2][:, strips[b]], False, False)
+        gather_diff(2, 2)
+        gather_diff(2, 3)
+        larger(2)
+
+        sum1, sum2, two, three = base[LAST], fresh("sum_2"), partial[LAST], gain[LAST]
         pieces = (halves[0], strips[2], strips[3])
-        sum3 = [diffs[last, 3][:, :HALF], sum1[:, :P], three[:, :P]]
-        sum4 = [diffs[last, 2][:, :HALF], sum3[0][:, :P], three[:, strips[2]]]
-        three_of = [three[:, :HALF], three[:, strips[2]], three[:, strips[3]]]
+        first3, first4 = fresh("sum_3"), fresh("sum_4")
+        z_last = keep.tile([P, T - P], BF16)
+        sum3 = [first3[:, :HALF], sum1[:, :P], three[:, :P]]
+        sum4 = [first4[:, :HALF], sum3[0][:, :P], z_last[:, pieces[0]].bitcast(F32)]
 
         def third(i):
-            nc.vector.tensor_tensor(three_of[i], two[:, pieces[i]], sum3[i], ALU.max)
+            nc.vector.tensor_tensor(three[:, pieces[i]], two[:, pieces[i]], sum3[i], ALU.max)
 
-        def fourth(i):
-            nc.vector.tensor_tensor(z_last[:, pieces[i]], three_of[i], sum4[i], ALU.max)
+        def fourth(i, target):
+            nc.vector.tensor_tensor(target, three[:, pieces[i]], sum4[i], ALU.max)
 
+        gather_sum(1, everything, sum1)
+        largest(2)
+        for b in range(STRIPS):
+            add_turned(totals[b][:], gain[2][:, strips[b]], False, True)
+            nc.scalar.activation(z_rows[:, b, 2 * P :], totals[b][:], RELU)
+        turn_back(0)
+        turn_back(2)
         gather_sum(2, everything, sum2)
         gather_sum(3, pieces[0], sum3[0])
         nc.vector.scalar_tensor_tensor(two, sum1, 0.0, sum2, ALU.max, ALU.max)
         gather_sum(4, pieces[0], sum4[0])
         third(0)
         gather_sum(3, pieces[1], sum3[1])
-        fourth(0)
-        first_half = psum_sums.tile([P, 2, P], BF16, name="total")
-        turn_last(0, 2, first_half[:])
-        place_last(0, 2, first_half[:])
-        turn_back(0)
-        group(0)
-        turn_back(1)
-        group(1)
+        fourth(0, z_last[:, pieces[0]])
+        nc.scalar.copy(out=z_grouped[:, pieces[0], LAST], in_=z_last[:, pieces[0]])
         third(1)
         gather_sum(4, pieces[1], sum4[1])
         gather_sum(3, pieces[2], sum3[2])
-        fourth(1)
-        third_strip = psum_sums.tile([P, 1, P], BF16, name="total")
-        turn_last(2, 1, third_strip[:])
-        place_last(2, 1, third_strip[:])
+        fourth(1, z_last[:, pieces[1]])
+        nc.scalar.copy(out=z_grouped[:, pieces[1], LAST], in_=z_last[:, pieces[1]])
         third(2)
         gather_sum(4, pieces[2], sum4[2])
-        fourth(2)
-        project(0, HALF)
-        turn_back(2)
-        group(2)
-        fourth_strip = psum_sums.tile([P, 1, P], BF16, name="total")
-        turn_last(3, 1, fourth_strip[:])
-        place_last(3, 1, fourth_strip[:])
-        project(2 * P, P)
-        turn_back(3)
-        group(3)
-        project(3 * P, P)
+        project(pieces[0])
+        fourth(2, z_grouped[:, pieces[2], LAST])
+        project(pieces[1])
+        project(pieces[2])

@@ -40,17 +40,16 @@ def tile_picked_wedgecv_relu_l_kernel(
             return PACK * PACK * (RANGES[r][1] - RANGES[r][0])
 
         windows = [keep.tile([P, T + size(h % LAST)], F32, name=f"window_{h}") for h in range(TILES)]
-        margined = {r: keep.tile([P, 2 * T], F32, name=f"margined_{r}") for r in (1, 2)}
-        late = keep.tile([P, 4 * T], F32)
+        margined = keep.tile([P, T - 16 + size(2)], F32)
+        late = keep.tile([P, T - 16 + 2 * size(2)], F32)
         staged = {}
         for r in range(len(RANGES)):
             staged["e", r, 0] = windows[r][:, T:]
-            if r > 0:
-                staged["e", r, 1] = margined[r][:, HALF : HALF + size(r)]
+        staged["e", 2, 1] = margined[:, T - 16 :]
         staged["y", 0, 0] = windows[LAST][:, T:]
         staged["y", 2, 0] = late[:, T - 16 : T - 16 + size(2)]
         staged["y", 2, 1] = late[:, T - 16 + size(2) : T - 16 + 2 * size(2)]
-        for key in (("e", 0, 1), ("y", 0, 1), ("y", 1, 0), ("y", 1, 1)):
+        for key in (("e", 0, 1), ("e", 1, 1), ("y", 0, 1), ("y", 1, 0), ("y", 1, 1)):
             staged[key] = keep.tile([P, size(key[1])], F32, name="staged_%s_%d_%d" % key)[:]
 
         def load_weights(label, r, passes=range(PASSES)):
@@ -62,43 +61,46 @@ def tile_picked_wedgecv_relu_l_kernel(
                     in_=rows.rearrange("(p j) c -> p j c", j=PACK),
                 )
 
-        def load_scale_rows(plane, scales):
+        def load_scale_rows(queue, plane, scales):
             passes = scales.shape[0]
-            nc.vector.memset(plane[:].bitcast(I32), 0)
+            nc.gpsimd.memset(plane[:].bitcast(I32), 0)
             for q in range(4):
-                nc.sync.dma_start(
+                queue.dma_start(
                     out=plane[32 * q : 32 * q + 4 * passes, :].bitcast(I32),
                     in_=scales[:, 4 * q : 4 * q + 4, :].bitcast(I32),
                 )
 
         x_plane = keep.tile([P, T], U8, align_bytes=64)
         load_weights("e", 0, [0])
-        load_scale_rows(x_plane, x_scales)
+        load_scale_rows(nc.sync, x_plane, x_scales)
         load_weights("e", 0, [1])
         x_codes = []
         for z in range(PASSES):
             x_codes.append(keep.tile([P, T], U32, name=f"x_codes_{z}", align_bytes=64))
             words = x_words[z].rearrange("p c r -> p (c r)").bitcast(I32)
-            for points in ((slice(0, T),), (slice(0, HALF), slice(HALF, T)))[z]:
+            for points in (slice(0, HALF), slice(HALF, T)):
                 nc.sync.dma_start(out=x_codes[z][:, points].bitcast(I32), in_=words[:, points])
-        load_weights("e", 1)
         lists = {}
-        for d, pos in ((4, pos4), (1, pos1), (2, pos2), (3, pos3)):
+
+        def load_list(d, pos):
             lists[d] = keep.tile([P, T // 16], U16, name=f"list_{d}")
             nc.sync.dma_start(lists[d][:], pos)
+
+        load_list(4, pos4)
+        load_weights("e", 1)
+        for d, pos in ((1, pos1), (2, pos2), (3, pos3)):
+            load_list(d, pos)
         for label, r in (("y", 0), ("y", 1), ("e", 2), ("y", 2)):
             load_weights(label, r)
         w3_codes = keep.tile([P, N], U32, align_bytes=64)
         nc.sync.dma_start(out=w3_codes[:].bitcast(I32), in_=w3_words[0].rearrange("p c r -> p (c r)").bitcast(I32))
         w3_plane = keep.tile([P, N], U8, align_bytes=64)
-        load_scale_rows(w3_plane, w3_scales)
+        load_scale_rows(nc.sync, w3_plane, w3_scales)
 
         ident = keep.tile([P, P], F32)
         make_identity(nc, ident[:])
         ident_bf16 = keep.tile([P, P], BF16)
         make_identity(nc, ident_bf16[:])
-        warm = keep.tile([P, 1], F32)
-        nc.scalar.activation(warm[:], ident[:, 0:1], RELU)
 
         front, back, codes, planes, accs, results = {}, {}, {}, {}, {}, {}
         for label in "ey":
@@ -169,13 +171,13 @@ def tile_picked_wedgecv_relu_l_kernel(
             for z in range(PASSES):
                 for acc, points in zip(parts, halves):
                     one_pass(acc, ("e", 0), z, points)
-            nc.scalar.copy(out=windows[0][:, halves[0]], in_=parts[0][:])
-            nc.vector.tensor_copy(out=windows[0][:, halves[1]], in_=parts[1][:])
+            nc.vector.tensor_copy(out=windows[0][:, halves[0]], in_=parts[0][:])
+            nc.scalar.copy(out=windows[0][:, halves[1]], in_=parts[1][:])
 
         def fresh(name):
             return keep.tile([P, T], F32, name=name)[:]
 
-        y_places = [margined[2][:, :T], late[:, :T], fresh("y_2"), fresh("y_3")]
+        y_places = [margined[:, :T], late[:, :T], fresh("y_2"), fresh("y_3")]
 
         def unload(key):
             label, h = key
@@ -191,10 +193,14 @@ def tile_picked_wedgecv_relu_l_kernel(
         base = [fresh("base_0")] + [windows[h][:, T : 2 * T] for h in range(LAST)]
         partial = [fresh(f"partial_{h}") for h in range(TILES)]
         gain = [fresh(f"gain_{h}") for h in range(TILES)]
+
+        def spent(values):
+            return values[:].bitcast(F32)
+
         diffs = [
-            (margined[1][:, :T], margined[1][:, T:], front["e", 1][:].bitcast(F32)[:, :T]),
-            (margined[2][:, T:], front["e", 1][:].bitcast(F32)[:, HALF:], back["e"][:].bitcast(F32)),
-            (late[:, 5 * HALF : 7 * HALF], back["y"][:].bitcast(F32), front["y", 1][:].bitcast(F32)[:, HALF:]),
+            (fresh("diff_0"), spent(front["e", 0])[:, :T], spent(front["e", 1])[:, :T]),
+            (fresh("diff_1"), spent(front["e", 0])[:, HALF:], spent(back["e"])),
+            (fresh("diff_2"), spent(back["y"]), spent(front["y", 1])[:, HALF:]),
         ]
 
         def looked_up(d, h, part):
@@ -224,14 +230,16 @@ def tile_picked_wedgecv_relu_l_kernel(
 
         z_grouped = keep.tile([P, T, PACK], BF16, align_bytes=64)
 
-        def turn_back(first):
-            turned = psum.tile([P, 2, LAST, P], BF16, name="acc_y")
-            for b in range(2):
+        def turn_back(pair):
+            turned = psum.tile([P, 2 * LAST, P], BF16, name="acc_y")
+            for i, b in enumerate(pair):
                 for t in range(LAST):
-                    nc.tensor.transpose(turned[:, b, t, :], z_rows[:, first + b, t::LAST], ident_bf16[:])
+                    nc.tensor.transpose(turned[:, i * LAST + t, :], z_rows[:, b, t::LAST], ident_bf16[:])
+            return turned
+
+        def group(turned, first, b, slots):
             nc.scalar.copy(
-                out=z_grouped[:, first * P : (first + 2) * P, :LAST].rearrange("p (b v) t -> p b v t", b=2),
-                in_=turned[:].rearrange("p b t v -> p b v t"),
+                out=z_grouped[:, strips[b], :slots], in_=turned[:, first : first + slots, :].rearrange("p t v -> p v t")
             )
 
         def project(part):
@@ -320,11 +328,13 @@ def tile_picked_wedgecv_relu_l_kernel(
 
         gather_sum(1, everything, sum1)
         largest(2)
-        for b in range(STRIPS):
+        for b in (0, 3, 2, 1):
             add_turned(totals[b][:], gain[2][:, strips[b]], False, True)
             nc.scalar.activation(z_rows[:, b, 2 * P :], totals[b][:], RELU)
-        turn_back(0)
-        turn_back(2)
+        for ahead, behind in ((0, 3), (2, 1)):
+            turned = turn_back((ahead, behind))
+            group(turned, LAST, behind, LAST)
+            group(turned, 0, ahead, PACK)
         gather_sum(2, everything, sum2)
         gather_sum(3, pieces[0], sum3[0])
         nc.vector.scalar_tensor_tensor(two, sum1, 0.0, sum2, ALU.max, ALU.max)

@@ -24,7 +24,7 @@ TILES = H // P
 LAST = TILES - 1
 HALF = T // 2
 STRIPS = T // P
-RANGES = ((0, 44), (44, 88), (88, 128))
+RANGES = {"e": ((0, 44), (44, 96), (96, 128)), "y": ((0, 48), (48, 96), (96, 128))}
 
 
 def tile_picked_wedgecv_relu_l_kernel(
@@ -36,26 +36,27 @@ def tile_picked_wedgecv_relu_l_kernel(
         psum = ctx.enter_context(tc.psum_pool(name="psum", bufs=2))
         psum_sums = ctx.enter_context(tc.psum_pool(name="psum_sums", bufs=4))
 
-        def size(r):
-            return PACK * PACK * (RANGES[r][1] - RANGES[r][0])
+        def size(label, r):
+            return PACK * PACK * (RANGES[label][r][1] - RANGES[label][r][0])
 
-        windows = [keep.tile([P, T + size(h % LAST)], F32, name=f"window_{h}") for h in range(TILES)]
-        margined = keep.tile([P, T - 16 + size(2)], F32)
-        late = keep.tile([P, T - 16 + 2 * size(2)], F32)
+        spare = [size("e", 0), size("e", 1), size("e", 2), size("y", 0)]
+        windows = [keep.tile([P, T + spare[h]], F32, name=f"window_{h}") for h in range(TILES)]
+        margined = keep.tile([P, T - 16 + size("e", 2)], F32)
+        late = keep.tile([P, T - 16 + 2 * size("y", 2)], F32)
         staged = {}
-        for r in range(len(RANGES)):
+        for r in range(LAST):
             staged["e", r, 0] = windows[r][:, T:]
         staged["e", 2, 1] = margined[:, T - 16 :]
         staged["y", 0, 0] = windows[LAST][:, T:]
-        staged["y", 2, 0] = late[:, T - 16 : T - 16 + size(2)]
-        staged["y", 2, 1] = late[:, T - 16 + size(2) : T - 16 + 2 * size(2)]
+        staged["y", 2, 0] = late[:, T - 16 : T - 16 + size("y", 2)]
+        staged["y", 2, 1] = late[:, T - 16 + size("y", 2) :]
         for key in (("e", 0, 1), ("e", 1, 1), ("y", 0, 1), ("y", 1, 0), ("y", 1, 1)):
-            staged[key] = keep.tile([P, size(key[1])], F32, name="staged_%s_%d_%d" % key)[:]
+            staged[key] = keep.tile([P, size(*key[:2])], F32, name="staged_%s_%d_%d" % key)[:]
 
         def load_weights(label, r, passes=range(PASSES)):
             w = w2 if label == "e" else w1
             for z in passes:
-                rows = w[z * K_PASS : (z + 1) * K_PASS, PACK * RANGES[r][0] : PACK * RANGES[r][1]]
+                rows = w[z * K_PASS : (z + 1) * K_PASS, PACK * RANGES[label][r][0] : PACK * RANGES[label][r][1]]
                 nc.sync.dma_start(
                     out=staged[label, r, z].rearrange("p (j c) -> p j c", j=PACK),
                     in_=rows.rearrange("(p j) c -> p j c", j=PACK),
@@ -88,8 +89,9 @@ def tile_picked_wedgecv_relu_l_kernel(
 
         load_list(4, pos4)
         load_weights("e", 1)
-        for d, pos in ((1, pos1), (2, pos2), (3, pos3)):
-            load_list(d, pos)
+        load_list(1, pos1)
+        load_list(2, pos2)
+        load_list(3, pos3)
         for label, r in (("y", 0), ("y", 1), ("e", 2), ("y", 2)):
             load_weights(label, r)
         w3_codes = keep.tile([P, N], U32, align_bytes=64)
@@ -112,14 +114,14 @@ def tile_picked_wedgecv_relu_l_kernel(
             return staged[label, r, z].rearrange("p (j w t) -> p w j t", j=PACK, t=PACK)
 
         def cast_front(label, r, z, copy=nc.scalar.copy):
-            lo, hi = (LAST * PACK * w for w in RANGES[r])
+            lo, hi = (LAST * PACK * w for w in RANGES[label][r])
             copy(
                 out=front[label, z][:, lo:hi].rearrange("p (w t j) -> p w j t", t=LAST, j=PACK),
                 in_=by_word(label, r, z)[:, :, :, :LAST],
             )
 
         def cast_back(label, r, z):
-            lo, hi = (PACK * (z * P + w) for w in RANGES[r])
+            lo, hi = (PACK * (z * P + w) for w in RANGES[label][r])
             nc.scalar.copy(
                 out=back[label][:, lo:hi].rearrange("p (w j) -> p w j", j=PACK), in_=by_word(label, r, z)[:, :, :, LAST]
             )
@@ -191,7 +193,7 @@ def tile_picked_wedgecv_relu_l_kernel(
 
         z_rows = late[:, T : T + STRIPS * LAST * P // 2].bitcast(BF16).rearrange("p (b c) -> p b c", b=STRIPS)
         base = [fresh("base_0")] + [windows[h][:, T : 2 * T] for h in range(LAST)]
-        partial = [fresh(f"partial_{h}") for h in range(TILES)]
+        partial = [fresh("partial_0"), back["e"][:].bitcast(F32), fresh("partial_2"), fresh("partial_3")]
         gain = [fresh(f"gain_{h}") for h in range(TILES)]
 
         def spent(values):
@@ -199,7 +201,7 @@ def tile_picked_wedgecv_relu_l_kernel(
 
         diffs = [
             (fresh("diff_0"), spent(front["e", 0])[:, :T], spent(front["e", 1])[:, :T]),
-            (fresh("diff_1"), spent(front["e", 0])[:, HALF:], spent(back["e"])),
+            (fresh("diff_1"), spent(front["e", 0])[:, HALF:], fresh("diff_1_3")),
             (fresh("diff_2"), spent(back["y"]), spent(front["y", 1])[:, HALF:]),
         ]
 
@@ -284,13 +286,13 @@ def tile_picked_wedgecv_relu_l_kernel(
             gather_diff(0, 1, part)
         product(("e", 1))
         gather_diff(0, 2)
-        product(("y", 0))
         gather_diff(0, 3)
+        product(("y", 0))
         larger(0)
-        product(("y", 1))
 
         gather_base(1)
         largest(0)
+        product(("y", 1))
         gather_diff(1, 1)
         product(("e", 2))
         product(("e", 3))

@@ -24,6 +24,7 @@ TILES = H // P
 LAST = TILES - 1
 HALF = T // 2
 STRIPS = T // P
+STRIP_ORDER = (0, 3, 2, 1)
 RANGES = {"e": ((0, 44), (44, 96), (96, 128)), "y": ((0, 48), (48, 96), (96, 128))}
 
 
@@ -41,16 +42,14 @@ def tile_picked_wedgecv_relu_l_kernel(
 
         spare = [size("e", 0), size("e", 1), size("e", 2), size("y", 0)]
         windows = [keep.tile([P, T + spare[h]], F32, name=f"window_{h}") for h in range(TILES)]
-        margined = keep.tile([P, T - 16 + size("e", 2)], F32)
         late = keep.tile([P, T - 16 + 2 * size("y", 2)], F32)
         staged = {}
         for r in range(LAST):
             staged["e", r, 0] = windows[r][:, T:]
-        staged["e", 2, 1] = margined[:, T - 16 :]
         staged["y", 0, 0] = windows[LAST][:, T:]
         staged["y", 2, 0] = late[:, T - 16 : T - 16 + size("y", 2)]
         staged["y", 2, 1] = late[:, T - 16 + size("y", 2) :]
-        for key in (("e", 0, 1), ("e", 1, 1), ("y", 0, 1), ("y", 1, 0), ("y", 1, 1)):
+        for key in (("e", 0, 1), ("e", 1, 1), ("e", 2, 1), ("y", 0, 1), ("y", 1, 0), ("y", 1, 1)):
             staged[key] = keep.tile([P, size(*key[:2])], F32, name="staged_%s_%d_%d" % key)[:]
 
         def load_weights(label, r, passes=range(PASSES)):
@@ -169,17 +168,19 @@ def tile_picked_wedgecv_relu_l_kernel(
                 one_pass(accs[key], key, z, everything)
 
         def first_product():
-            parts = [psum.tile([P, HALF], F32, name="acc_e") for points in halves]
+            parts = (halves[0], strips[2], strips[3])
+            banks = [psum.tile([P, HALF], F32, name="acc_e"), psum.tile([P, P], F32, name="acc_e")]
+            banks.append(psum.tile([P, P], F32, name="acc_y"))
             for z in range(PASSES):
-                for acc, points in zip(parts, halves):
+                for acc, points in zip(banks, parts):
                     one_pass(acc, ("e", 0), z, points)
-            nc.vector.tensor_copy(out=windows[0][:, halves[0]], in_=parts[0][:])
-            nc.scalar.copy(out=windows[0][:, halves[1]], in_=parts[1][:])
+            for acc, points, copy in zip(banks, parts, (nc.vector.tensor_copy, nc.vector.tensor_copy, nc.scalar.copy)):
+                copy(out=windows[0][:, points], in_=acc[:])
 
         def fresh(name):
             return keep.tile([P, T], F32, name=name)[:]
 
-        y_places = [margined[:, :T], late[:, :T], fresh("y_2"), fresh("y_3")]
+        y_places = [staged["y", 1, 1][:, :T], late[:, :T], fresh("y_2"), fresh("y_3")]
 
         def unload(key):
             label, h = key
@@ -223,12 +224,18 @@ def tile_picked_wedgecv_relu_l_kernel(
         def add_turned(total, term, start, stop):
             nc.tensor.matmul(total, term, ident[:], start=start, stop=stop, is_transpose=True)
 
-        def sum_tile(h):
-            totals = psum_sums.tile([P, STRIPS, P], F32, name="total")
-            for b in range(STRIPS):
-                for i, term in enumerate((results["y", h], base[h], gain[h])):
-                    add_turned(totals[:, b, :], term[:, strips[b]], i == 0, i == 2)
-            nc.scalar.activation(z_rows[:, :, h * P : (h + 1) * P], totals[:], RELU)
+        totals = {}
+
+        def open_sums(h):
+            for b in STRIP_ORDER:
+                totals[h, b] = psum_sums.tile([P, P], F32, name="total")
+                add_turned(totals[h, b][:], base[h][:, strips[b]], True, False)
+                add_turned(totals[h, b][:], results["y", h][:, strips[b]], False, False)
+
+        def close_sums(h):
+            for b in STRIP_ORDER:
+                add_turned(totals[h, b][:], gain[h][:, strips[b]], False, True)
+                nc.scalar.activation(z_rows[:, b, h * P : (h + 1) * P], totals[h, b][:], RELU)
 
         z_grouped = keep.tile([P, T, PACK], BF16, align_bytes=64)
 
@@ -244,7 +251,7 @@ def tile_picked_wedgecv_relu_l_kernel(
                 out=z_grouped[:, strips[b], :slots], in_=turned[:, first : first + slots, :].rearrange("p t v -> p v t")
             )
 
-        def project(part):
+        def project(part, copy=nc.scalar.copy):
             width = part.stop - part.start
             z_codes = keep.tile([P, width], U32, name=f"z_codes_{part.start}", align_bytes=64)
             z_plane = keep.tile([P, width], U8, name=f"z_plane_{part.start}", align_bytes=64)
@@ -264,7 +271,7 @@ def tile_picked_wedgecv_relu_l_kernel(
                 stop=True,
             )
             result = keep.tile([P, width], F32, name=f"result_{part.start}")
-            nc.scalar.copy(out=result[:], in_=projected[:])
+            copy(out=result[:], in_=projected[:])
             nc.sync.dma_start(out=out[:, part], in_=result[:])
 
         def gather_sum(d, part, target):
@@ -288,6 +295,7 @@ def tile_picked_wedgecv_relu_l_kernel(
         gather_diff(0, 2)
         gather_diff(0, 3)
         product(("y", 0))
+        open_sums(0)
         larger(0)
 
         gather_base(1)
@@ -296,7 +304,8 @@ def tile_picked_wedgecv_relu_l_kernel(
         gather_diff(1, 1)
         product(("e", 2))
         product(("e", 3))
-        sum_tile(0)
+        close_sums(0)
+        open_sums(1)
         gather_diff(1, 2)
         gather_diff(1, 3)
         larger(1)
@@ -306,11 +315,8 @@ def tile_picked_wedgecv_relu_l_kernel(
         gather_diff(2, 1)
         product(("y", 3))
         product(("y", 2))
-        sum_tile(1)
-        totals = [psum_sums.tile([P, P], F32, name="total") for b in range(STRIPS)]
-        for b in range(STRIPS):
-            add_turned(totals[b][:], base[2][:, strips[b]], True, False)
-            add_turned(totals[b][:], results["y", 2][:, strips[b]], False, False)
+        close_sums(1)
+        open_sums(2)
         gather_diff(2, 2)
         gather_diff(2, 3)
         larger(2)
@@ -330,9 +336,7 @@ def tile_picked_wedgecv_relu_l_kernel(
 
         gather_sum(1, everything, sum1)
         largest(2)
-        for b in (0, 3, 2, 1):
-            add_turned(totals[b][:], gain[2][:, strips[b]], False, True)
-            nc.scalar.activation(z_rows[:, b, 2 * P :], totals[b][:], RELU)
+        close_sums(2)
         for ahead, behind in ((0, 3), (2, 1)):
             turned = turn_back((ahead, behind))
             group(turned, LAST, behind, LAST)
@@ -355,4 +359,4 @@ def tile_picked_wedgecv_relu_l_kernel(
         project(pieces[0])
         fourth(2, z_grouped[:, pieces[2], LAST])
         project(pieces[1])
-        project(pieces[2])
+        project(pieces[2], nc.vector.tensor_copy)

@@ -61,18 +61,17 @@ def tile_picked_wedgecv_relu_l_kernel(
                     in_=rows.rearrange("(p j) c -> p j c", j=PACK),
                 )
 
-        def load_scale_rows(queue, plane, scales):
-            passes = scales.shape[0]
+        def load_scale_rows(plane, scales):
             nc.gpsimd.memset(plane[:].bitcast(I32), 0)
             for q in range(4):
-                queue.dma_start(
-                    out=plane[32 * q : 32 * q + 4 * passes, :].bitcast(I32),
-                    in_=scales[:, 4 * q : 4 * q + 4, :].bitcast(I32),
+                nc.sync.dma_start(
+                    out=plane[32 * q : 32 * q + 4, :, :].bitcast(I32),
+                    in_=scales[:, 4 * q : 4 * q + 4, :].bitcast(I32).rearrange("z r c -> r z c"),
                 )
 
-        x_plane = keep.tile([P, T], U8, align_bytes=64)
+        x_plane = keep.tile([P, PASSES, T], U8, align_bytes=64)
         load_weights("e", 0, [0])
-        load_scale_rows(nc.sync, x_plane, x_scales)
+        load_scale_rows(x_plane, x_scales)
         load_weights("e", 0, [1])
         x_codes = []
         for z in range(PASSES):
@@ -95,8 +94,8 @@ def tile_picked_wedgecv_relu_l_kernel(
             load_weights(label, r)
         w3_codes = keep.tile([P, N], U32, align_bytes=64)
         nc.sync.dma_start(out=w3_codes[:].bitcast(I32), in_=w3_words[0].rearrange("p c r -> p (c r)").bitcast(I32))
-        w3_plane = keep.tile([P, N], U8, align_bytes=64)
-        load_scale_rows(nc.sync, w3_plane, w3_scales)
+        w3_plane = keep.tile([P, 1, N], U8, align_bytes=64)
+        load_scale_rows(w3_plane, w3_scales)
 
         ident = keep.tile([P, P], F32)
         make_identity(nc, ident[:])
@@ -153,7 +152,7 @@ def tile_picked_wedgecv_relu_l_kernel(
                 lhsT=codes[key][:, cols].bitcast(FP8X4),
                 lhsT_scale=planes[key][:, cols],
                 rhs=x_codes[z][:, points].bitcast(FP8X4),
-                rhs_scale=x_plane[4 * z :, points],
+                rhs_scale=x_plane[:, z, points],
                 start=(z == 0),
                 stop=(z == PASSES - 1),
             )
@@ -264,7 +263,7 @@ def tile_picked_wedgecv_relu_l_kernel(
             nc.tensor.matmul_mx(
                 out=projected[:],
                 lhsT=w3_codes[:].bitcast(FP8X4),
-                lhsT_scale=w3_plane[:],
+                lhsT_scale=w3_plane[:, 0, :],
                 rhs=z_codes[:].bitcast(FP8X4),
                 rhs_scale=z_plane[:],
                 start=True,

@@ -24,7 +24,7 @@ TILES = H // P
 LAST = TILES - 1
 HALF = T // 2
 STRIPS = T // P
-STRIP_ORDER = (0, 3, 2, 1)
+STRIP_ORDER = (0, 1, 3, 2)
 RANGES = {"e": ((0, 44), (44, 96), (96, 128)), "y": ((0, 48), (48, 96), (96, 128))}
 
 
@@ -193,8 +193,8 @@ def tile_picked_wedgecv_relu_l_kernel(
 
         z_rows = late[:, T : T + STRIPS * LAST * P // 2].bitcast(BF16).rearrange("p (b c) -> p b c", b=STRIPS)
         base = [fresh("base_0")] + [windows[h][:, T : 2 * T] for h in range(LAST)]
-        partial = [fresh("partial_0"), back["e"][:].bitcast(F32), fresh("partial_2"), fresh("partial_3")]
-        gain = [fresh(f"gain_{h}") for h in range(TILES)]
+        partial = [fresh("partial_0"), back["e"][:].bitcast(F32), fresh("partial_2")]
+        gain = [fresh(f"gain_{h}") for h in range(LAST)]
 
         def spent(values):
             return values[:].bitcast(F32)
@@ -217,8 +217,8 @@ def tile_picked_wedgecv_relu_l_kernel(
         def larger(h):
             nc.vector.scalar_tensor_tensor(partial[h], diffs[h][0], 0.0, diffs[h][1], ALU.max, ALU.max)
 
-        def largest(h):
-            nc.vector.tensor_tensor(gain[h], partial[h], diffs[h][2], ALU.max)
+        def largest(h, part=everything):
+            nc.vector.tensor_tensor(gain[h][:, part], partial[h][:, part], diffs[h][2][:, part], ALU.max)
 
         def add_turned(total, term, start, stop):
             nc.tensor.matmul(total, term, ident[:], start=start, stop=stop, is_transpose=True)
@@ -250,9 +250,9 @@ def tile_picked_wedgecv_relu_l_kernel(
                 out=z_grouped[:, strips[b], :slots], in_=turned[:, first : first + slots, :].rearrange("p t v -> p v t")
             )
 
-        def project(part, copy=nc.scalar.copy):
+        def project(part, copy=nc.scalar.copy, slot=None):
             width = part.stop - part.start
-            z_codes = keep.tile([P, width], U32, name=f"z_codes_{part.start}", align_bytes=64)
+            z_codes = keep.tile([P, width], U32, name=slot or f"z_codes_{part.start}", align_bytes=64)
             z_plane = keep.tile([P, width], U8, name=f"z_plane_{part.start}", align_bytes=64)
             nc.vector.quantize_mx(
                 out=z_codes[:].bitcast(FP8X4),
@@ -317,45 +317,54 @@ def tile_picked_wedgecv_relu_l_kernel(
         close_sums(1)
         open_sums(2)
         gather_diff(2, 2)
-        gather_diff(2, 3)
+        gather_diff(2, 3, halves[0])
         larger(2)
+        gather_diff(2, 3, halves[1])
+        for part in halves:
+            largest(2, part)
+        close_sums(2)
 
-        sum1, sum2, two, three = base[LAST], fresh("sum_2"), partial[LAST], gain[LAST]
         pieces = (halves[0], strips[2], strips[3])
-        first3, first4 = fresh("sum_3"), fresh("sum_4")
-        z_last = keep.tile([P, T - P], BF16)
-        sum3 = [first3[:, :HALF], sum1[:, :P], three[:, :P]]
-        sum4 = [first4[:, :HALF], sum3[0][:, :P], z_last[:, pieces[0]].bitcast(F32)]
-
-        def third(i):
-            nc.vector.tensor_tensor(three[:, pieces[i]], two[:, pieces[i]], sum3[i], ALU.max)
+        sum1, sum2, sum3 = base[LAST], fresh("sum_2"), fresh("sum_3")
+        rounded1 = gain[2][:, HALF:].bitcast(BF16)
+        rounded2 = late[:, T : T + HALF].bitcast(BF16)
+        rounded3 = [late[:, T + HALF : T + HALF + P].bitcast(BF16), sum2[:, :P].bitcast(BF16)]
+        two = keep.tile([P, T], BF16)
+        three = keep.tile([P, T], BF16)
+        z_last = keep.tile([P, T - P], BF16, name="z_last", align_bytes=64)
+        sum4 = [sum3[:, part] for part in pieces]
 
         def fourth(i, target):
-            nc.vector.tensor_tensor(target, three[:, pieces[i]], sum4[i], ALU.max)
+            nc.vector.tensor_tensor(target, sum4[i], three[:, pieces[i]], ALU.max)
 
         gather_sum(1, everything, sum1)
-        largest(2)
-        close_sums(2)
-        for ahead, behind in ((0, 3), (2, 1)):
-            turned = turn_back((ahead, behind))
-            group(turned, LAST, behind, LAST)
-            group(turned, 0, ahead, PACK)
+        nc.scalar.activation(rounded1, sum1, RELU)
         gather_sum(2, everything, sum2)
-        gather_sum(3, pieces[0], sum3[0])
-        nc.vector.scalar_tensor_tensor(two, sum1, 0.0, sum2, ALU.max, ALU.max)
+        turned = turn_back((0, 1))
+        group(turned, 0, 0, LAST)
+        nc.scalar.activation(rounded2, sum2, RELU)
+        for i, part in enumerate(halves):
+            gather_sum(3, part, sum3[:, part])
+            nc.scalar.activation(rounded3[i], sum3[:, part], RELU)
+        group(turned, LAST, 1, LAST)
+        turned = turn_back((3, 2))
+        group(turned, 0, 3, PACK)
+        group(turned, LAST, 2, LAST)
+        nc.vector.tensor_tensor(two[:], rounded1, rounded2, ALU.max)
+
+        def third(i):
+            nc.vector.tensor_tensor(three[:, halves[i]], two[:, halves[i]], rounded3[i], ALU.max)
+
         gather_sum(4, pieces[0], sum4[0])
         third(0)
-        gather_sum(3, pieces[1], sum3[1])
+        gather_sum(4, pieces[1], sum4[1])
         fourth(0, z_last[:, pieces[0]])
         nc.scalar.copy(out=z_grouped[:, pieces[0], LAST], in_=z_last[:, pieces[0]])
         third(1)
-        gather_sum(4, pieces[1], sum4[1])
-        gather_sum(3, pieces[2], sum3[2])
+        gather_sum(4, pieces[2], sum4[2])
         fourth(1, z_last[:, pieces[1]])
         nc.scalar.copy(out=z_grouped[:, pieces[1], LAST], in_=z_last[:, pieces[1]])
-        third(2)
-        gather_sum(4, pieces[2], sum4[2])
-        project(pieces[0])
         fourth(2, z_grouped[:, pieces[2], LAST])
-        project(pieces[1])
-        project(pieces[2], nc.vector.tensor_copy)
+        project(pieces[0])
+        project(pieces[2], slot="z_last")
+        project(pieces[1], nc.vector.tensor_copy)

@@ -24,6 +24,7 @@ TILES = H // P
 LAST = TILES - 1
 HALF = T // 2
 STRIPS = T // P
+PER_COLUMN = 16
 STRIP_ORDER = (0, 1, 3, 2)
 RANGES = {"e": ((0, 44), (44, 96), (96, 128)), "y": ((0, 48), (48, 96), (96, 128))}
 
@@ -35,20 +36,21 @@ def tile_picked_wedgecv_relu_l_kernel(
     with ExitStack() as ctx:
         keep = ctx.enter_context(tc.tile_pool(name="keep", bufs=1))
         psum = ctx.enter_context(tc.psum_pool(name="psum", bufs=2))
-        psum_sums = ctx.enter_context(tc.psum_pool(name="psum_sums", bufs=4))
+        psum_sums = ctx.enter_context(tc.psum_pool(name="psum_sums", bufs=STRIPS))
 
         def size(label, r):
             return PACK * PACK * (RANGES[label][r][1] - RANGES[label][r][0])
 
         spare = [size("e", 0), size("e", 1), size("e", 2), size("y", 0)]
         windows = [keep.tile([P, T + spare[h]], F32, name=f"window_{h}") for h in range(TILES)]
-        late = keep.tile([P, T - 16 + 2 * size("y", 2)], F32)
+        late_start = T - 16
+        late = keep.tile([P, late_start + PASSES * size("y", 2)], F32)
         staged = {}
         for r in range(LAST):
             staged["e", r, 0] = windows[r][:, T:]
         staged["y", 0, 0] = windows[LAST][:, T:]
-        staged["y", 2, 0] = late[:, T - 16 : T - 16 + size("y", 2)]
-        staged["y", 2, 1] = late[:, T - 16 + size("y", 2) :]
+        staged["y", 2, 0] = late[:, late_start : late_start + size("y", 2)]
+        staged["y", 2, 1] = late[:, late_start + size("y", 2) :]
         for key in (("e", 0, 1), ("e", 1, 1), ("e", 2, 1), ("y", 0, 1), ("y", 1, 0), ("y", 1, 1)):
             staged[key] = keep.tile([P, size(*key[:2])], F32, name="staged_%s_%d_%d" % key)[:]
 
@@ -82,7 +84,7 @@ def tile_picked_wedgecv_relu_l_kernel(
         lists = {}
 
         def load_list(d, pos):
-            lists[d] = keep.tile([P, T // 16], U16, name=f"list_{d}")
+            lists[d] = keep.tile([P, T // PER_COLUMN], U16, name=f"list_{d}")
             nc.sync.dma_start(lists[d][:], pos)
 
         load_list(4, pos4)
@@ -102,7 +104,7 @@ def tile_picked_wedgecv_relu_l_kernel(
         ident_bf16 = keep.tile([P, P], BF16)
         make_identity(nc, ident_bf16[:])
 
-        front, back, codes, planes, accs, results = {}, {}, {}, {}, {}, {}
+        front, back, codes, planes, results = {}, {}, {}, {}, {}
         for label in "ey":
             back[label] = keep.tile([P, PASSES * P * PACK], BF16, name=f"back_{label}", align_bytes=64)
             for z in range(PASSES):
@@ -161,11 +163,6 @@ def tile_picked_wedgecv_relu_l_kernel(
         halves = (slice(0, HALF), slice(HALF, T))
         strips = [slice(b * P, (b + 1) * P) for b in range(STRIPS)]
 
-        def multiply(key):
-            accs[key] = psum.tile([P, T], F32, name=f"acc_{key[0]}")
-            for z in range(PASSES):
-                one_pass(accs[key], key, z, everything)
-
         def first_product():
             parts = (halves[0], strips[2], strips[3])
             banks = [psum.tile([P, HALF], F32, name="acc_e"), psum.tile([P, P], F32, name="acc_e")]
@@ -181,18 +178,18 @@ def tile_picked_wedgecv_relu_l_kernel(
 
         y_places = [staged["y", 1, 1][:, :T], late[:, :T], fresh("y_2"), fresh("y_3")]
 
-        def unload(key):
-            label, h = key
-            results[key] = windows[h][:, :T] if label == "e" else y_places[h]
-            nc.scalar.copy(out=results[key], in_=accs[key][:])
-
         def product(key):
+            label, h = key
             quantize(key)
-            multiply(key)
-            unload(key)
+            acc = psum.tile([P, T], F32, name=f"acc_{label}")
+            for z in range(PASSES):
+                one_pass(acc, key, z, everything)
+            results[key] = windows[h][:, :T] if label == "e" else y_places[h]
+            nc.scalar.copy(out=results[key], in_=acc[:])
 
         z_rows = late[:, T : T + STRIPS * LAST * P // 2].bitcast(BF16).rearrange("p (b c) -> p b c", b=STRIPS)
-        base = [fresh("base_0")] + [windows[h][:, T : 2 * T] for h in range(LAST)]
+        first_places = [fresh("base_0")] + [windows[h][:, T : 2 * T] for h in range(LAST)]
+        base = first_places[:LAST]
         partial = [fresh("partial_0"), back["e"][:].bitcast(F32), fresh("partial_2")]
         gain = [fresh(f"gain_{h}") for h in range(LAST)]
 
@@ -206,7 +203,7 @@ def tile_picked_wedgecv_relu_l_kernel(
         ]
 
         def looked_up(d, h, part):
-            return windows[h][:].indirect(lists[d][:, part.start // 16 : part.stop // 16])
+            return windows[h][:].indirect(lists[d][:, part.start // PER_COLUMN : part.stop // PER_COLUMN])
 
         def gather_base(h, part=everything):
             nc.vector.tensor_copy(base[h][:, part], looked_up(4, h, part))
@@ -250,9 +247,9 @@ def tile_picked_wedgecv_relu_l_kernel(
                 out=z_grouped[:, strips[b], :slots], in_=turned[:, first : first + slots, :].rearrange("p t v -> p v t")
             )
 
-        def project(part, copy=nc.scalar.copy, slot=None):
+        def project(part, copy=nc.scalar.copy, codes_tag=None):
             width = part.stop - part.start
-            z_codes = keep.tile([P, width], U32, name=slot or f"z_codes_{part.start}", align_bytes=64)
+            z_codes = keep.tile([P, width], U32, name=codes_tag or f"z_codes_{part.start}", align_bytes=64)
             z_plane = keep.tile([P, width], U8, name=f"z_plane_{part.start}", align_bytes=64)
             nc.vector.quantize_mx(
                 out=z_codes[:].bitcast(FP8X4),
@@ -325,46 +322,45 @@ def tile_picked_wedgecv_relu_l_kernel(
         close_sums(2)
 
         pieces = (halves[0], strips[2], strips[3])
-        sum1, sum2, sum3 = base[LAST], fresh("sum_2"), fresh("sum_3")
+        sum1, sum2, sum3 = first_places[LAST], fresh("sum_2"), fresh("sum_3")
         rounded1 = gain[2][:, HALF:].bitcast(BF16)
         rounded2 = late[:, T : T + HALF].bitcast(BF16)
-        rounded3 = [late[:, T + HALF : T + HALF + P].bitcast(BF16), sum2[:, :P].bitcast(BF16)]
-        two = keep.tile([P, T], BF16)
-        three = keep.tile([P, T], BF16)
+        rounded3 = late[:, T + HALF : T + HALF + P].bitcast(BF16)
+        of_two = keep.tile([P, T], BF16)
+        of_three = keep.tile([P, T], BF16)
         z_last = keep.tile([P, T - P], BF16, name="z_last", align_bytes=64)
         sum4 = [sum3[:, part] for part in pieces]
 
-        def fourth(i, target):
-            nc.vector.tensor_tensor(target, sum4[i], three[:, pieces[i]], ALU.max)
+        def of_four(i, target):
+            nc.vector.tensor_tensor(target, sum4[i], of_three[:, pieces[i]], ALU.max)
+
+        def weave(i):
+            nc.scalar.copy(out=z_grouped[:, pieces[i], LAST], in_=z_last[:, pieces[i]])
 
         gather_sum(1, everything, sum1)
         nc.scalar.activation(rounded1, sum1, RELU)
         gather_sum(2, everything, sum2)
-        turned = turn_back((0, 1))
-        group(turned, 0, 0, LAST)
+        turned = turn_back(STRIP_ORDER[:2])
+        group(turned, 0, STRIP_ORDER[0], LAST)
         nc.scalar.activation(rounded2, sum2, RELU)
-        for i, part in enumerate(halves):
+        for part in halves:
             gather_sum(3, part, sum3[:, part])
-            nc.scalar.activation(rounded3[i], sum3[:, part], RELU)
-        group(turned, LAST, 1, LAST)
-        turned = turn_back((3, 2))
-        group(turned, 0, 3, PACK)
-        group(turned, LAST, 2, LAST)
-        nc.vector.tensor_tensor(two[:], rounded1, rounded2, ALU.max)
-
-        def third(i):
-            nc.vector.tensor_tensor(three[:, halves[i]], two[:, halves[i]], rounded3[i], ALU.max)
-
+        nc.scalar.activation(rounded3, sum3[:, halves[0]], RELU)
+        group(turned, LAST, STRIP_ORDER[1], LAST)
+        turned = turn_back(STRIP_ORDER[2:])
+        group(turned, 0, STRIP_ORDER[2], PACK)
+        group(turned, LAST, STRIP_ORDER[3], LAST)
+        nc.vector.tensor_tensor(of_two[:], rounded1, rounded2, ALU.max)
         gather_sum(4, pieces[0], sum4[0])
-        third(0)
+        nc.vector.tensor_tensor(of_three[:, halves[0]], of_two[:, halves[0]], rounded3, ALU.max)
+        nc.vector.tensor_tensor(of_three[:, halves[1]], sum3[:, halves[1]], of_two[:, halves[1]], ALU.max)
+        of_four(0, z_last[:, pieces[0]])
+        weave(0)
         gather_sum(4, pieces[1], sum4[1])
-        fourth(0, z_last[:, pieces[0]])
-        nc.scalar.copy(out=z_grouped[:, pieces[0], LAST], in_=z_last[:, pieces[0]])
-        third(1)
         gather_sum(4, pieces[2], sum4[2])
-        fourth(1, z_last[:, pieces[1]])
-        nc.scalar.copy(out=z_grouped[:, pieces[1], LAST], in_=z_last[:, pieces[1]])
-        fourth(2, z_grouped[:, pieces[2], LAST])
+        of_four(1, z_last[:, pieces[1]])
+        weave(1)
+        of_four(2, z_grouped[:, pieces[2], LAST])
         project(pieces[0])
-        project(pieces[2], slot="z_last")
+        project(pieces[2], codes_tag="z_last")
         project(pieces[1], nc.vector.tensor_copy)

@@ -41,18 +41,23 @@ def tile_picked_wedgecv_relu_l_kernel(
         def size(label, r):
             return PACK * PACK * (RANGES[label][r][1] - RANGES[label][r][0])
 
-        spare = [size("e", 0), size("e", 1), size("e", 2), size("y", 0)]
-        windows = [keep.tile([P, T + spare[h]], F32, name=f"window_{h}") for h in range(TILES)]
-        late_start = T - 16
-        late = keep.tile([P, late_start + PASSES * size("y", 2)], F32)
-        staged = {}
-        for r in range(LAST):
-            staged["e", r, 0] = windows[r][:, T:]
-        staged["y", 0, 0] = windows[LAST][:, T:]
-        staged["y", 2, 0] = late[:, late_start : late_start + size("y", 2)]
-        staged["y", 2, 1] = late[:, late_start + size("y", 2) :]
-        for key in (("e", 0, 1), ("e", 1, 1), ("e", 2, 1), ("y", 0, 1), ("y", 1, 0), ("y", 1, 1)):
-            staged[key] = keep.tile([P, size(*key[:2])], F32, name="staged_%s_%d_%d" % key)[:]
+        widths = [T + size("e", 0), T + size("e", 1), T + size("y", 0), 2 * T]
+        windows = [keep.tile([P, widths[h]], F32, name=f"window_{h}") for h in range(TILES)]
+        staged = {
+            ("e", 0, 0): windows[0][:, T:],
+            ("e", 2, 0): windows[1][:, :T],
+            ("e", 1, 0): windows[1][:, T:],
+            ("y", 2, 0): windows[2][:, :T],
+            ("y", 0, 0): windows[2][:, T:],
+            ("y", 2, 1): windows[LAST][:, T - P : 2 * T - P],
+        }
+        staged["e", 0, 1] = keep.tile([P, size("e", 0)], F32, name="staged_e_0_1")[:]
+        rooms, ahead = {}, {}
+        for key in (("e", 1, 1), ("y", 0, 1), ("e", 2, 1), ("y", 1, 0), ("y", 1, 1)):
+            rooms[key] = keep.tile([P, 2 * T + size(*key[:2])], F32, name="room_%s_%d_%d" % key)
+            staged[key] = rooms[key][:, 2 * T :]
+            ahead[key] = rooms[key][:, T + 2 : 2 * T + 2]
+        late = keep.tile([P, STRIPS * LAST * P // 2], F32)
 
         def load_weights(label, r, passes=range(PASSES)):
             w = w2 if label == "e" else w1
@@ -88,11 +93,11 @@ def tile_picked_wedgecv_relu_l_kernel(
             nc.sync.dma_start(lists[d][:], pos)
 
         load_list(4, pos4)
+        load_list(2, pos2)
         load_weights("e", 1)
         load_list(1, pos1)
-        load_list(2, pos2)
         load_list(3, pos3)
-        for label, r in (("y", 0), ("y", 1), ("e", 2), ("y", 2)):
+        for label, r in (("y", 0), ("e", 2), ("y", 1), ("y", 2)):
             load_weights(label, r)
         w3_codes = keep.tile([P, N], U32, align_bytes=64)
         nc.sync.dma_start(out=w3_codes[:].bitcast(I32), in_=w3_words[0].rearrange("p c r -> p (c r)").bitcast(I32))
@@ -106,9 +111,12 @@ def tile_picked_wedgecv_relu_l_kernel(
 
         front, back, codes, planes, results = {}, {}, {}, {}, {}
         for label in "ey":
-            back[label] = keep.tile([P, PASSES * P * PACK], BF16, name=f"back_{label}", align_bytes=64)
             for z in range(PASSES):
                 front[label, z] = keep.tile([P, LAST * P * PACK], BF16, name=f"front_{label}_{z}", align_bytes=64)
+
+        back["e"] = keep.tile([P, PASSES * P * PACK], BF16, name="back_e", align_bytes=64)[:]
+        wide = keep.tile([P, 2 * T + HALF - 32], F32, align_bytes=64)
+        back["y"] = wide[:, T - 32 : 2 * T - 32].bitcast(BF16)
 
         def by_word(label, r, z):
             return staged[label, r, z].rearrange("p (j w t) -> p w j t", j=PACK, t=PACK)
@@ -120,24 +128,19 @@ def tile_picked_wedgecv_relu_l_kernel(
                 in_=by_word(label, r, z)[:, :, :, :LAST],
             )
 
-        def cast_back(label, r, z):
-            lo, hi = (PACK * (z * P + w) for w in RANGES[label][r])
-            nc.scalar.copy(
-                out=back[label][:, lo:hi].rearrange("p (w j) -> p w j", j=PACK), in_=by_word(label, r, z)[:, :, :, LAST]
-            )
+        def pool_cast(out, in_):
+            nc.gpsimd.tensor_scalar(out, in_, 1.0, 0.0, ALU.mult, ALU.add)
 
-        def cast(label, r):
-            for z in range(PASSES):
-                cast_front(label, r, z)
-            for z in range(PASSES):
-                cast_back(label, r, z)
+        def cast_back(label, r, z, copy=nc.scalar.copy):
+            lo, hi = (PACK * (z * P + w) for w in RANGES[label][r])
+            copy(out=back[label][:, lo:hi].rearrange("p (w j) -> p w j", j=PACK), in_=by_word(label, r, z)[:, :, :, LAST])
 
         def quantize(key):
             label, h = key
             codes[key] = keep.tile([P, PASSES * P], U32, name=f"codes_{label}_{h}", align_bytes=64)
             planes[key] = keep.tile([P, PASSES * P], U8, name=f"plane_{label}_{h}", align_bytes=64)
             if h == LAST:
-                nc.vector.quantize_mx(out=codes[key][:].bitcast(FP8X4), scales=planes[key][:], in_=back[label][:])
+                nc.vector.quantize_mx(out=codes[key][:].bitcast(FP8X4), scales=planes[key][:], in_=back[label])
                 return
             for z in range(PASSES):
                 cols = slice(z * P, (z + 1) * P)
@@ -176,31 +179,39 @@ def tile_picked_wedgecv_relu_l_kernel(
         def fresh(name):
             return keep.tile([P, T], F32, name=name)[:]
 
-        y_places = [staged["y", 1, 1][:, :T], late[:, :T], fresh("y_2"), fresh("y_3")]
+        first_room, third_room = rooms["e", 1, 1], rooms["y", 0, 1]
+        y_places = [ahead["y", 1, 0], first_room[:, 64 : T + 64], fresh("y_2"), fresh("y_3")]
+        banks = {}
 
-        def product(key):
-            label, h = key
+        def multiply(key):
             quantize(key)
-            acc = psum.tile([P, T], F32, name=f"acc_{label}")
+            banks[key] = psum.tile([P, T], F32, name=f"acc_{key[0]}")
             for z in range(PASSES):
-                one_pass(acc, key, z, everything)
+                one_pass(banks[key], key, z, everything)
+
+        def unload(key):
+            label, h = key
             results[key] = windows[h][:, :T] if label == "e" else y_places[h]
-            nc.scalar.copy(out=results[key], in_=acc[:])
+            nc.scalar.copy(out=results[key], in_=banks[key][:])
 
-        z_rows = late[:, T : T + STRIPS * LAST * P // 2].bitcast(BF16).rearrange("p (b c) -> p b c", b=STRIPS)
-        first_places = [fresh("base_0")] + [windows[h][:, T : 2 * T] for h in range(LAST)]
-        base = first_places[:LAST]
-        partial = [fresh("partial_0"), back["e"][:].bitcast(F32), fresh("partial_2")]
-        gain = [fresh(f"gain_{h}") for h in range(LAST)]
-
-        def spent(values):
-            return values[:].bitcast(F32)
-
-        diffs = [
-            (fresh("diff_0"), spent(front["e", 0])[:, :T], spent(front["e", 1])[:, :T]),
-            (fresh("diff_1"), spent(front["e", 0])[:, HALF:], fresh("diff_1_3")),
-            (fresh("diff_2"), spent(back["y"]), spent(front["y", 1])[:, HALF:]),
+        z_rows = late[:].bitcast(BF16).rearrange("p (b c) -> p b c", b=STRIPS)
+        base = [fresh(f"base_{h}") for h in range(LAST)]
+        other = [wide[:, :T], wide[:, T + HALF - 32 :], fresh("other_2")]
+        larger = front["y", 1][:].bitcast(F32)[:, HALF:]
+        gain = third_room[:, T + 8 : 2 * T + 8]
+        paired = {1: ahead["e", 1, 1], 3: ahead["y", 0, 1]}
+        diffs = [paired, paired, {1: back["y"].bitcast(F32), 3: fresh("diff_2_3")}]
+        rises = [
+            {1: ahead["e", 2, 1], 3: ahead["y", 1, 1]},
+            {1: windows[LAST][:, T:], 3: first_room[:, 2 * T - 64 : 3 * T - 64]},
         ]
+        rounded = {
+            (0, 1): first_room[:, T + P : T + P + HALF],
+            (0, 3): gain[:, :HALF],
+            (1, 1): keep.tile([P, HALF], F32, name="rounded_1_1")[:],
+            (1, 3): gain[:, HALF:],
+        }
+        rounded = {key: place.bitcast(BF16).rearrange("p (b c) -> p b c", b=STRIPS) for key, place in rounded.items()}
 
         def looked_up(d, h, part):
             return windows[h][:].indirect(lists[d][:, part.start // PER_COLUMN : part.stop // PER_COLUMN])
@@ -208,30 +219,49 @@ def tile_picked_wedgecv_relu_l_kernel(
         def gather_base(h, part=everything):
             nc.vector.tensor_copy(base[h][:, part], looked_up(4, h, part))
 
-        def gather_diff(h, d, part=everything):
-            nc.vector.tensor_tensor(diffs[h][d - 1][:, part], looked_up(d, h, part), base[h][:, part], ALU.subtract)
+        def gather_other(h):
+            nc.vector.tensor_copy(other[h], looked_up(2, h, everything))
 
-        def larger(h):
-            nc.vector.scalar_tensor_tensor(partial[h], diffs[h][0], 0.0, diffs[h][1], ALU.max, ALU.max)
-
-        def largest(h, part=everything):
-            nc.vector.tensor_tensor(gain[h][:, part], partial[h][:, part], diffs[h][2][:, part], ALU.max)
+        def gather_diff(h, d, of, part=everything):
+            nc.vector.tensor_tensor(diffs[h][d][:, part], looked_up(d, h, part), of[:, part], ALU.subtract)
 
         def add_turned(total, term, start, stop):
             nc.tensor.matmul(total, term, ident[:], start=start, stop=stop, is_transpose=True)
 
+        def add_strips(total, term, which, start=False, stop=False):
+            for i, b in enumerate(which):
+                add_turned(total[:, i, :], term[:, strips[b]], start and i == 0, stop and i == len(which) - 1)
+
         totals = {}
 
-        def open_sums(h):
-            for b in STRIP_ORDER:
-                totals[h, b] = psum_sums.tile([P, P], F32, name="total")
-                add_turned(totals[h, b][:], base[h][:, strips[b]], True, False)
-                add_turned(totals[h, b][:], results["y", h][:, strips[b]], False, False)
+        def open_pair(h, d):
+            totals[h, d] = psum_sums.tile([P, STRIPS, P], F32, name="total")
+            add_strips(totals[h, d], base[h] if d == 1 else other[h], range(STRIPS), start=True)
 
-        def close_sums(h):
-            for b in STRIP_ORDER:
-                add_turned(totals[h, b][:], gain[h][:, strips[b]], False, True)
-                nc.scalar.activation(z_rows[:, b, h * P : (h + 1) * P], totals[h, b][:], RELU)
+        def rise(h, d):
+            nc.scalar.activation(rises[h][d], diffs[h][d], RELU)
+
+        def close_pair(h, d):
+            add_strips(totals[h, d], results["y", h], range(STRIPS))
+            add_strips(totals[h, d], rises[h][d], range(STRIPS), stop=True)
+
+        def round_pair(h, d):
+            nc.scalar.activation(rounded[h, d], totals[h, d][:], RELU)
+
+        def join(h):
+            nc.vector.tensor_tensor(z_rows[:, :, h * P : (h + 1) * P], rounded[h, 1], rounded[h, 3], ALU.max)
+
+        pairs = (STRIP_ORDER[:2], STRIP_ORDER[2:])
+
+        def open_sums():
+            for pair in pairs:
+                totals[pair] = psum_sums.tile([P, 2, P], F32, name="total")
+                add_strips(totals[pair], larger, sorted(pair), start=True)
+
+        def close_sums():
+            for pair in pairs:
+                add_strips(totals[pair], gain, sorted(pair), stop=True)
+                nc.scalar.activation(z_rows[:, min(pair) : min(pair) + 2, 2 * P :], totals[pair][:], RELU)
 
         z_grouped = keep.tile([P, T, PACK], BF16, align_bytes=64)
 
@@ -277,55 +307,87 @@ def tile_picked_wedgecv_relu_l_kernel(
         cast_front("e", 0, 1)
         quantize(("e", 0))
         first_product()
-        cast("e", 1)
         for z in range(PASSES):
             cast_back("e", 0, z)
-        for label, r in (("y", 0), ("y", 1), ("e", 2), ("y", 2)):
-            cast(label, r)
+            cast_front("e", 1, z)
+            cast_back("e", 1, z, pool_cast)
+        for z in range(PASSES):
+            cast_front("y", 0, z)
+        cast_front("e", 2, 0)
+        cast_back("e", 2, 0)
 
-        for part in halves:
-            gather_base(0, part)
-        for part in halves:
-            gather_diff(0, 1, part)
-        product(("e", 1))
-        gather_diff(0, 2)
-        gather_diff(0, 3)
-        product(("y", 0))
-        open_sums(0)
-        larger(0)
+        gather_base(0)
+        gather_other(0)
+        open_pair(0, 1)
+        open_pair(0, 3)
+        multiply(("e", 1))
+        unload(("e", 1))
+        gather_diff(0, 1, base[0])
+        multiply(("y", 0))
+        gather_diff(0, 3, other[0])
+        cast_back("y", 0, 0, pool_cast)
+        cast_back("e", 2, 1, pool_cast)
+        cast_back("y", 1, 0, pool_cast)
+        cast_front("e", 2, 1)
+        rise(0, 1)
+        cast_front("y", 1, 0)
+        unload(("y", 0))
+        cast_front("y", 1, 1)
+        rise(0, 3)
+        cast_front("y", 2, 0)
+        cast_back("y", 2, 0)
 
         gather_base(1)
-        largest(0)
-        product(("y", 1))
-        gather_diff(1, 1)
-        product(("e", 2))
-        product(("e", 3))
-        close_sums(0)
-        open_sums(1)
-        gather_diff(1, 2)
-        gather_diff(1, 3)
-        larger(1)
+        gather_other(1)
+        open_pair(1, 1)
+        open_pair(1, 3)
+        multiply(("e", 2))
+        unload(("e", 2))
+        close_pair(0, 1)
+        close_pair(0, 3)
+        gather_diff(1, 1, base[1])
+        multiply(("y", 1))
+        multiply(("e", 3))
+        gather_diff(1, 3, other[1])
+        cast_back("y", 0, 1, pool_cast)
+        cast_back("y", 1, 1, pool_cast)
+        cast_front("y", 2, 1)
+        cast_back("y", 2, 1)
+        rise(1, 1)
+        unload(("y", 1))
+        round_pair(0, 1)
+        rise(1, 3)
+        round_pair(0, 3)
+        close_pair(1, 1)
+        close_pair(1, 3)
+        unload(("e", 3))
 
         gather_base(2)
-        largest(1)
-        gather_diff(2, 1)
-        product(("y", 3))
-        product(("y", 2))
-        close_sums(1)
-        open_sums(2)
-        gather_diff(2, 2)
-        gather_diff(2, 3, halves[0])
-        larger(2)
-        gather_diff(2, 3, halves[1])
-        for part in halves:
-            largest(2, part)
-        close_sums(2)
+        gather_other(2)
+        multiply(("y", 2))
+        multiply(("y", 3))
+        nc.vector.tensor_tensor(larger, base[2], other[2], ALU.max)
+        unload(("y", 2))
+        round_pair(1, 1)
+        round_pair(1, 3)
+        unload(("y", 3))
+        gather_diff(2, 1, larger)
+        open_sums()
+        for pair in pairs:
+            add_strips(totals[pair], results["y", 2], sorted(pair))
+        gather_diff(2, 3, larger)
+        for h, part in enumerate(halves):
+            join(h)
+            nc.vector.scalar_tensor_tensor(
+                gain[:, part], diffs[2][1][:, part], 0.0, diffs[2][3][:, part], ALU.max, ALU.max
+            )
+        close_sums()
 
         pieces = (halves[0], strips[2], strips[3])
-        sum1, sum2, sum3 = first_places[LAST], fresh("sum_2"), fresh("sum_3")
-        rounded1 = gain[2][:, HALF:].bitcast(BF16)
-        rounded2 = late[:, T : T + HALF].bitcast(BF16)
-        rounded3 = late[:, T + HALF : T + HALF + P].bitcast(BF16)
+        sum1, sum2, sum3 = windows[2][:, T : 2 * T], fresh("sum_2"), fresh("sum_3")
+        rounded1 = gain[:, HALF:].bitcast(BF16)
+        rounded2 = late[:, :HALF].bitcast(BF16)
+        rounded3 = late[:, HALF : HALF + P].bitcast(BF16)
         of_two = keep.tile([P, T], BF16)
         of_three = keep.tile([P, T], BF16)
         z_last = keep.tile([P, T - P], BF16, name="z_last", align_bytes=64)

@@ -41,22 +41,23 @@ def tile_picked_wedgecv_relu_l_kernel(
         def size(label, r):
             return PACK * PACK * (RANGES[label][r][1] - RANGES[label][r][0])
 
-        widths = [T + size("e", 0), T + size("e", 1), T + size("y", 0), 2 * T]
+        widths = [T + size("e", 0), size("y", 0) + size("e", 1), T + size("y", 0), 2 * T]
         windows = [keep.tile([P, widths[h]], F32, name=f"window_{h}") for h in range(TILES)]
         staged = {
             ("e", 0, 0): windows[0][:, T:],
-            ("e", 2, 0): windows[1][:, :T],
-            ("e", 1, 0): windows[1][:, T:],
+            ("y", 0, 1): windows[1][:, : size("y", 0)],
+            ("e", 1, 0): windows[1][:, size("y", 0) :],
             ("y", 2, 0): windows[2][:, :T],
             ("y", 0, 0): windows[2][:, T:],
             ("y", 2, 1): windows[LAST][:, T - P : 2 * T - P],
         }
-        staged["e", 0, 1] = keep.tile([P, size("e", 0)], F32, name="staged_e_0_1")[:]
+        for key in (("e", 0, 1), ("e", 2, 0), ("y", 1, 0)):
+            staged[key] = keep.tile([P, size(*key[:2])], F32, name="staged_%s_%d_%d" % key)[:]
         rooms, ahead = {}, {}
-        for key in (("e", 1, 1), ("y", 0, 1), ("e", 2, 1), ("y", 1, 0), ("y", 1, 1)):
-            rooms[key] = keep.tile([P, 2 * T + size(*key[:2])], F32, name="room_%s_%d_%d" % key)
-            staged[key] = rooms[key][:, 2 * T :]
-            ahead[key] = rooms[key][:, T + 2 : 2 * T + 2]
+        for key in (("e", 1, 1), ("e", 2, 1), ("y", 1, 1)):
+            rooms[key] = keep.tile([P, 4 * T], F32, name="room_%s_%d_%d" % key)
+            staged[key] = rooms[key][:, 2 * T : 2 * T + size(*key[:2])]
+            ahead[key] = rooms[key][:, T + 8 : 2 * T + 8]
         late = keep.tile([P, STRIPS * LAST * P // 2], F32)
 
         def load_weights(label, r, passes=range(PASSES)):
@@ -110,13 +111,15 @@ def tile_picked_wedgecv_relu_l_kernel(
         make_identity(nc, ident_bf16[:])
 
         front, back, codes, planes, results = {}, {}, {}, {}, {}
-        for label in "ey":
-            for z in range(PASSES):
-                front[label, z] = keep.tile([P, LAST * P * PACK], BF16, name=f"front_{label}_{z}", align_bytes=64)
-
+        for key in (("e", 0), ("e", 1), ("y", 0)):
+            front[key] = keep.tile([P, LAST * P * PACK], BF16, name="front_%s_%d" % key, align_bytes=64)[:]
         back["e"] = keep.tile([P, PASSES * P * PACK], BF16, name="back_e", align_bytes=64)[:]
-        wide = keep.tile([P, 2 * T + HALF - 32], F32, align_bytes=64)
-        back["y"] = wide[:, T - 32 : 2 * T - 32].bitcast(BF16)
+        wide = keep.tile([P, 2 * T], F32, align_bytes=64)
+        back["y"] = wide[:, :T].bitcast(BF16)
+        front["y", 1] = wide[:, HALF:].bitcast(BF16)
+
+        def place(label, h, z):
+            return 1 - z if (label, h) == ("y", LAST) else z
 
         def by_word(label, r, z):
             return staged[label, r, z].rearrange("p (j w t) -> p w j t", j=PACK, t=PACK)
@@ -132,7 +135,7 @@ def tile_picked_wedgecv_relu_l_kernel(
             nc.gpsimd.tensor_scalar(out, in_, 1.0, 0.0, ALU.mult, ALU.add)
 
         def cast_back(label, r, z, copy=nc.scalar.copy):
-            lo, hi = (PACK * (z * P + w) for w in RANGES[label][r])
+            lo, hi = (PACK * (place(label, LAST, z) * P + w) for w in RANGES[label][r])
             copy(out=back[label][:, lo:hi].rearrange("p (w j) -> p w j", j=PACK), in_=by_word(label, r, z)[:, :, :, LAST])
 
         def quantize(key):
@@ -151,7 +154,7 @@ def tile_picked_wedgecv_relu_l_kernel(
                 )
 
         def one_pass(acc, key, z, points):
-            cols = slice(z * P, (z + 1) * P)
+            cols = slice(place(*key, z) * P, (place(*key, z) + 1) * P)
             nc.tensor.matmul_mx(
                 out=acc[:],
                 lhsT=codes[key][:, cols].bitcast(FP8X4),
@@ -179,13 +182,17 @@ def tile_picked_wedgecv_relu_l_kernel(
         def fresh(name):
             return keep.tile([P, T], F32, name=name)[:]
 
-        first_room, third_room = rooms["e", 1, 1], rooms["y", 0, 1]
-        y_places = [ahead["y", 1, 0], first_room[:, 64 : T + 64], fresh("y_2"), fresh("y_3")]
+        first_room = rooms["e", 1, 1]
+        third_room = keep.tile([P, 2 * T - 64], F32)
+        y_places = [third_room[:, :T], first_room[:, T : 2 * T], fresh("y_2"), fresh("y_3")]
         banks = {}
 
         def multiply(key):
             quantize(key)
-            banks[key] = psum.tile([P, T], F32, name=f"acc_{key[0]}")
+            if key in (("y", 2), ("y", LAST)):
+                banks[key] = psum_sums.tile([P, T], F32, name="total")
+            else:
+                banks[key] = psum.tile([P, T], F32, name=f"acc_{key[0]}")
             for z in range(PASSES):
                 one_pass(banks[key], key, z, everything)
 
@@ -196,17 +203,20 @@ def tile_picked_wedgecv_relu_l_kernel(
 
         z_rows = late[:].bitcast(BF16).rearrange("p (b c) -> p b c", b=STRIPS)
         base = [fresh(f"base_{h}") for h in range(LAST)]
-        other = [wide[:, :T], wide[:, T + HALF - 32 :], fresh("other_2")]
-        larger = front["y", 1][:].bitcast(F32)[:, HALF:]
-        gain = third_room[:, T + 8 : 2 * T + 8]
-        paired = {1: ahead["e", 1, 1], 3: ahead["y", 0, 1]}
-        diffs = [paired, paired, {1: back["y"].bitcast(F32), 3: fresh("diff_2_3")}]
+        other = [fresh(f"other_{h}") for h in range(LAST)]
+        larger = wide[:, T:]
+        gain = rooms["y", 1, 1][:, T + 8 : 2 * T + 8]
+        diffs = [
+            {1: ahead["e", 1, 1], 3: third_room[:, T - 64 :]},
+            {1: first_room[:, 2 * T - 64 : 3 * T - 64], 3: ahead["y", 1, 1]},
+            {1: wide[:, :T], 3: fresh("diff_2_3")},
+        ]
         rises = [
-            {1: ahead["e", 2, 1], 3: ahead["y", 1, 1]},
-            {1: windows[LAST][:, T:], 3: first_room[:, 2 * T - 64 : 3 * T - 64]},
+            {1: ahead["e", 2, 1], 3: first_room[:, 64 : T + 64]},
+            {1: windows[LAST][:, T:], 3: first_room[:, 3 * T - P : 4 * T - P]},
         ]
         rounded = {
-            (0, 1): first_room[:, T + P : T + P + HALF],
+            (0, 1): first_room[:, 2 * T + 64 : 2 * T + 64 + HALF],
             (0, 3): gain[:, :HALF],
             (1, 1): keep.tile([P, HALF], F32, name="rounded_1_1")[:],
             (1, 3): gain[:, HALF:],
@@ -255,8 +265,8 @@ def tile_picked_wedgecv_relu_l_kernel(
 
         def open_sums():
             for pair in pairs:
-                totals[pair] = psum_sums.tile([P, 2, P], F32, name="total")
-                add_strips(totals[pair], larger, sorted(pair), start=True)
+                totals[pair] = psum.tile([P, 2, P], F32, name="acc_e")
+                add_strips(totals[pair], results["y", 2], sorted(pair), start=True)
 
         def close_sums():
             for pair in pairs:
@@ -313,8 +323,7 @@ def tile_picked_wedgecv_relu_l_kernel(
             cast_back("e", 1, z, pool_cast)
         for z in range(PASSES):
             cast_front("y", 0, z)
-        cast_front("e", 2, 0)
-        cast_back("e", 2, 0)
+        cast_back("y", 0, 1)
 
         gather_base(0)
         gather_other(0)
@@ -323,17 +332,23 @@ def tile_picked_wedgecv_relu_l_kernel(
         multiply(("e", 1))
         unload(("e", 1))
         gather_diff(0, 1, base[0])
-        multiply(("y", 0))
         gather_diff(0, 3, other[0])
+        multiply(("y", 0))
         cast_back("y", 0, 0, pool_cast)
-        cast_back("e", 2, 1, pool_cast)
         cast_back("y", 1, 0, pool_cast)
-        cast_front("e", 2, 1)
+        for z in range(PASSES):
+            cast_front("e", 2, z)
+            cast_back("e", 2, z)
         rise(0, 1)
-        cast_front("y", 1, 0)
-        unload(("y", 0))
-        cast_front("y", 1, 1)
         rise(0, 3)
+        unload(("y", 0))
+        for d in (1, 3):
+            add_strips(totals[0, d], rises[0][d], range(STRIPS))
+        for d in (1, 3):
+            add_strips(totals[0, d], results["y", 0], range(STRIPS), stop=True)
+        cast_front("y", 1, 0)
+        cast_front("y", 1, 1)
+        cast_back("y", 1, 1)
         cast_front("y", 2, 0)
         cast_back("y", 2, 0)
 
@@ -343,20 +358,16 @@ def tile_picked_wedgecv_relu_l_kernel(
         open_pair(1, 3)
         multiply(("e", 2))
         unload(("e", 2))
-        close_pair(0, 1)
-        close_pair(0, 3)
         gather_diff(1, 1, base[1])
         multiply(("y", 1))
         multiply(("e", 3))
         gather_diff(1, 3, other[1])
-        cast_back("y", 0, 1, pool_cast)
-        cast_back("y", 1, 1, pool_cast)
         cast_front("y", 2, 1)
         cast_back("y", 2, 1)
         rise(1, 1)
         unload(("y", 1))
-        round_pair(0, 1)
         rise(1, 3)
+        round_pair(0, 1)
         round_pair(0, 3)
         close_pair(1, 1)
         close_pair(1, 3)
@@ -367,14 +378,14 @@ def tile_picked_wedgecv_relu_l_kernel(
         multiply(("y", 2))
         multiply(("y", 3))
         nc.vector.tensor_tensor(larger, base[2], other[2], ALU.max)
-        unload(("y", 2))
         round_pair(1, 1)
+        unload(("y", 2))
         round_pair(1, 3)
         unload(("y", 3))
         gather_diff(2, 1, larger)
         open_sums()
         for pair in pairs:
-            add_strips(totals[pair], results["y", 2], sorted(pair))
+            add_strips(totals[pair], larger, sorted(pair))
         gather_diff(2, 3, larger)
         for h, part in enumerate(halves):
             join(h)

@@ -41,20 +41,20 @@ def tile_picked_wedgecv_relu_l_kernel(
         def size(label, r):
             return PACK * PACK * (RANGES[label][r][1] - RANGES[label][r][0])
 
-        widths = [T + size("e", 0), size("y", 0) + size("e", 1), T + size("y", 0), 2 * T]
+        widths = [T + size("e", 0), size("y", 0) + size("e", 1), size("y", 1) + size("y", 0), 2 * T]
         windows = [keep.tile([P, widths[h]], F32, name=f"window_{h}") for h in range(TILES)]
         staged = {
             ("e", 0, 0): windows[0][:, T:],
             ("y", 0, 1): windows[1][:, : size("y", 0)],
             ("e", 1, 0): windows[1][:, size("y", 0) :],
-            ("y", 2, 0): windows[2][:, :T],
-            ("y", 0, 0): windows[2][:, T:],
+            ("y", 1, 1): windows[2][:, : size("y", 1)],
+            ("y", 0, 0): windows[2][:, size("y", 1) :],
             ("y", 2, 1): windows[LAST][:, T - P : 2 * T - P],
         }
-        for key in (("e", 0, 1), ("e", 2, 0), ("y", 1, 0)):
+        for key in (("e", 0, 1), ("e", 2, 0), ("y", 1, 0), ("y", 2, 0)):
             staged[key] = keep.tile([P, size(*key[:2])], F32, name="staged_%s_%d_%d" % key)[:]
         rooms, ahead = {}, {}
-        for key in (("e", 1, 1), ("e", 2, 1), ("y", 1, 1)):
+        for key in (("e", 1, 1), ("e", 2, 1)):
             rooms[key] = keep.tile([P, 4 * T], F32, name="room_%s_%d_%d" % key)
             staged[key] = rooms[key][:, 2 * T : 2 * T + size(*key[:2])]
             ahead[key] = rooms[key][:, T + 8 : 2 * T + 8]
@@ -183,7 +183,7 @@ def tile_picked_wedgecv_relu_l_kernel(
             return keep.tile([P, T], F32, name=name)[:]
 
         first_room = rooms["e", 1, 1]
-        third_room = keep.tile([P, 2 * T - 64], F32)
+        third_room = keep.tile([P, 2 * T], F32)
         y_places = [third_room[:, :T], first_room[:, T : 2 * T], fresh("y_2"), fresh("y_3")]
         banks = {}
 
@@ -205,10 +205,10 @@ def tile_picked_wedgecv_relu_l_kernel(
         base = [fresh(f"base_{h}") for h in range(LAST)]
         other = [fresh(f"other_{h}") for h in range(LAST)]
         larger = wide[:, T:]
-        gain = rooms["y", 1, 1][:, T + 8 : 2 * T + 8]
+        gain = y_places[2]
         diffs = [
-            {1: ahead["e", 1, 1], 3: third_room[:, T - 64 :]},
-            {1: first_room[:, 2 * T - 64 : 3 * T - 64], 3: ahead["y", 1, 1]},
+            {1: ahead["e", 1, 1], 3: third_room[:, T - 64 : 2 * T - 64]},
+            {1: first_room[:, 2 * T - 64 : 3 * T - 64], 3: third_room[:, T:]},
             {1: wide[:, :T], 3: fresh("diff_2_3")},
         ]
         rises = [
@@ -217,9 +217,9 @@ def tile_picked_wedgecv_relu_l_kernel(
         ]
         rounded = {
             (0, 1): first_room[:, 2 * T + 64 : 2 * T + 64 + HALF],
-            (0, 3): gain[:, :HALF],
+            (0, 3): staged["y", 2, 0][:, :HALF],
             (1, 1): keep.tile([P, HALF], F32, name="rounded_1_1")[:],
-            (1, 3): gain[:, HALF:],
+            (1, 3): staged["y", 2, 0][:, HALF:],
         }
         rounded = {key: place.bitcast(BF16).rearrange("p (b c) -> p b c", b=STRIPS) for key, place in rounded.items()}
 
@@ -250,10 +250,6 @@ def tile_picked_wedgecv_relu_l_kernel(
 
         def rise(h, d):
             nc.scalar.activation(rises[h][d], diffs[h][d], RELU)
-
-        def close_pair(h, d):
-            add_strips(totals[h, d], results["y", h], range(STRIPS))
-            add_strips(totals[h, d], rises[h][d], range(STRIPS), stop=True)
 
         def round_pair(h, d):
             nc.scalar.activation(rounded[h, d], totals[h, d][:], RELU)
@@ -320,7 +316,7 @@ def tile_picked_wedgecv_relu_l_kernel(
         for z in range(PASSES):
             cast_back("e", 0, z)
             cast_front("e", 1, z)
-            cast_back("e", 1, z, pool_cast)
+            cast_back("e", 1, z, nc.scalar.copy if z else pool_cast)
         for z in range(PASSES):
             cast_front("y", 0, z)
         cast_back("y", 0, 1)
@@ -335,10 +331,11 @@ def tile_picked_wedgecv_relu_l_kernel(
         gather_diff(0, 3, other[0])
         multiply(("y", 0))
         cast_back("y", 0, 0, pool_cast)
+        cast_back("e", 2, 0, pool_cast)
         cast_back("y", 1, 0, pool_cast)
         for z in range(PASSES):
             cast_front("e", 2, z)
-            cast_back("e", 2, z)
+        cast_back("e", 2, 1)
         rise(0, 1)
         rise(0, 3)
         unload(("y", 0))
@@ -349,8 +346,6 @@ def tile_picked_wedgecv_relu_l_kernel(
         cast_front("y", 1, 0)
         cast_front("y", 1, 1)
         cast_back("y", 1, 1)
-        cast_front("y", 2, 0)
-        cast_back("y", 2, 0)
 
         gather_base(1)
         gather_other(1)
@@ -359,18 +354,21 @@ def tile_picked_wedgecv_relu_l_kernel(
         multiply(("e", 2))
         unload(("e", 2))
         gather_diff(1, 1, base[1])
-        multiply(("y", 1))
-        multiply(("e", 3))
         gather_diff(1, 3, other[1])
-        cast_front("y", 2, 1)
-        cast_back("y", 2, 1)
+        multiply(("e", 3))
+        multiply(("y", 1))
+        for z in range(PASSES):
+            cast_front("y", 2, z)
+            cast_back("y", 2, z)
         rise(1, 1)
         unload(("y", 1))
         rise(1, 3)
         round_pair(0, 1)
         round_pair(0, 3)
-        close_pair(1, 1)
-        close_pair(1, 3)
+        for d in (1, 3):
+            add_strips(totals[1, d], rises[1][d], range(STRIPS))
+        for d in (1, 3):
+            add_strips(totals[1, d], results["y", 1], range(STRIPS), stop=True)
         unload(("e", 3))
 
         gather_base(2)
@@ -379,16 +377,17 @@ def tile_picked_wedgecv_relu_l_kernel(
         multiply(("y", 3))
         nc.vector.tensor_tensor(larger, base[2], other[2], ALU.max)
         round_pair(1, 1)
-        unload(("y", 2))
         round_pair(1, 3)
+        unload(("y", 2))
         unload(("y", 3))
         gather_diff(2, 1, larger)
         open_sums()
         for pair in pairs:
             add_strips(totals[pair], larger, sorted(pair))
         gather_diff(2, 3, larger)
-        for h, part in enumerate(halves):
-            join(h)
+        join(0)
+        join(1)
+        for part in halves:
             nc.vector.scalar_tensor_tensor(
                 gain[:, part], diffs[2][1][:, part], 0.0, diffs[2][3][:, part], ALU.max, ALU.max
             )

@@ -26,7 +26,7 @@ HALF = T // 2
 STRIPS = T // P
 PER_COLUMN = 16
 STRIP_ORDER = (0, 1, 3, 2)
-RANGES = {"e": ((0, 44), (44, 96), (96, 128)), "y": ((0, 48), (48, 96), (96, 128))}
+RANGES = {label: ((0, 44), (44, 88), (88, 128)) for label in "ey"}
 
 
 def tile_picked_wedgecv_relu_l_kernel(
@@ -49,7 +49,7 @@ def tile_picked_wedgecv_relu_l_kernel(
             ("e", 1, 0): windows[1][:, size("y", 0) :],
             ("y", 1, 1): windows[2][:, : size("y", 1)],
             ("y", 0, 0): windows[2][:, size("y", 1) :],
-            ("y", 2, 1): windows[LAST][:, T - P : 2 * T - P],
+            ("y", 2, 1): windows[LAST][:, 2 * T - size("y", 2) :],
         }
         for key in (("e", 0, 1), ("e", 2, 0), ("y", 1, 0), ("y", 2, 0)):
             staged[key] = keep.tile([P, size(*key[:2])], F32, name="staged_%s_%d_%d" % key)[:]
@@ -219,7 +219,7 @@ def tile_picked_wedgecv_relu_l_kernel(
             (0, 1): first_room[:, 2 * T + 64 : 2 * T + 64 + HALF],
             (0, 3): staged["y", 2, 0][:, :HALF],
             (1, 1): keep.tile([P, HALF], F32, name="rounded_1_1")[:],
-            (1, 3): staged["y", 2, 0][:, HALF:],
+            (1, 3): staged["y", 2, 0][:, HALF:T],
         }
         rounded = {key: place.bitcast(BF16).rearrange("p (b c) -> p b c", b=STRIPS) for key, place in rounded.items()}
 
@@ -357,6 +357,9 @@ def tile_picked_wedgecv_relu_l_kernel(
         gather_diff(1, 3, other[1])
         multiply(("e", 3))
         multiply(("y", 1))
+        unread = psum.tile([P, T], F32, name="acc_y")
+        for z in range(PASSES):
+            one_pass(unread, ("y", 1), z, everything)
         for z in range(PASSES):
             cast_front("y", 2, z)
             cast_back("y", 2, z)

@@ -1,7 +1,6 @@
 from contextlib import ExitStack
 
 import concourse.mybir as mybir
-from concourse.masks import make_identity
 
 K, T, H, N = 1024, 512, 512, 128
 FLOPS = 2 * (2 * K * H * T + H * N * T)
@@ -14,6 +13,7 @@ U16 = mybir.dt.uint16
 U8 = mybir.dt.uint8
 FP8X4 = mybir.dt.float8_e4m3fn_x4
 ALU = mybir.AluOpType
+COPY = mybir.ActivationFunctionType.Copy
 RELU = mybir.ActivationFunctionType.Relu
 
 P = 128
@@ -21,12 +21,9 @@ PACK = 4
 K_PASS = P * PACK
 PASSES = K // K_PASS
 TILES = H // P
-LAST = TILES - 1
 HALF = T // 2
-STRIPS = T // P
+WORDS = P // 2
 PER_COLUMN = 16
-STRIP_ORDER = (0, 1, 3, 2)
-RANGES = {label: ((0, 44), (44, 88), (88, 128)) for label in "ey"}
 
 
 def tile_picked_wedgecv_relu_l_kernel(
@@ -35,130 +32,93 @@ def tile_picked_wedgecv_relu_l_kernel(
     nc = tc.nc
     with ExitStack() as ctx:
         keep = ctx.enter_context(tc.tile_pool(name="keep", bufs=1))
-        psum = ctx.enter_context(tc.psum_pool(name="psum", bufs=2))
-        psum_sums = ctx.enter_context(tc.psum_pool(name="psum_sums", bufs=STRIPS))
+        psum_e = ctx.enter_context(tc.psum_pool(name="psum_e", bufs=4))
+        psum_y = ctx.enter_context(tc.psum_pool(name="psum_y", bufs=4))
 
-        def size(label, r):
-            return PACK * PACK * (RANGES[label][r][1] - RANGES[label][r][0])
+        staged = {}
+        for label in "ey":
+            for r in range(2):
+                for z in range(PASSES):
+                    staged[label, r, z] = keep.tile([P, 2 * T], F32, name=f"staged_{label}_{r}_{z}")
+        windows = [staged["e", 0, 0], staged["e", 0, 1], staged["y", 0, 0], staged["y", 0, 1]]
 
-        widths = [T + size("e", 0), size("y", 0) + size("e", 1), size("y", 1) + size("y", 0), 2 * T]
-        windows = [keep.tile([P, widths[h]], F32, name=f"window_{h}") for h in range(TILES)]
-        staged = {
-            ("e", 0, 0): windows[0][:, T:],
-            ("y", 0, 1): windows[1][:, : size("y", 0)],
-            ("e", 1, 0): windows[1][:, size("y", 0) :],
-            ("y", 1, 1): windows[2][:, : size("y", 1)],
-            ("y", 0, 0): windows[2][:, size("y", 1) :],
-            ("y", 2, 1): windows[LAST][:, 2 * T - size("y", 2) :],
-        }
-        for key in (("e", 0, 1), ("e", 2, 0), ("y", 1, 0), ("y", 2, 0)):
-            staged[key] = keep.tile([P, size(*key[:2])], F32, name="staged_%s_%d_%d" % key)[:]
-        rooms, ahead = {}, {}
-        for key in (("e", 1, 1), ("e", 2, 1)):
-            rooms[key] = keep.tile([P, 4 * T], F32, name="room_%s_%d_%d" % key)
-            staged[key] = rooms[key][:, 2 * T : 2 * T + size(*key[:2])]
-            ahead[key] = rooms[key][:, T + 8 : 2 * T + 8]
-        late = keep.tile([P, STRIPS * LAST * P // 2], F32)
-
-        def load_weights(label, r, passes=range(PASSES)):
+        def load_weights(label, r, z):
             w = w2 if label == "e" else w1
-            for z in passes:
-                rows = w[z * K_PASS : (z + 1) * K_PASS, PACK * RANGES[label][r][0] : PACK * RANGES[label][r][1]]
-                nc.sync.dma_start(
-                    out=staged[label, r, z].rearrange("p (j c) -> p j c", j=PACK),
-                    in_=rows.rearrange("(p j) c -> p j c", j=PACK),
-                )
+            rows = w[z * K_PASS : (z + 1) * K_PASS, r * HALF : (r + 1) * HALF]
+            nc.sync.dma_start(
+                out=staged[label, r, z][:].rearrange("p (j c) -> p j c", j=PACK),
+                in_=rows.rearrange("(p j) c -> p j c", j=PACK),
+            )
 
-        def load_scale_rows(plane, scales):
+        def load_scale_rows(plane, scales, queue):
             nc.gpsimd.memset(plane[:].bitcast(I32), 0)
             for q in range(4):
-                nc.sync.dma_start(
+                queue.dma_start(
                     out=plane[32 * q : 32 * q + 4, :, :].bitcast(I32),
                     in_=scales[:, 4 * q : 4 * q + 4, :].bitcast(I32).rearrange("z r c -> r z c"),
                 )
 
-        x_plane = keep.tile([P, PASSES, T], U8, align_bytes=64)
-        load_weights("e", 0, [0])
-        load_scale_rows(x_plane, x_scales)
-        load_weights("e", 0, [1])
-        x_codes = []
-        for z in range(PASSES):
-            x_codes.append(keep.tile([P, T], U32, name=f"x_codes_{z}", align_bytes=64))
-            words = x_words[z].rearrange("p c r -> p (c r)").bitcast(I32)
-            for points in (slice(0, HALF), slice(HALF, T)):
-                nc.sync.dma_start(out=x_codes[z][:, points].bitcast(I32), in_=words[:, points])
         lists = {}
 
         def load_list(d, pos):
             lists[d] = keep.tile([P, T // PER_COLUMN], U16, name=f"list_{d}")
             nc.sync.dma_start(lists[d][:], pos)
 
-        load_list(4, pos4)
-        load_list(2, pos2)
-        load_weights("e", 1)
-        load_list(1, pos1)
-        load_list(3, pos3)
-        for label, r in (("y", 0), ("e", 2), ("y", 1), ("y", 2)):
-            load_weights(label, r)
+        x_plane = keep.tile([P, PASSES, T], U8, align_bytes=64)
+        load_weights("e", 0, 0)
+        load_scale_rows(x_plane, x_scales, nc.sync)
+        load_weights("e", 0, 1)
+        x_codes = []
+        for z in range(PASSES):
+            x_codes.append(keep.tile([P, T], U32, name=f"x_codes_{z}", align_bytes=64))
+            nc.sync.dma_start(out=x_codes[z][:].bitcast(I32), in_=x_words[z].rearrange("p c r -> p (c r)").bitcast(I32))
+        load_list(0, pos1)
+        load_list(1, pos2)
+        load_weights("e", 1, 0)
+        load_list(2, pos3)
+        load_list(3, pos4)
+        load_weights("e", 1, 1)
+        for r in range(2):
+            for z in range(PASSES):
+                load_weights("y", r, z)
         w3_codes = keep.tile([P, N], U32, align_bytes=64)
         nc.sync.dma_start(out=w3_codes[:].bitcast(I32), in_=w3_words[0].rearrange("p c r -> p (c r)").bitcast(I32))
         w3_plane = keep.tile([P, 1, N], U8, align_bytes=64)
-        load_scale_rows(w3_plane, w3_scales)
+        load_scale_rows(w3_plane, w3_scales, nc.sync)
 
-        ident = keep.tile([P, P], F32)
-        make_identity(nc, ident[:])
-        ident_bf16 = keep.tile([P, P], BF16)
-        make_identity(nc, ident_bf16[:])
-
-        front, back, codes, planes, results = {}, {}, {}, {}, {}
-        for key in (("e", 0), ("e", 1), ("y", 0)):
-            front[key] = keep.tile([P, LAST * P * PACK], BF16, name="front_%s_%d" % key, align_bytes=64)[:]
-        back["e"] = keep.tile([P, PASSES * P * PACK], BF16, name="back_e", align_bytes=64)[:]
-        wide = keep.tile([P, 2 * T], F32, align_bytes=64)
-        back["y"] = wide[:, :T].bitcast(BF16)
-        front["y", 1] = wide[:, HALF:].bitcast(BF16)
-
-        def place(label, h, z):
-            return 1 - z if (label, h) == ("y", LAST) else z
-
-        def by_word(label, r, z):
-            return staged[label, r, z].rearrange("p (j w t) -> p w j t", j=PACK, t=PACK)
-
-        def cast_front(label, r, z, copy=nc.scalar.copy):
-            lo, hi = (LAST * PACK * w for w in RANGES[label][r])
-            copy(
-                out=front[label, z][:, lo:hi].rearrange("p (w t j) -> p w j t", t=LAST, j=PACK),
-                in_=by_word(label, r, z)[:, :, :, :LAST],
-            )
-
-        def pool_cast(out, in_):
-            nc.gpsimd.tensor_scalar(out, in_, 1.0, 0.0, ALU.mult, ALU.add)
-
-        def cast_back(label, r, z, copy=nc.scalar.copy):
-            lo, hi = (PACK * (place(label, LAST, z) * P + w) for w in RANGES[label][r])
-            copy(out=back[label][:, lo:hi].rearrange("p (w j) -> p w j", j=PACK), in_=by_word(label, r, z)[:, :, :, LAST])
-
-        def quantize(key):
-            label, h = key
-            codes[key] = keep.tile([P, PASSES * P], U32, name=f"codes_{label}_{h}", align_bytes=64)
-            planes[key] = keep.tile([P, PASSES * P], U8, name=f"plane_{label}_{h}", align_bytes=64)
-            if h == LAST:
-                nc.vector.quantize_mx(out=codes[key][:].bitcast(FP8X4), scales=planes[key][:], in_=back[label])
-                return
+        operands = {}
+        back = {}
+        for label in "ey":
             for z in range(PASSES):
-                cols = slice(z * P, (z + 1) * P)
-                nc.vector.quantize_mx(
-                    out=codes[key][:, cols].bitcast(FP8X4),
-                    scales=planes[key][:, cols],
-                    in_=front[label, z][:, h * P * PACK : (h + 1) * P * PACK],
-                )
+                back[label, z] = keep.tile([P, 2 * P * PACK], BF16, name=f"back_{label}_{z}", align_bytes=64)
 
-        def one_pass(acc, key, z, points):
-            cols = slice(place(*key, z) * P, (place(*key, z) + 1) * P)
+        def quantize(name, source, width):
+            codes = keep.tile([P, width], U32, name=f"codes_{name}", align_bytes=64)
+            plane = keep.tile([P, width], U8, name=f"plane_{name}", align_bytes=64)
+            nc.vector.quantize_mx(out=codes[:].bitcast(FP8X4), scales=plane[:], in_=source)
+            return codes, plane
+
+        def prepare(label, r, z):
+            by_word = staged[label, r, z][:].rearrange("p (j w t) -> p w j t", j=PACK, t=PACK)
+            front = keep.tile([P, P * PACK], BF16, name=f"front_{label}_{r}_{z}", align_bytes=64)
+            nc.vector.tensor_copy(out=front[:].rearrange("p (t w j) -> p w j t", t=2, j=PACK), in_=by_word[:, :, :, :2])
+            nc.vector.tensor_copy(
+                out=back[label, z][:].rearrange("p (t w j) -> p w j t", t=2, j=PACK)[:, r * WORDS : (r + 1) * WORDS],
+                in_=by_word[:, :, :, 2:],
+            )
+            codes, plane = quantize(f"{label}_{r}_{z}", front[:], P)
+            operands[label, r, z] = (codes[:], plane[:])
+            if r == 1:
+                codes, plane = quantize(f"back_{label}_{z}", back[label, z][:], 2 * P)
+                for t in range(2):
+                    operands[label, 2 + t, z] = (codes[:, t * P : (t + 1) * P], plane[:, t * P : (t + 1) * P])
+
+        def one_pass(acc, label, h, z, points):
+            codes, plane = operands[label, h, z]
             nc.tensor.matmul_mx(
-                out=acc[:],
-                lhsT=codes[key][:, cols].bitcast(FP8X4),
-                lhsT_scale=planes[key][:, cols],
+                out=acc,
+                lhsT=codes.bitcast(FP8X4),
+                lhsT_scale=plane,
                 rhs=x_codes[z][:, points].bitcast(FP8X4),
                 rhs_scale=x_plane[:, z, points],
                 start=(z == 0),
@@ -167,275 +127,130 @@ def tile_picked_wedgecv_relu_l_kernel(
 
         everything = slice(0, T)
         halves = (slice(0, HALF), slice(HALF, T))
-        strips = [slice(b * P, (b + 1) * P) for b in range(STRIPS)]
-
-        def first_product():
-            parts = (halves[0], strips[2], strips[3])
-            banks = [psum.tile([P, HALF], F32, name="acc_e"), psum.tile([P, P], F32, name="acc_e")]
-            banks.append(psum.tile([P, P], F32, name="acc_y"))
-            for z in range(PASSES):
-                for acc, points in zip(banks, parts):
-                    one_pass(acc, ("e", 0), z, points)
-            for acc, points, copy in zip(banks, parts, (nc.vector.tensor_copy, nc.vector.tensor_copy, nc.scalar.copy)):
-                copy(out=windows[0][:, points], in_=acc[:])
-
-        def fresh(name):
-            return keep.tile([P, T], F32, name=name)[:]
-
-        first_room = rooms["e", 1, 1]
-        third_room = keep.tile([P, 2 * T], F32)
-        y_places = [third_room[:, :T], first_room[:, T : 2 * T], fresh("y_2"), fresh("y_3")]
         banks = {}
 
-        def multiply(key):
-            quantize(key)
-            if key in (("y", 2), ("y", LAST)):
-                banks[key] = psum_sums.tile([P, T], F32, name="total")
-            else:
-                banks[key] = psum.tile([P, T], F32, name=f"acc_{key[0]}")
-            for z in range(PASSES):
-                one_pass(banks[key], key, z, everything)
+        def multiply(label, tiles, z):
+            for h in tiles:
+                if z == 0:
+                    pool = psum_e if label == "e" else psum_y
+                    banks[label, h] = pool.tile([P, T], F32, name=f"acc_{label}")
+                one_pass(banks[label, h][:], label, h, z, everything)
 
-        def unload(key):
-            label, h = key
-            results[key] = windows[h][:, :T] if label == "e" else y_places[h]
-            nc.scalar.copy(out=results[key], in_=banks[key][:])
+        def fresh(name, dtype=F32):
+            return keep.tile([P, T], dtype, name=name)[:]
 
-        z_rows = late[:].bitcast(BF16).rearrange("p (b c) -> p b c", b=STRIPS)
-        base = [fresh(f"base_{h}") for h in range(LAST)]
-        other = [fresh(f"other_{h}") for h in range(LAST)]
-        larger = wide[:, T:]
-        gain = y_places[2]
-        diffs = [
-            {1: ahead["e", 1, 1], 3: third_room[:, T - 64 : 2 * T - 64]},
-            {1: first_room[:, 2 * T - 64 : 3 * T - 64], 3: third_room[:, T:]},
-            {1: wide[:, :T], 3: fresh("diff_2_3")},
-        ]
-        rises = [
-            {1: ahead["e", 2, 1], 3: first_room[:, 64 : T + 64]},
-            {1: windows[LAST][:, T:], 3: first_room[:, 3 * T - P : 4 * T - P]},
-        ]
-        rounded = {
-            (0, 1): first_room[:, 2 * T + 64 : 2 * T + 64 + HALF],
-            (0, 3): staged["y", 2, 0][:, :HALF],
-            (1, 1): keep.tile([P, HALF], F32, name="rounded_1_1")[:],
-            (1, 3): staged["y", 2, 0][:, HALF:T],
-        }
-        rounded = {key: place.bitcast(BF16).rearrange("p (b c) -> p b c", b=STRIPS) for key, place in rounded.items()}
-
-        def looked_up(d, h, part):
-            return windows[h][:].indirect(lists[d][:, part.start // PER_COLUMN : part.stop // PER_COLUMN])
-
-        def gather_base(h, part=everything):
-            nc.vector.tensor_copy(base[h][:, part], looked_up(4, h, part))
-
-        def gather_other(h):
-            nc.vector.tensor_copy(other[h], looked_up(2, h, everything))
-
-        def gather_diff(h, d, of, part=everything):
-            nc.vector.tensor_tensor(diffs[h][d][:, part], looked_up(d, h, part), of[:, part], ALU.subtract)
-
-        def add_turned(total, term, start, stop):
-            nc.tensor.matmul(total, term, ident[:], start=start, stop=stop, is_transpose=True)
-
-        def add_strips(total, term, which, start=False, stop=False):
-            for i, b in enumerate(which):
-                add_turned(total[:, i, :], term[:, strips[b]], start and i == 0, stop and i == len(which) - 1)
-
-        totals = {}
-
-        def open_pair(h, d):
-            totals[h, d] = psum_sums.tile([P, STRIPS, P], F32, name="total")
-            add_strips(totals[h, d], base[h] if d == 1 else other[h], range(STRIPS), start=True)
-
-        def rise(h, d):
-            nc.scalar.activation(rises[h][d], diffs[h][d], RELU)
-
-        def round_pair(h, d):
-            nc.scalar.activation(rounded[h, d], totals[h, d][:], RELU)
-
-        def join(h):
-            nc.vector.tensor_tensor(z_rows[:, :, h * P : (h + 1) * P], rounded[h, 1], rounded[h, 3], ALU.max)
-
-        pairs = (STRIP_ORDER[:2], STRIP_ORDER[2:])
-
-        def open_sums():
-            for pair in pairs:
-                totals[pair] = psum.tile([P, 2, P], F32, name="acc_e")
-                add_strips(totals[pair], results["y", 2], sorted(pair), start=True)
-
-        def close_sums():
-            for pair in pairs:
-                add_strips(totals[pair], gain, sorted(pair), stop=True)
-                nc.scalar.activation(z_rows[:, min(pair) : min(pair) + 2, 2 * P :], totals[pair][:], RELU)
-
+        fetched = {(h, d): fresh(f"fetched_{h}_{d}") for h in range(TILES) for d in range(4)}
+        low = [staged["y", 1, 0][:, :T]] + [fresh(f"low_{h}") for h in range(1, TILES)]
+        high = [staged["y", 1, 1][:, :T]] + [fresh(f"high_{h}") for h in range(1, TILES)]
+        top = [fresh(f"top_{h}") for h in range(TILES)]
+        slots = keep.tile([P, PACK, T], BF16)
+        spare = fresh("spare", BF16)
+        sums = [slots[:, 0, :], spare, slots[:, 2, :], slots[:, 3, :]]
         z_grouped = keep.tile([P, T, PACK], BF16, align_bytes=64)
 
-        def turn_back(pair):
-            turned = psum.tile([P, 2 * LAST, P], BF16, name="acc_y")
-            for i, b in enumerate(pair):
-                for t in range(LAST):
-                    nc.tensor.transpose(turned[:, i * LAST + t, :], z_rows[:, b, t::LAST], ident_bf16[:])
-            return turned
+        def gather(h, part):
+            for d in range(4):
+                offsets = lists[d][:, part.start // PER_COLUMN : part.stop // PER_COLUMN]
+                nc.scalar.activation(fetched[h, d][:, part], windows[h][:].indirect(offsets), COPY)
 
-        def group(turned, first, b, slots):
-            nc.scalar.copy(
-                out=z_grouped[:, strips[b], :slots], in_=turned[:, first : first + slots, :].rearrange("p t v -> p v t")
+        def pair(h, which, part):
+            target = (low, high)[which][h]
+            nc.vector.tensor_tensor(
+                target[:, part], fetched[h, 2 * which][:, part], fetched[h, 2 * which + 1][:, part], ALU.max
             )
 
-        def project(part, copy=nc.scalar.copy, codes_tag=None):
+        def join(h, part):
+            nc.vector.tensor_tensor(top[h][:, part], low[h][:, part], high[h][:, part], ALU.max)
+
+        def add(h, part):
+            nc.vector.tensor_tensor(sums[h][:, part], top[h][:, part], banks["y", h][:, part], ALU.add)
+
+        def weave(part, on_scalar=False):
+            source = slots[:, :, part].rearrange("p t v -> p v t")
+            if on_scalar:
+                nc.scalar.activation(z_grouped[:, part, :], source, RELU)
+            else:
+                nc.vector.tensor_scalar_max(z_grouped[:, part, :], source, 0.0)
+
+        def project(part):
             width = part.stop - part.start
-            z_codes = keep.tile([P, width], U32, name=codes_tag or f"z_codes_{part.start}", align_bytes=64)
-            z_plane = keep.tile([P, width], U8, name=f"z_plane_{part.start}", align_bytes=64)
-            nc.vector.quantize_mx(
-                out=z_codes[:].bitcast(FP8X4),
-                scales=z_plane[:],
-                in_=z_grouped[:, part, :].rearrange("p v t -> p (v t)"),
-            )
-            projected = psum_sums.tile([P, width], F32, name="total")
+            codes, plane = quantize(f"z_{part.start}", z_grouped[:, part, :].rearrange("p v t -> p (v t)"), width)
+            projected = psum_e.tile([P, width], F32, name="acc_e")
             nc.tensor.matmul_mx(
                 out=projected[:],
                 lhsT=w3_codes[:].bitcast(FP8X4),
                 lhsT_scale=w3_plane[:, 0, :],
-                rhs=z_codes[:].bitcast(FP8X4),
-                rhs_scale=z_plane[:],
+                rhs=codes[:].bitcast(FP8X4),
+                rhs_scale=plane[:],
                 start=True,
                 stop=True,
             )
             result = keep.tile([P, width], F32, name=f"result_{part.start}")
-            copy(out=result[:], in_=projected[:])
+            nc.scalar.copy(out=result[:], in_=projected[:])
             nc.sync.dma_start(out=out[:, part], in_=result[:])
 
-        def gather_sum(d, part, target):
-            nc.vector.tensor_tensor(target, looked_up(d, LAST, part), results["y", LAST][:, part], ALU.add)
-
-        cast_front("e", 0, 0, nc.vector.tensor_copy)
-        cast_front("e", 0, 1)
-        quantize(("e", 0))
-        first_product()
         for z in range(PASSES):
-            cast_back("e", 0, z)
-            cast_front("e", 1, z)
-            cast_back("e", 1, z, nc.scalar.copy if z else pool_cast)
+            prepare("e", 0, z)
+        first = [psum_e.tile([P, HALF], F32, name="acc_e"), psum_y.tile([P, HALF], F32, name="acc_y")]
         for z in range(PASSES):
-            cast_front("y", 0, z)
-        cast_back("y", 0, 1)
-
-        gather_base(0)
-        gather_other(0)
-        open_pair(0, 1)
-        open_pair(0, 3)
-        multiply(("e", 1))
-        unload(("e", 1))
-        gather_diff(0, 1, base[0])
-        gather_diff(0, 3, other[0])
-        multiply(("y", 0))
-        cast_back("y", 0, 0, pool_cast)
-        cast_back("e", 2, 0, pool_cast)
-        cast_back("y", 1, 0, pool_cast)
+            for acc, points in zip(first, halves):
+                one_pass(acc[:], "e", 0, z, points)
+        nc.vector.tensor_copy(out=windows[0][:, halves[0]], in_=first[0][:])
+        nc.scalar.copy(out=windows[0][:, halves[1]], in_=first[1][:])
+        gather(0, everything)
         for z in range(PASSES):
-            cast_front("e", 2, z)
-        cast_back("e", 2, 1)
-        rise(0, 1)
-        rise(0, 3)
-        unload(("y", 0))
-        for d in (1, 3):
-            add_strips(totals[0, d], rises[0][d], range(STRIPS))
-        for d in (1, 3):
-            add_strips(totals[0, d], results["y", 0], range(STRIPS), stop=True)
-        cast_front("y", 1, 0)
-        cast_front("y", 1, 1)
-        cast_back("y", 1, 1)
-
-        gather_base(1)
-        gather_other(1)
-        open_pair(1, 1)
-        open_pair(1, 3)
-        multiply(("e", 2))
-        unload(("e", 2))
-        gather_diff(1, 1, base[1])
-        gather_diff(1, 3, other[1])
-        multiply(("e", 3))
-        multiply(("y", 1))
-        unread = psum.tile([P, T], F32, name="acc_y")
+            prepare("e", 1, z)
+            multiply("e", (1, 2, 3), z)
+        nc.scalar.copy(out=windows[1][:, :T], in_=banks["e", 1][:])
+        gather(1, everything)
         for z in range(PASSES):
-            one_pass(unread, ("y", 1), z, everything)
+            prepare("y", 0, z)
+            multiply("y", (0,), z)
+            nc.vector.tensor_copy(out=windows[2 + z][:, :T], in_=banks["e", 2 + z][:])
         for z in range(PASSES):
-            cast_front("y", 2, z)
-            cast_back("y", 2, z)
-        rise(1, 1)
-        unload(("y", 1))
-        rise(1, 3)
-        round_pair(0, 1)
-        round_pair(0, 3)
-        for d in (1, 3):
-            add_strips(totals[1, d], rises[1][d], range(STRIPS))
-        for d in (1, 3):
-            add_strips(totals[1, d], results["y", 1], range(STRIPS), stop=True)
-        unload(("e", 3))
+            prepare("y", 1, z)
+            multiply("y", (1, 2, 3), z)
+            pair(0, z, everything)
 
-        gather_base(2)
-        gather_other(2)
-        multiply(("y", 2))
-        multiply(("y", 3))
-        nc.vector.tensor_tensor(larger, base[2], other[2], ALU.max)
-        round_pair(1, 1)
-        round_pair(1, 3)
-        unload(("y", 2))
-        unload(("y", 3))
-        gather_diff(2, 1, larger)
-        open_sums()
-        for pair in pairs:
-            add_strips(totals[pair], larger, sorted(pair))
-        gather_diff(2, 3, larger)
-        join(0)
-        join(1)
-        for part in halves:
-            nc.vector.scalar_tensor_tensor(
-                gain[:, part], diffs[2][1][:, part], 0.0, diffs[2][3][:, part], ALU.max, ALU.max
-            )
-        close_sums()
+        pieces = (halves[0], slice(HALF, HALF + P), slice(HALF + P, T))
+        gather(2, halves[0])
+        gather(3, halves[0])
+        gather(2, halves[1])
+        gather(3, pieces[1])
+        gather(3, pieces[2])
 
-        pieces = (halves[0], strips[2], strips[3])
-        sum1, sum2, sum3 = windows[2][:, T : 2 * T], fresh("sum_2"), fresh("sum_3")
-        rounded1 = gain[:, HALF:].bitcast(BF16)
-        rounded2 = late[:, :HALF].bitcast(BF16)
-        rounded3 = late[:, HALF : HALF + P].bitcast(BF16)
-        of_two = keep.tile([P, T], BF16)
-        of_three = keep.tile([P, T], BF16)
-        z_last = keep.tile([P, T - P], BF16, name="z_last", align_bytes=64)
-        sum4 = [sum3[:, part] for part in pieces]
-
-        def of_four(i, target):
-            nc.vector.tensor_tensor(target, sum4[i], of_three[:, pieces[i]], ALU.max)
-
-        def weave(i):
-            nc.scalar.copy(out=z_grouped[:, pieces[i], LAST], in_=z_last[:, pieces[i]])
-
-        gather_sum(1, everything, sum1)
-        nc.scalar.activation(rounded1, sum1, RELU)
-        gather_sum(2, everything, sum2)
-        turned = turn_back(STRIP_ORDER[:2])
-        group(turned, 0, STRIP_ORDER[0], LAST)
-        nc.scalar.activation(rounded2, sum2, RELU)
-        for part in halves:
-            gather_sum(3, part, sum3[:, part])
-        nc.scalar.activation(rounded3, sum3[:, halves[0]], RELU)
-        group(turned, LAST, STRIP_ORDER[1], LAST)
-        turned = turn_back(STRIP_ORDER[2:])
-        group(turned, 0, STRIP_ORDER[2], PACK)
-        group(turned, LAST, STRIP_ORDER[3], LAST)
-        nc.vector.tensor_tensor(of_two[:], rounded1, rounded2, ALU.max)
-        gather_sum(4, pieces[0], sum4[0])
-        nc.vector.tensor_tensor(of_three[:, halves[0]], of_two[:, halves[0]], rounded3, ALU.max)
-        nc.vector.tensor_tensor(of_three[:, halves[1]], sum3[:, halves[1]], of_two[:, halves[1]], ALU.max)
-        of_four(0, z_last[:, pieces[0]])
-        weave(0)
-        gather_sum(4, pieces[1], sum4[1])
-        gather_sum(4, pieces[2], sum4[2])
-        of_four(1, z_last[:, pieces[1]])
-        weave(1)
-        of_four(2, z_grouped[:, pieces[2], LAST])
+        pair(1, 0, everything)
+        join(0, everything)
+        pair(1, 1, everything)
+        add(0, everything)
+        nc.sync.dma_start(out=slots[:WORDS, 1, :], in_=slots[WORDS:, 0, :])
+        join(1, everything)
+        pair(2, 0, halves[0])
+        add(1, everything)
+        nc.sync.dma_start(out=slots[WORDS:, 0, :], in_=spare[:WORDS, :])
+        nc.sync.dma_start(out=slots[WORDS:, 1, :], in_=spare[WORDS:, :])
+        pair(2, 1, halves[0])
+        pair(3, 0, halves[0])
+        join(2, halves[0])
+        pair(3, 1, halves[0])
+        add(2, halves[0])
+        join(3, halves[0])
+        pair(2, 0, halves[1])
+        add(3, halves[0])
+        pair(2, 1, halves[1])
+        weave(pieces[0])
+        join(2, halves[1])
         project(pieces[0])
-        project(pieces[2], codes_tag="z_last")
-        project(pieces[1], nc.vector.tensor_copy)
+        add(2, halves[1])
+        pair(3, 0, pieces[1])
+        pair(3, 1, pieces[1])
+        pair(3, 0, pieces[2])
+        join(3, pieces[1])
+        pair(3, 1, pieces[2])
+        add(3, pieces[1])
+        join(3, pieces[2])
+        weave(pieces[1], on_scalar=True)
+        add(3, pieces[2])
+        project(pieces[1])
+        weave(pieces[2])
+        project(pieces[2])

@@ -36,11 +36,11 @@ def tile_picked_wedgecv_relu_l_kernel(
         psum_y = ctx.enter_context(tc.psum_pool(name="psum_y", bufs=4))
 
         staged = {}
-        for label in "ey":
-            for r in range(2):
-                for z in range(PASSES):
-                    staged[label, r, z] = keep.tile([P, 2 * T], F32, name=f"staged_{label}_{r}_{z}")
-        windows = [staged["e", 0, 0], staged["e", 0, 1], staged["y", 0, 0], staged["y", 0, 1]]
+        for label, r, z in (("e", 0, 0), ("e", 0, 1), ("e", 1, 0), ("e", 1, 1), ("y", 0, 0), ("y", 1, 0), ("y", 0, 1)):
+            staged[label, r, z] = keep.tile([P, 2 * T], F32, name=f"staged_{label}_{r}_{z}")
+        windows = [staged["e", r, z] for r in range(2) for z in range(PASSES)]
+        pair_room = keep.tile([P, 4 * T], F32)
+        staged["y", 1, 1] = pair_room[:, T : 3 * T]
 
         def load_weights(label, r, z):
             w = w2 if label == "e" else w1
@@ -64,22 +64,32 @@ def tile_picked_wedgecv_relu_l_kernel(
             lists[d] = keep.tile([P, T // PER_COLUMN], U16, name=f"list_{d}")
             nc.sync.dma_start(lists[d][:], pos)
 
+        everything = slice(0, T)
+        halves = (slice(0, HALF), slice(HALF, T))
+        pieces = (halves[0], slice(HALF, HALF + P), slice(HALF + P, T))
+
         x_plane = keep.tile([P, PASSES, T], U8, align_bytes=64)
+        x_codes = [keep.tile([P, T], U32, name=f"x_codes_{z}", align_bytes=64) for z in range(PASSES)]
+
+        def load_x(z, points):
+            words = x_words[z].rearrange("p c r -> p (c r)").bitcast(I32)
+            nc.sync.dma_start(out=x_codes[z][:, points].bitcast(I32), in_=words[:, points])
+
         load_weights("e", 0, 0)
         load_scale_rows(x_plane, x_scales, nc.sync)
+        load_x(0, halves[0])
         load_weights("e", 0, 1)
-        x_codes = []
-        for z in range(PASSES):
-            x_codes.append(keep.tile([P, T], U32, name=f"x_codes_{z}", align_bytes=64))
-            nc.sync.dma_start(out=x_codes[z][:].bitcast(I32), in_=x_words[z].rearrange("p c r -> p (c r)").bitcast(I32))
+        load_x(0, halves[1])
+        load_x(1, halves[0])
+        load_x(1, halves[1])
         load_list(0, pos1)
-        load_list(1, pos2)
         load_weights("e", 1, 0)
+        load_list(1, pos2)
+        load_weights("e", 1, 1)
         load_list(2, pos3)
         load_list(3, pos4)
-        load_weights("e", 1, 1)
-        for r in range(2):
-            for z in range(PASSES):
+        for z in range(PASSES):
+            for r in range(2):
                 load_weights("y", r, z)
         w3_codes = keep.tile([P, N], U32, align_bytes=64)
         nc.sync.dma_start(out=w3_codes[:].bitcast(I32), in_=w3_words[0].rearrange("p c r -> p (c r)").bitcast(I32))
@@ -87,10 +97,10 @@ def tile_picked_wedgecv_relu_l_kernel(
         load_scale_rows(w3_plane, w3_scales, nc.sync)
 
         operands = {}
-        back = {}
-        for label in "ey":
-            for z in range(PASSES):
-                back[label, z] = keep.tile([P, 2 * P * PACK], BF16, name=f"back_{label}_{z}", align_bytes=64)
+        room = keep.tile([P, 6 * T], F32, align_bytes=64)
+        rounded = {("e", 1): room[:, 3 * T : 5 * T].bitcast(BF16), ("y", 0): room[:, 4 * T :].bitcast(BF16)}
+        for key in (("e", 0), ("y", 1)):
+            rounded[key] = keep.tile([P, TILES * K_PASS], BF16, name="rounded_%s_%d" % key, align_bytes=64)[:]
 
         def quantize(name, source, width):
             codes = keep.tile([P, width], U32, name=f"codes_{name}", align_bytes=64)
@@ -98,20 +108,24 @@ def tile_picked_wedgecv_relu_l_kernel(
             nc.vector.quantize_mx(out=codes[:].bitcast(FP8X4), scales=plane[:], in_=source)
             return codes, plane
 
-        def prepare(label, r, z):
-            by_word = staged[label, r, z][:].rearrange("p (j w t) -> p w j t", j=PACK, t=PACK)
-            front = keep.tile([P, P * PACK], BF16, name=f"front_{label}_{r}_{z}", align_bytes=64)
-            nc.vector.tensor_copy(out=front[:].rearrange("p (t w j) -> p w j t", t=2, j=PACK), in_=by_word[:, :, :, :2])
-            nc.vector.tensor_copy(
-                out=back[label, z][:].rearrange("p (t w j) -> p w j t", t=2, j=PACK)[:, r * WORDS : (r + 1) * WORDS],
-                in_=by_word[:, :, :, 2:],
-            )
-            codes, plane = quantize(f"{label}_{r}_{z}", front[:], P)
-            operands[label, r, z] = (codes[:], plane[:])
-            if r == 1:
-                codes, plane = quantize(f"back_{label}_{z}", back[label, z][:], 2 * P)
-                for t in range(2):
-                    operands[label, 2 + t, z] = (codes[:, t * P : (t + 1) * P], plane[:, t * P : (t + 1) * P])
+        def quantize_tiles(label, z, first, last):
+            source = rounded[label, z][:, first * K_PASS : last * K_PASS]
+            codes, plane = quantize(f"{label}_{z}_{first}", source, (last - first) * P)
+            for h in range(first, last):
+                cols = slice((h - first) * P, (h - first + 1) * P)
+                operands[label, h, z] = (codes[:, cols], plane[:, cols])
+
+        def cast(label, r, z, on_gpsimd=False):
+            by_word = staged[label, r, z][:].rearrange("p (j w t) -> p w t j", j=PACK, t=PACK)
+            front = rounded[label, z][:, r * K_PASS : (r + 1) * K_PASS].rearrange("p (t w j) -> p w t j", t=2, j=PACK)
+            back = rounded[label, z][:, 2 * K_PASS :].rearrange("p (t w j) -> p w t j", t=2, j=PACK)
+            back = back[:, r * WORDS : (r + 1) * WORDS]
+            for target, source in ((front, by_word[:, :, :2, :]), (back, by_word[:, :, 2:, :])):
+                if on_gpsimd:
+                    nc.gpsimd.tensor_scalar(target, source, 1.0, 0.0, ALU.mult, ALU.add)
+                else:
+                    order = "p w t j -> p w j t"
+                    nc.vector.tensor_copy(out=target.rearrange(order), in_=source.rearrange(order))
 
         def one_pass(acc, label, h, z, points):
             codes, plane = operands[label, h, z]
@@ -125,8 +139,6 @@ def tile_picked_wedgecv_relu_l_kernel(
                 stop=(z == PASSES - 1),
             )
 
-        everything = slice(0, T)
-        halves = (slice(0, HALF), slice(HALF, T))
         banks = {}
 
         def multiply(label, tiles, z):
@@ -136,31 +148,37 @@ def tile_picked_wedgecv_relu_l_kernel(
                     banks[label, h] = pool.tile([P, T], F32, name=f"acc_{label}")
                 one_pass(banks[label, h][:], label, h, z, everything)
 
-        def fresh(name, dtype=F32):
-            return keep.tile([P, T], dtype, name=name)[:]
+        def fresh(name, rows=1):
+            return keep.tile([P, rows * T], F32, name=name)[:]
 
-        fetched = {(h, d): fresh(f"fetched_{h}_{d}") for h in range(TILES) for d in range(4)}
-        low = [staged["y", 1, 0][:, :T]] + [fresh(f"low_{h}") for h in range(1, TILES)]
-        high = [staged["y", 1, 1][:, :T]] + [fresh(f"high_{h}") for h in range(1, TILES)]
+        fetched = [room[:, : 4 * T] if h == 0 else fresh(f"fetched_{h}", 4) for h in range(TILES)]
+        fetched = [place.rearrange("p (d v) -> p d v", d=4) for place in fetched]
+        paired = [pair_room[:, : 2 * T], pair_room[:, 2 * T :]] * 2
+        paired = [place.rearrange("p (i v) -> p i v", i=2) for place in paired]
         top = [fresh(f"top_{h}") for h in range(TILES)]
         slots = keep.tile([P, PACK, T], BF16)
-        spare = fresh("spare", BF16)
-        sums = [slots[:, 0, :], spare, slots[:, 2, :], slots[:, 3, :]]
+        spare = keep.tile([P, T], BF16)
+        sums = [slots[:, 0, :], spare[:], slots[:, 2, :], slots[:, 3, :]]
         z_grouped = keep.tile([P, T, PACK], BF16, align_bytes=64)
 
-        def gather(h, part):
-            for d in range(4):
-                offsets = lists[d][:, part.start // PER_COLUMN : part.stop // PER_COLUMN]
-                nc.scalar.activation(fetched[h, d][:, part], windows[h][:].indirect(offsets), COPY)
+        def looked_up(h, d, part):
+            return windows[h][:].indirect(lists[d][:, part.start // PER_COLUMN : part.stop // PER_COLUMN])
 
-        def pair(h, which, part):
-            target = (low, high)[which][h]
-            nc.vector.tensor_tensor(
-                target[:, part], fetched[h, 2 * which][:, part], fetched[h, 2 * which + 1][:, part], ALU.max
-            )
+        def gather(h, part, which=range(4)):
+            for d in which:
+                nc.scalar.activation(fetched[h][:, d, part], looked_up(h, d, part), COPY)
+
+        def gather_on_vector(h, d, target):
+            nc.vector.tensor_copy(target, looked_up(h, d, everything))
+
+        def pair(h, part):
+            nc.vector.tensor_tensor(paired[h][:, :, part], fetched[h][:, :2, part], fetched[h][:, 2:, part], ALU.max)
+
+        def larger(target, one, other, part):
+            nc.vector.tensor_tensor(target[:, part], one[:, part], other[:, part], ALU.max)
 
         def join(h, part):
-            nc.vector.tensor_tensor(top[h][:, part], low[h][:, part], high[h][:, part], ALU.max)
+            larger(top[h], paired[h][:, 0, :], paired[h][:, 1, :], part)
 
         def add(h, part):
             nc.vector.tensor_tensor(sums[h][:, part], top[h][:, part], banks["y", h][:, part], ALU.add)
@@ -172,7 +190,7 @@ def tile_picked_wedgecv_relu_l_kernel(
             else:
                 nc.vector.tensor_scalar_max(z_grouped[:, part, :], source, 0.0)
 
-        def project(part):
+        def project(part, copy=nc.scalar.copy):
             width = part.stop - part.start
             codes, plane = quantize(f"z_{part.start}", z_grouped[:, part, :].rearrange("p v t -> p (v t)"), width)
             projected = psum_e.tile([P, width], F32, name="acc_e")
@@ -186,71 +204,75 @@ def tile_picked_wedgecv_relu_l_kernel(
                 stop=True,
             )
             result = keep.tile([P, width], F32, name=f"result_{part.start}")
-            nc.scalar.copy(out=result[:], in_=projected[:])
+            copy(out=result[:], in_=projected[:])
             nc.sync.dma_start(out=out[:, part], in_=result[:])
 
-        for z in range(PASSES):
-            prepare("e", 0, z)
+        def unload(h):
+            nc.vector.tensor_copy(out=windows[h][:, :T], in_=banks["e", h][:])
+
         first = [psum_e.tile([P, HALF], F32, name="acc_e"), psum_y.tile([P, HALF], F32, name="acc_y")]
         for z in range(PASSES):
+            cast("e", 0, z)
+            quantize_tiles("e", z, 0, 1)
             for acc, points in zip(first, halves):
                 one_pass(acc[:], "e", 0, z, points)
-        nc.vector.tensor_copy(out=windows[0][:, halves[0]], in_=first[0][:])
-        nc.scalar.copy(out=windows[0][:, halves[1]], in_=first[1][:])
-        gather(0, everything)
+        for acc, points, copy in zip(first, halves, (nc.scalar.copy, nc.vector.tensor_copy)):
+            copy(out=windows[0][:, points], in_=acc[:])
+        gather(0, everything, (0, 1, 2))
         for z in range(PASSES):
-            prepare("e", 1, z)
+            cast("e", 1, z)
+            quantize_tiles("e", z, 1, 2)
+            quantize_tiles("e", z, 2, TILES)
             multiply("e", (1, 2, 3), z)
-        nc.scalar.copy(out=windows[1][:, :T], in_=banks["e", 1][:])
-        gather(1, everything)
-        for z in range(PASSES):
-            prepare("y", 0, z)
-            multiply("y", (0,), z)
-            nc.vector.tensor_copy(out=windows[2 + z][:, :T], in_=banks["e", 2 + z][:])
-        for z in range(PASSES):
-            prepare("y", 1, z)
-            multiply("y", (1, 2, 3), z)
-            pair(0, z, everything)
+        cast("y", 0, 0, on_gpsimd=True)
+        cast("y", 1, 0, on_gpsimd=True)
+        cast("y", 0, 1, on_gpsimd=True)
+        gather_on_vector(0, 3, fetched[0][:, 3, :])
+        unload(1)
+        unload(2)
+        gather_on_vector(1, 3, fetched[1][:, 3, :])
+        unload(3)
+        gather(1, everything, (0, 1, 2))
+        quantize_tiles("y", 0, 0, TILES)
+        multiply("y", range(TILES), 0)
+        cast("y", 1, 1)
+        quantize_tiles("y", 1, 0, 2)
+        quantize_tiles("y", 1, 2, TILES)
+        multiply("y", range(TILES), 1)
 
-        pieces = (halves[0], slice(HALF, HALF + P), slice(HALF + P, T))
-        gather(2, halves[0])
+        gather(2, everything)
         gather(3, halves[0])
-        gather(2, halves[1])
-        gather(3, pieces[1])
-        gather(3, pieces[2])
+        gather(3, halves[1], (0, 1, 2))
+        gather(3, pieces[1], (3,))
+        gather(3, pieces[2], (3,))
 
-        pair(1, 0, everything)
+        low, high = ([paired[h][:, i, :] for h in range(TILES)] for i in range(2))
+        pair(0, everything)
+        pair(1, everything)
         join(0, everything)
-        pair(1, 1, everything)
+        join(1, everything)
         add(0, everything)
         nc.sync.dma_start(out=slots[:WORDS, 1, :], in_=slots[WORDS:, 0, :])
-        join(1, everything)
-        pair(2, 0, halves[0])
+        larger(low[2], fetched[2][:, 0, :], fetched[2][:, 1, :], everything)
         add(1, everything)
         nc.sync.dma_start(out=slots[WORDS:, 0, :], in_=spare[:WORDS, :])
         nc.sync.dma_start(out=slots[WORDS:, 1, :], in_=spare[WORDS:, :])
-        pair(2, 1, halves[0])
-        pair(3, 0, halves[0])
-        join(2, halves[0])
-        pair(3, 1, halves[0])
-        add(2, halves[0])
-        join(3, halves[0])
-        pair(2, 0, halves[1])
+        larger(high[2], fetched[2][:, 2, :], fetched[2][:, 3, :], everything)
+        larger(low[3], fetched[3][:, 0, :], fetched[3][:, 1, :], halves[0])
+        join(2, everything)
+        larger(high[3], low[3], fetched[3][:, 2, :], halves[0])
+        add(2, everything)
+        larger(top[3], high[3], fetched[3][:, 3, :], halves[0])
+        larger(low[3], fetched[3][:, 0, :], fetched[3][:, 1, :], halves[1])
         add(3, halves[0])
-        pair(2, 1, halves[1])
-        weave(pieces[0])
-        join(2, halves[1])
-        project(pieces[0])
-        add(2, halves[1])
-        pair(3, 0, pieces[1])
-        pair(3, 1, pieces[1])
-        pair(3, 0, pieces[2])
-        join(3, pieces[1])
-        pair(3, 1, pieces[2])
+        weave(pieces[0], on_scalar=True)
+        larger(high[3], low[3], fetched[3][:, 2, :], halves[1])
+        larger(top[3], high[3], fetched[3][:, 3, :], pieces[1])
+        larger(top[3], high[3], fetched[3][:, 3, :], pieces[2])
         add(3, pieces[1])
-        join(3, pieces[2])
-        weave(pieces[1], on_scalar=True)
         add(3, pieces[2])
-        project(pieces[1])
+        weave(pieces[1], on_scalar=True)
         weave(pieces[2])
-        project(pieces[2])
+        project(pieces[0])
+        project(pieces[2], nc.vector.tensor_copy)
+        project(pieces[1])

@@ -36,19 +36,24 @@ def tile_picked_wedgecv_relu_l_kernel(
         psum_y = ctx.enter_context(tc.psum_pool(name="psum_y", bufs=4))
 
         staged = {}
-        for label, r, z in (("e", 0, 0), ("e", 0, 1), ("e", 1, 0), ("e", 1, 1), ("y", 0, 0), ("y", 1, 0), ("y", 0, 1)):
-            staged[label, r, z] = keep.tile([P, 2 * T], F32, name=f"staged_{label}_{r}_{z}")
+        for r in range(2):
+            for z in range(PASSES):
+                staged["e", r, z] = keep.tile([P, 2 * T], F32, name=f"staged_e_{r}_{z}")
         windows = [staged["e", r, z] for r in range(2) for z in range(PASSES)]
-        pair_room = keep.tile([P, 4 * T], F32)
-        staged["y", 1, 1] = pair_room[:, T : 3 * T]
+        staged["y", 0] = keep.tile([P, 4 * T], F32, name="staged_y_0")[:]
+        late_room = keep.tile([P, 10 * T + HALF], F32)
+        staged["y", 1] = late_room[:, 3 * T + HALF : 7 * T + HALF]
 
-        def load_weights(label, r, z):
-            w = w2 if label == "e" else w1
-            rows = w[z * K_PASS : (z + 1) * K_PASS, r * HALF : (r + 1) * HALF]
+        def load_w2(r, z):
+            rows = w2[z * K_PASS : (z + 1) * K_PASS, r * HALF : (r + 1) * HALF]
             nc.sync.dma_start(
-                out=staged[label, r, z][:].rearrange("p (j c) -> p j c", j=PACK),
+                out=staged["e", r, z][:].rearrange("p (j c) -> p j c", j=PACK),
                 in_=rows.rearrange("(p j) c -> p j c", j=PACK),
             )
+
+        def load_w1(z):
+            rows = w1[z * K_PASS : (z + 1) * K_PASS, :]
+            nc.sync.dma_start(out=staged["y", z], in_=rows.rearrange("(p j) c -> p (j c)", j=PACK))
 
         def load_scale_rows(plane, scales, queue):
             nc.gpsimd.memset(plane[:].bitcast(I32), 0)
@@ -75,31 +80,30 @@ def tile_picked_wedgecv_relu_l_kernel(
             words = x_words[z].rearrange("p c r -> p (c r)").bitcast(I32)
             nc.sync.dma_start(out=x_codes[z][:, points].bitcast(I32), in_=words[:, points])
 
-        load_weights("e", 0, 0)
+        load_w2(0, 0)
         load_scale_rows(x_plane, x_scales, nc.sync)
         load_x(0, halves[0])
-        load_weights("e", 0, 1)
+        load_w2(0, 1)
         load_x(0, halves[1])
         load_x(1, halves[0])
         load_x(1, halves[1])
         load_list(0, pos1)
-        load_weights("e", 1, 0)
+        load_w2(1, 0)
         load_list(1, pos2)
-        load_weights("e", 1, 1)
+        load_w2(1, 1)
         load_list(2, pos3)
         load_list(3, pos4)
         for z in range(PASSES):
-            for r in range(2):
-                load_weights("y", r, z)
+            load_w1(z)
         w3_codes = keep.tile([P, N], U32, align_bytes=64)
         nc.sync.dma_start(out=w3_codes[:].bitcast(I32), in_=w3_words[0].rearrange("p c r -> p (c r)").bitcast(I32))
         w3_plane = keep.tile([P, 1, N], U8, align_bytes=64)
         load_scale_rows(w3_plane, w3_scales, nc.sync)
 
         operands = {}
-        room = keep.tile([P, 6 * T], F32, align_bytes=64)
-        rounded = {("e", 1): room[:, 3 * T : 5 * T].bitcast(BF16), ("y", 0): room[:, 4 * T :].bitcast(BF16)}
-        for key in (("e", 0), ("y", 1)):
+        room = keep.tile([P, 5 * T], F32, align_bytes=64)
+        rounded = {("e", 1): room[:, 3 * T :].bitcast(BF16)}
+        for key in (("e", 0), ("y", 0), ("y", 1)):
             rounded[key] = keep.tile([P, TILES * K_PASS], BF16, name="rounded_%s_%d" % key, align_bytes=64)[:]
 
         def quantize(name, source, width):
@@ -115,17 +119,19 @@ def tile_picked_wedgecv_relu_l_kernel(
                 cols = slice((h - first) * P, (h - first + 1) * P)
                 operands[label, h, z] = (codes[:, cols], plane[:, cols])
 
-        def cast(label, r, z, on_gpsimd=False):
-            by_word = staged[label, r, z][:].rearrange("p (j w t) -> p w t j", j=PACK, t=PACK)
-            front = rounded[label, z][:, r * K_PASS : (r + 1) * K_PASS].rearrange("p (t w j) -> p w t j", t=2, j=PACK)
-            back = rounded[label, z][:, 2 * K_PASS :].rearrange("p (t w j) -> p w t j", t=2, j=PACK)
-            back = back[:, r * WORDS : (r + 1) * WORDS]
-            for target, source in ((front, by_word[:, :, :2, :]), (back, by_word[:, :, 2:, :])):
-                if on_gpsimd:
-                    nc.gpsimd.tensor_scalar(target, source, 1.0, 0.0, ALU.mult, ALU.add)
-                else:
-                    order = "p w t j -> p w j t"
-                    nc.vector.tensor_copy(out=target.rearrange(order), in_=source.rearrange(order))
+        def cast_w2(r, z):
+            by_word = staged["e", r, z][:].rearrange("p (j w t) -> p w j t", j=PACK, t=PACK)
+            front = rounded["e", z][:, r * K_PASS : (r + 1) * K_PASS].rearrange("p (t w j) -> p w j t", t=2, j=PACK)
+            back = rounded["e", z][:, 2 * K_PASS :].rearrange("p (t w j) -> p w j t", t=2, j=PACK)
+            nc.vector.tensor_copy(out=front, in_=by_word[:, :, :, :2])
+            nc.vector.tensor_copy(out=back[:, r * WORDS : (r + 1) * WORDS], in_=by_word[:, :, :, 2:])
+
+        def cast_w1(z):
+            by_word = staged["y", z].rearrange("p (j r w t) -> p r w j t", j=PACK, r=2, t=PACK)
+            front = rounded["y", z][:, : 2 * K_PASS].rearrange("p (r t w j) -> p r w j t", r=2, t=2, j=PACK)
+            back = rounded["y", z][:, 2 * K_PASS :].rearrange("p (t r w j) -> p r w j t", r=2, t=2, j=PACK)
+            nc.vector.tensor_copy(out=front, in_=by_word[:, :, :, :, :2])
+            nc.vector.tensor_copy(out=back, in_=by_word[:, :, :, :, 2:])
 
         def one_pass(acc, label, h, z, points):
             codes, plane = operands[label, h, z]
@@ -151,9 +157,9 @@ def tile_picked_wedgecv_relu_l_kernel(
         def fresh(name, rows=1):
             return keep.tile([P, rows * T], F32, name=name)[:]
 
-        fetched = [room[:, : 4 * T] if h == 0 else fresh(f"fetched_{h}", 4) for h in range(TILES)]
+        fetched = [room[:, : 4 * T], late_room[:, : 4 * T], late_room[:, 6 * T + HALF :], fresh("fetched_3", 4)]
         fetched = [place.rearrange("p (d v) -> p d v", d=4) for place in fetched]
-        paired = [pair_room[:, : 2 * T], pair_room[:, 2 * T :]] * 2
+        paired = [late_room[:, 4 * T : 6 * T], fresh("paired_1", 2)] * 2
         paired = [place.rearrange("p (i v) -> p i v", i=2) for place in paired]
         top = [fresh(f"top_{h}") for h in range(TILES)]
         slots = keep.tile([P, PACK, T], BF16)
@@ -208,11 +214,11 @@ def tile_picked_wedgecv_relu_l_kernel(
             nc.sync.dma_start(out=out[:, part], in_=result[:])
 
         def unload(h):
-            nc.vector.tensor_copy(out=windows[h][:, :T], in_=banks["e", h][:])
+            nc.scalar.copy(out=windows[h][:, :T], in_=banks["e", h][:])
 
         first = [psum_e.tile([P, HALF], F32, name="acc_e"), psum_y.tile([P, HALF], F32, name="acc_y")]
         for z in range(PASSES):
-            cast("e", 0, z)
+            cast_w2(0, z)
             quantize_tiles("e", z, 0, 1)
             for acc, points in zip(first, halves):
                 one_pass(acc[:], "e", 0, z, points)
@@ -220,27 +226,24 @@ def tile_picked_wedgecv_relu_l_kernel(
             copy(out=windows[0][:, points], in_=acc[:])
         gather(0, everything, (0, 1, 2))
         for z in range(PASSES):
-            cast("e", 1, z)
+            cast_w2(1, z)
             quantize_tiles("e", z, 1, 2)
             quantize_tiles("e", z, 2, TILES)
             multiply("e", (1, 2, 3), z)
-        cast("y", 0, 0, on_gpsimd=True)
-        cast("y", 1, 0, on_gpsimd=True)
-        cast("y", 0, 1, on_gpsimd=True)
         gather_on_vector(0, 3, fetched[0][:, 3, :])
         unload(1)
-        unload(2)
-        gather_on_vector(1, 3, fetched[1][:, 3, :])
-        unload(3)
         gather(1, everything, (0, 1, 2))
-        quantize_tiles("y", 0, 0, TILES)
-        multiply("y", range(TILES), 0)
-        cast("y", 1, 1)
-        quantize_tiles("y", 1, 0, 2)
-        quantize_tiles("y", 1, 2, TILES)
-        multiply("y", range(TILES), 1)
+        for z in range(PASSES):
+            cast_w1(z)
+            quantize_tiles("y", z, 0, 2)
+            quantize_tiles("y", z, 2, TILES)
+            multiply("y", range(TILES), z)
+        gather_on_vector(1, 3, fetched[1][:, 3, :])
 
-        gather(2, everything)
+        unload(2)
+        gather_on_vector(2, 0, fetched[2][:, 0, :])
+        gather(2, everything, (1, 2, 3))
+        unload(3)
         gather(3, halves[0])
         gather(3, halves[1], (0, 1, 2))
         gather(3, pieces[1], (3,))
@@ -253,11 +256,10 @@ def tile_picked_wedgecv_relu_l_kernel(
         join(1, everything)
         add(0, everything)
         nc.sync.dma_start(out=slots[:WORDS, 1, :], in_=slots[WORDS:, 0, :])
-        larger(low[2], fetched[2][:, 0, :], fetched[2][:, 1, :], everything)
         add(1, everything)
         nc.sync.dma_start(out=slots[WORDS:, 0, :], in_=spare[:WORDS, :])
         nc.sync.dma_start(out=slots[WORDS:, 1, :], in_=spare[WORDS:, :])
-        larger(high[2], fetched[2][:, 2, :], fetched[2][:, 3, :], everything)
+        pair(2, everything)
         larger(low[3], fetched[3][:, 0, :], fetched[3][:, 1, :], halves[0])
         join(2, everything)
         larger(high[3], low[3], fetched[3][:, 2, :], halves[0])

@@ -40,9 +40,9 @@ def tile_picked_wedgecv_relu_l_kernel(
             for z in range(PASSES):
                 staged["e", r, z] = keep.tile([P, 2 * T], F32, name=f"staged_e_{r}_{z}")
         windows = [staged["e", r, z] for r in range(2) for z in range(PASSES)]
-        staged["y", 0] = keep.tile([P, 4 * T], F32, name="staged_y_0")[:]
-        late_room = keep.tile([P, 10 * T + HALF], F32)
-        staged["y", 1] = late_room[:, 3 * T + HALF : 7 * T + HALF]
+        rooms = [keep.tile([P, 7 * T], F32, name=f"room_{z}") for z in range(PASSES)]
+        for z in range(PASSES):
+            staged["y", z] = rooms[z][:, 3 * T :]
 
         def load_w2(r, z):
             rows = w2[z * K_PASS : (z + 1) * K_PASS, r * HALF : (r + 1) * HALF]
@@ -121,17 +121,17 @@ def tile_picked_wedgecv_relu_l_kernel(
 
         def cast_w2(r, z):
             by_word = staged["e", r, z][:].rearrange("p (j w t) -> p w j t", j=PACK, t=PACK)
-            front = rounded["e", z][:, r * K_PASS : (r + 1) * K_PASS].rearrange("p (t w j) -> p w j t", t=2, j=PACK)
+            front = rounded["e", z][:, r * K_PASS : (r + 1) * K_PASS].rearrange("p (w t j) -> p w j t", t=2, j=PACK)
             back = rounded["e", z][:, 2 * K_PASS :].rearrange("p (t w j) -> p w j t", t=2, j=PACK)
             nc.vector.tensor_copy(out=front, in_=by_word[:, :, :, :2])
             nc.vector.tensor_copy(out=back[:, r * WORDS : (r + 1) * WORDS], in_=by_word[:, :, :, 2:])
 
         def cast_w1(z):
-            by_word = staged["y", z].rearrange("p (j r w t) -> p r w j t", j=PACK, r=2, t=PACK)
-            front = rounded["y", z][:, : 2 * K_PASS].rearrange("p (r t w j) -> p r w j t", r=2, t=2, j=PACK)
-            back = rounded["y", z][:, 2 * K_PASS :].rearrange("p (t r w j) -> p r w j t", r=2, t=2, j=PACK)
-            nc.vector.tensor_copy(out=front, in_=by_word[:, :, :, :, :2])
-            nc.vector.tensor_copy(out=back, in_=by_word[:, :, :, :, 2:])
+            by_word = staged["y", z].rearrange("p (j w t) -> p w j t", j=PACK, t=PACK)
+            front = rounded["y", z][:, : 2 * K_PASS].rearrange("p (w t j) -> p w j t", t=2, j=PACK)
+            back = rounded["y", z][:, 2 * K_PASS :].rearrange("p (t w j) -> p w j t", t=2, j=PACK)
+            nc.vector.tensor_copy(out=front, in_=by_word[:, :, :, :2])
+            nc.vector.tensor_copy(out=back, in_=by_word[:, :, :, 2:])
 
         def one_pass(acc, label, h, z, points):
             codes, plane = operands[label, h, z]
@@ -157,14 +157,18 @@ def tile_picked_wedgecv_relu_l_kernel(
         def fresh(name, rows=1):
             return keep.tile([P, rows * T], F32, name=name)[:]
 
-        fetched = [room[:, : 4 * T], late_room[:, : 4 * T], late_room[:, 6 * T + HALF :], fresh("fetched_3", 4)]
+        fetched = [room[:, : 4 * T], rooms[0][:, : 4 * T], rooms[1][:, : 4 * T], fresh("fetched_3", 4)]
         fetched = [place.rearrange("p (d v) -> p d v", d=4) for place in fetched]
-        paired = [late_room[:, 4 * T : 6 * T], fresh("paired_1", 2)] * 2
+        paired = [rooms[z][:, 4 * T : 6 * T] for z in range(PASSES)] * 2
         paired = [place.rearrange("p (i v) -> p i v", i=2) for place in paired]
         top = [fresh(f"top_{h}") for h in range(TILES)]
         slots = keep.tile([P, PACK, T], BF16)
-        spare = keep.tile([P, T], BF16)
-        sums = [slots[:, 0, :], spare[:], slots[:, 2, :], slots[:, 3, :]]
+        undealt = [keep.tile([P, T], BF16, name=f"undealt_{h}") for h in range(2)]
+        sums = [undealt[0][:], undealt[1][:], slots[:, 2, :], slots[:, 3, :]]
+
+        def deal(h):
+            for t in range(2):
+                nc.sync.dma_start(out=slots[h * WORDS : (h + 1) * WORDS, t, :], in_=undealt[h][t:P:2, :])
         z_grouped = keep.tile([P, T, PACK], BF16, align_bytes=64)
 
         def looked_up(h, d, part):
@@ -190,11 +194,12 @@ def tile_picked_wedgecv_relu_l_kernel(
             nc.vector.tensor_tensor(sums[h][:, part], top[h][:, part], banks["y", h][:, part], ALU.add)
 
         def weave(part, on_scalar=False):
-            source = slots[:, :, part].rearrange("p t v -> p v t")
+            source = slots[:, :, part].rearrange("p t (c i) -> p c t i", i=PACK)
+            target = z_grouped[:, part, :].rearrange("p (c i) t -> p c t i", i=PACK)
             if on_scalar:
-                nc.scalar.activation(z_grouped[:, part, :], source, RELU)
+                nc.scalar.activation(target, source, RELU)
             else:
-                nc.vector.tensor_scalar_max(z_grouped[:, part, :], source, 0.0)
+                nc.vector.tensor_scalar_max(target, source, 0.0)
 
         def project(part, copy=nc.scalar.copy):
             width = part.stop - part.start
@@ -233,16 +238,21 @@ def tile_picked_wedgecv_relu_l_kernel(
         gather_on_vector(0, 3, fetched[0][:, 3, :])
         unload(1)
         gather(1, everything, (0, 1, 2))
-        for z in range(PASSES):
+
+        def prepare_y(z):
             cast_w1(z)
             quantize_tiles("y", z, 0, 2)
             quantize_tiles("y", z, 2, TILES)
             multiply("y", range(TILES), z)
+
+        prepare_y(0)
+        pair(0, everything)
         gather_on_vector(1, 3, fetched[1][:, 3, :])
+        join(0, everything)
+        prepare_y(1)
 
         unload(2)
-        gather_on_vector(2, 0, fetched[2][:, 0, :])
-        gather(2, everything, (1, 2, 3))
+        gather(2, everything, (0, 1, 2))
         unload(3)
         gather(3, halves[0])
         gather(3, halves[1], (0, 1, 2))
@@ -250,15 +260,13 @@ def tile_picked_wedgecv_relu_l_kernel(
         gather(3, pieces[2], (3,))
 
         low, high = ([paired[h][:, i, :] for h in range(TILES)] for i in range(2))
-        pair(0, everything)
         pair(1, everything)
-        join(0, everything)
-        join(1, everything)
         add(0, everything)
-        nc.sync.dma_start(out=slots[:WORDS, 1, :], in_=slots[WORDS:, 0, :])
+        deal(0)
+        join(1, everything)
+        gather_on_vector(2, 3, fetched[2][:, 3, :])
         add(1, everything)
-        nc.sync.dma_start(out=slots[WORDS:, 0, :], in_=spare[:WORDS, :])
-        nc.sync.dma_start(out=slots[WORDS:, 1, :], in_=spare[WORDS:, :])
+        deal(1)
         pair(2, everything)
         larger(low[3], fetched[3][:, 0, :], fetched[3][:, 1, :], halves[0])
         join(2, everything)
@@ -274,7 +282,7 @@ def tile_picked_wedgecv_relu_l_kernel(
         add(3, pieces[1])
         add(3, pieces[2])
         weave(pieces[1], on_scalar=True)
-        weave(pieces[2])
         project(pieces[0])
-        project(pieces[2], nc.vector.tensor_copy)
+        weave(pieces[2])
         project(pieces[1])
+        project(pieces[2], nc.vector.tensor_copy)

@@ -55,10 +55,14 @@ def tile_picked_wedgecv_relu_l_kernel(
             rows = w1[z * K_PASS : (z + 1) * K_PASS, :]
             nc.sync.dma_start(out=staged["y", z], in_=rows.rearrange("(p j) c -> p (j c)", j=PACK))
 
-        def load_scale_rows(plane, scales, queue):
-            nc.gpsimd.memset(plane[:].bitcast(I32), 0)
+        scale_rows = keep.tile([P, PASSES * T + N], U8, align_bytes=64)
+        nc.vector.memset(scale_rows[:].bitcast(I32), 0)
+        x_plane = scale_rows[:, : PASSES * T].rearrange("p (z c) -> p z c", z=PASSES)
+        w3_plane = scale_rows[:, PASSES * T :].rearrange("p (z c) -> p z c", z=1)
+
+        def load_scale_rows(plane, scales):
             for q in range(4):
-                queue.dma_start(
+                nc.sync.dma_start(
                     out=plane[32 * q : 32 * q + 4, :, :].bitcast(I32),
                     in_=scales[:, 4 * q : 4 * q + 4, :].bitcast(I32).rearrange("z r c -> r z c"),
                 )
@@ -73,7 +77,6 @@ def tile_picked_wedgecv_relu_l_kernel(
         halves = (slice(0, HALF), slice(HALF, T))
         pieces = (halves[0], slice(HALF, HALF + P), slice(HALF + P, T))
 
-        x_plane = keep.tile([P, PASSES, T], U8, align_bytes=64)
         x_codes = [keep.tile([P, T], U32, name=f"x_codes_{z}", align_bytes=64) for z in range(PASSES)]
 
         def load_x(z, points):
@@ -81,7 +84,7 @@ def tile_picked_wedgecv_relu_l_kernel(
             nc.sync.dma_start(out=x_codes[z][:, points].bitcast(I32), in_=words[:, points])
 
         load_w2(0, 0)
-        load_scale_rows(x_plane, x_scales, nc.sync)
+        load_scale_rows(x_plane, x_scales)
         load_x(0, halves[0])
         load_w2(0, 1)
         load_x(0, halves[1])
@@ -97,8 +100,7 @@ def tile_picked_wedgecv_relu_l_kernel(
             load_w1(z)
         w3_codes = keep.tile([P, N], U32, align_bytes=64)
         nc.sync.dma_start(out=w3_codes[:].bitcast(I32), in_=w3_words[0].rearrange("p c r -> p (c r)").bitcast(I32))
-        w3_plane = keep.tile([P, 1, N], U8, align_bytes=64)
-        load_scale_rows(w3_plane, w3_scales, nc.sync)
+        load_scale_rows(w3_plane, w3_scales)
 
         operands = {}
         room = keep.tile([P, 5 * T], F32, align_bytes=64)

@@ -40,9 +40,9 @@ def tile_picked_wedgecv_relu_l_kernel(
             for z in range(PASSES):
                 staged["e", r, z] = keep.tile([P, 2 * T], F32, name=f"staged_e_{r}_{z}")
         windows = [staged["e", r, z] for r in range(2) for z in range(PASSES)]
-        rooms = [keep.tile([P, 7 * T], F32, name=f"room_{z}") for z in range(PASSES)]
+        rooms = [keep.tile([P, 7 * T + z * P], F32, name=f"room_{z}") for z in range(PASSES)]
         for z in range(PASSES):
-            staged["y", z] = rooms[z][:, 3 * T :]
+            staged["y", z] = rooms[z][:, 3 * T + z * P :]
 
         def load_w2(r, z):
             rows = w2[z * K_PASS : (z + 1) * K_PASS, r * HALF : (r + 1) * HALF]
@@ -180,8 +180,8 @@ def tile_picked_wedgecv_relu_l_kernel(
             for d in which:
                 nc.scalar.activation(fetched[h][:, d, part], looked_up(h, d, part), COPY)
 
-        def gather_on_vector(h, d, target):
-            nc.vector.tensor_copy(target, looked_up(h, d, everything))
+        def gather_on_vector(h, d, part=everything):
+            nc.vector.tensor_copy(fetched[h][:, d, part], looked_up(h, d, part))
 
         def pair(h, part):
             nc.vector.tensor_tensor(paired[h][:, :, part], fetched[h][:, :2, part], fetched[h][:, 2:, part], ALU.max)
@@ -237,7 +237,7 @@ def tile_picked_wedgecv_relu_l_kernel(
             quantize_tiles("e", z, 1, 2)
             quantize_tiles("e", z, 2, TILES)
             multiply("e", (1, 2, 3), z)
-        gather_on_vector(0, 3, fetched[0][:, 3, :])
+        gather_on_vector(0, 3)
         unload(1)
         gather(1, everything, (0, 1, 2))
 
@@ -249,12 +249,13 @@ def tile_picked_wedgecv_relu_l_kernel(
 
         prepare_y(0)
         pair(0, everything)
-        gather_on_vector(1, 3, fetched[1][:, 3, :])
+        gather_on_vector(1, 3)
         join(0, everything)
         prepare_y(1)
 
         unload(2)
         gather(2, everything, (0, 1, 2))
+        gather(2, slice(0, P), (3,))
         unload(3)
         gather(3, halves[0])
         gather(3, halves[1], (0, 1, 2))
@@ -266,7 +267,7 @@ def tile_picked_wedgecv_relu_l_kernel(
         add(0, everything)
         deal(0)
         join(1, everything)
-        gather_on_vector(2, 3, fetched[2][:, 3, :])
+        gather_on_vector(2, 3, slice(P, T))
         add(1, everything)
         deal(1)
         pair(2, everything)

@@ -32,7 +32,8 @@ def tile_picked_wedgecv_relu_l_kernel(
     nc = tc.nc
     with ExitStack() as ctx:
         keep = ctx.enter_context(tc.tile_pool(name="keep", bufs=1))
-        psum_e = ctx.enter_context(tc.psum_pool(name="psum_e", bufs=4))
+        psum_e = ctx.enter_context(tc.psum_pool(name="psum_e", bufs=1))
+        psum_out = ctx.enter_context(tc.psum_pool(name="psum_out", bufs=3))
         psum_y = ctx.enter_context(tc.psum_pool(name="psum_y", bufs=4))
 
         staged = {}
@@ -84,8 +85,8 @@ def tile_picked_wedgecv_relu_l_kernel(
             nc.sync.dma_start(out=x_codes[z][:, points].bitcast(I32), in_=words[:, points])
 
         load_w2(0, 0)
-        load_scale_rows(x_plane, x_scales)
         load_x(0, halves[0])
+        load_scale_rows(x_plane, x_scales)
         load_w2(0, 1)
         load_x(0, halves[1])
         load_x(1, halves[0])
@@ -152,8 +153,10 @@ def tile_picked_wedgecv_relu_l_kernel(
         def multiply(label, tiles, z):
             for h in tiles:
                 if z == 0:
-                    pool = psum_e if label == "e" else psum_y
-                    banks[label, h] = pool.tile([P, T], F32, name=f"acc_{label}")
+                    pool, name = (psum_e, "acc_e") if label == "e" else (psum_y, "acc_y")
+                    if (label, h) == ("e", 3):
+                        pool, name = psum_out, "acc_out"
+                    banks[label, h] = pool.tile([P, T], F32, name=name)
                 one_pass(banks[label, h][:], label, h, z, everything)
 
         def fresh(name, rows=1):
@@ -206,7 +209,7 @@ def tile_picked_wedgecv_relu_l_kernel(
         def project(part, copy=nc.scalar.copy):
             width = part.stop - part.start
             codes, plane = quantize(f"z_{part.start}", z_grouped[:, part, :].rearrange("p v t -> p (v t)"), width)
-            projected = psum_e.tile([P, width], F32, name="acc_e")
+            projected = psum_out.tile([P, width], F32, name="acc_out")
             nc.tensor.matmul_mx(
                 out=projected[:],
                 lhsT=w3_codes[:].bitcast(FP8X4),
@@ -223,7 +226,7 @@ def tile_picked_wedgecv_relu_l_kernel(
         def unload(h):
             nc.scalar.copy(out=windows[h][:, :T], in_=banks["e", h][:])
 
-        first = [psum_e.tile([P, HALF], F32, name="acc_e"), psum_y.tile([P, HALF], F32, name="acc_y")]
+        first = [psum_out.tile([P, HALF], F32, name="acc_out"), psum_y.tile([P, HALF], F32, name="acc_y")]
         for z in range(PASSES):
             cast_w2(0, z)
             quantize_tiles("e", z, 0, 1)
@@ -236,7 +239,7 @@ def tile_picked_wedgecv_relu_l_kernel(
             cast_w2(1, z)
             quantize_tiles("e", z, 1, 2)
             quantize_tiles("e", z, 2, TILES)
-            multiply("e", (1, 2, 3), z)
+            multiply("e", (1, 3), z)
         gather_on_vector(0, 3)
         unload(1)
         gather(1, everything, (0, 1, 2))
@@ -253,6 +256,8 @@ def tile_picked_wedgecv_relu_l_kernel(
         join(0, everything)
         prepare_y(1)
 
+        for z in range(PASSES):
+            multiply("e", (2,), z)
         unload(2)
         gather(2, everything, (0, 1, 2))
         gather(2, slice(0, P), (3,))

from contextlib import ExitStack

import concourse.mybir as mybir

K, T, H, N = 1024, 512, 512, 128
FLOPS = 2 * (2 * K * H * T + H * N * T)

F32 = mybir.dt.float32
BF16 = mybir.dt.bfloat16
I32 = mybir.dt.int32
U32 = mybir.dt.uint32
U16 = mybir.dt.uint16
U8 = mybir.dt.uint8
FP8X4 = mybir.dt.float8_e4m3fn_x4
ALU = mybir.AluOpType
COPY = mybir.ActivationFunctionType.Copy
RELU = mybir.ActivationFunctionType.Relu

P = 128
PACK = 4
K_PASS = P * PACK
PASSES = K // K_PASS
TILES = H // P
HALF = T // 2
WORDS = P // 2
PER_COLUMN = 16


def tile_picked_wedgecv_relu_l_kernel(
    tc, x_words, x_scales, w1, w2, w3_words, w3_scales, pos1, pos2, pos3, pos4, out
):
    nc = tc.nc
    with ExitStack() as ctx:
        keep = ctx.enter_context(tc.tile_pool(name="keep", bufs=1))
        psum_e = ctx.enter_context(tc.psum_pool(name="psum_e", bufs=1))
        psum_out = ctx.enter_context(tc.psum_pool(name="psum_out", bufs=3))
        psum_y = ctx.enter_context(tc.psum_pool(name="psum_y", bufs=4))

        staged = {}
        for r in range(2):
            for z in range(PASSES):
                staged["e", r, z] = keep.tile([P, 2 * T], F32, name=f"staged_e_{r}_{z}")
        windows = [staged["e", r, z] for r in range(2) for z in range(PASSES)]
        rooms = [keep.tile([P, 7 * T + z * P], F32, name=f"room_{z}") for z in range(PASSES)]
        for z in range(PASSES):
            staged["y", z] = rooms[z][:, 3 * T + z * P :]

        def load_w2(r, z):
            rows = w2[z * K_PASS : (z + 1) * K_PASS, r * HALF : (r + 1) * HALF]
            nc.sync.dma_start(
                out=staged["e", r, z][:].rearrange("p (j c) -> p j c", j=PACK),
                in_=rows.rearrange("(p j) c -> p j c", j=PACK),
            )

        def load_w1(z):
            rows = w1[z * K_PASS : (z + 1) * K_PASS, :]
            nc.sync.dma_start(out=staged["y", z], in_=rows.rearrange("(p j) c -> p (j c)", j=PACK))

        scale_rows = keep.tile([P, PASSES * T + N], U8, align_bytes=64)
        nc.vector.memset(scale_rows[:].bitcast(I32), 0)
        x_plane = scale_rows[:, : PASSES * T].rearrange("p (z c) -> p z c", z=PASSES)
        w3_plane = scale_rows[:, PASSES * T :].rearrange("p (z c) -> p z c", z=1)

        def load_scale_rows(plane, scales):
            for q in range(4):
                nc.sync.dma_start(
                    out=plane[32 * q : 32 * q + 4, :, :].bitcast(I32),
                    in_=scales[:, 4 * q : 4 * q + 4, :].bitcast(I32).rearrange("z r c -> r z c"),
                )

        lists = {}

        def load_list(d, pos):
            lists[d] = keep.tile([P, T // PER_COLUMN], U16, name=f"list_{d}")
            nc.sync.dma_start(lists[d][:], pos)

        everything = slice(0, T)
        halves = (slice(0, HALF), slice(HALF, T))
        pieces = (halves[0], slice(HALF, HALF + P), slice(HALF + P, T))

        x_codes = [keep.tile([P, T], U32, name=f"x_codes_{z}", align_bytes=64) for z in range(PASSES)]

        def load_x(z, points):
            words = x_words[z].rearrange("p c r -> p (c r)").bitcast(I32)
            nc.sync.dma_start(out=x_codes[z][:, points].bitcast(I32), in_=words[:, points])

        load_w2(0, 0)
        load_x(0, halves[0])
        load_scale_rows(x_plane, x_scales)
        load_w2(0, 1)
        load_x(0, halves[1])
        load_x(1, halves[0])
        load_x(1, halves[1])
        load_list(0, pos1)
        load_w2(1, 0)
        load_list(1, pos2)
        load_w2(1, 1)
        load_list(2, pos3)
        load_list(3, pos4)
        for z in range(PASSES):
            load_w1(z)
        w3_codes = keep.tile([P, N], U32, align_bytes=64)
        nc.sync.dma_start(out=w3_codes[:].bitcast(I32), in_=w3_words[0].rearrange("p c r -> p (c r)").bitcast(I32))
        load_scale_rows(w3_plane, w3_scales)

        operands = {}
        room = keep.tile([P, 5 * T], F32, align_bytes=64)
        rounded = {("e", 1): room[:, 3 * T :].bitcast(BF16)}
        for key in (("e", 0), ("y", 0), ("y", 1)):
            rounded[key] = keep.tile([P, TILES * K_PASS], BF16, name="rounded_%s_%d" % key, align_bytes=64)[:]

        def quantize(name, source, width):
            codes = keep.tile([P, width], U32, name=f"codes_{name}", align_bytes=64)
            plane = keep.tile([P, width], U8, name=f"plane_{name}", align_bytes=64)
            nc.vector.quantize_mx(out=codes[:].bitcast(FP8X4), scales=plane[:], in_=source)
            return codes, plane

        def quantize_tiles(label, z, first, last):
            source = rounded[label, z][:, first * K_PASS : last * K_PASS]
            codes, plane = quantize(f"{label}_{z}_{first}", source, (last - first) * P)
            for h in range(first, last):
                cols = slice((h - first) * P, (h - first + 1) * P)
                operands[label, h, z] = (codes[:, cols], plane[:, cols])

        def cast_w2(r, z):
            by_word = staged["e", r, z][:].rearrange("p (j w t) -> p w j t", j=PACK, t=PACK)
            front = rounded["e", z][:, r * K_PASS : (r + 1) * K_PASS].rearrange("p (w t j) -> p w j t", t=2, j=PACK)
            back = rounded["e", z][:, 2 * K_PASS :].rearrange("p (t w j) -> p w j t", t=2, j=PACK)
            nc.vector.tensor_copy(out=front, in_=by_word[:, :, :, :2])
            nc.vector.tensor_copy(out=back[:, r * WORDS : (r + 1) * WORDS], in_=by_word[:, :, :, 2:])

        def cast_w1(z):
            by_word = staged["y", z].rearrange("p (j w t) -> p w j t", j=PACK, t=PACK)
            front = rounded["y", z][:, : 2 * K_PASS].rearrange("p (w t j) -> p w j t", t=2, j=PACK)
            back = rounded["y", z][:, 2 * K_PASS :].rearrange("p (t w j) -> p w j t", t=2, j=PACK)
            nc.vector.tensor_copy(out=front, in_=by_word[:, :, :, :2])
            nc.vector.tensor_copy(out=back, in_=by_word[:, :, :, 2:])

        def one_pass(acc, label, h, z, points):
            codes, plane = operands[label, h, z]
            nc.tensor.matmul_mx(
                out=acc,
                lhsT=codes.bitcast(FP8X4),
                lhsT_scale=plane,
                rhs=x_codes[z][:, points].bitcast(FP8X4),
                rhs_scale=x_plane[:, z, points],
                start=(z == 0),
                stop=(z == PASSES - 1),
            )

        banks = {}

        def multiply(label, tiles, z):
            for h in tiles:
                if z == 0:
                    pool, name = (psum_e, "acc_e") if label == "e" else (psum_y, "acc_y")
                    if (label, h) == ("e", 3):
                        pool, name = psum_out, "acc_out"
                    banks[label, h] = pool.tile([P, T], F32, name=name)
                one_pass(banks[label, h][:], label, h, z, everything)

        def fresh(name, rows=1):
            return keep.tile([P, rows * T], F32, name=name)[:]

        fetched = [room[:, : 4 * T], rooms[0][:, : 4 * T], rooms[1][:, : 4 * T], fresh("fetched_3", 4)]
        fetched = [place.rearrange("p (d v) -> p d v", d=4) for place in fetched]
        paired = [rooms[z][:, 4 * T : 6 * T] for z in range(PASSES)] * 2
        paired = [place.rearrange("p (i v) -> p i v", i=2) for place in paired]
        top = [fresh(f"top_{h}") for h in range(TILES)]
        slots = keep.tile([P, PACK, T], BF16)
        undealt = [keep.tile([P, T], BF16, name=f"undealt_{h}") for h in range(2)]
        sums = [undealt[0][:], undealt[1][:], slots[:, 2, :], slots[:, 3, :]]

        def deal(h):
            for t in range(2):
                nc.sync.dma_start(out=slots[h * WORDS : (h + 1) * WORDS, t, :], in_=undealt[h][t:P:2, :])
        z_grouped = keep.tile([P, T, PACK], BF16, align_bytes=64)

        def looked_up(h, d, part):
            return windows[h][:].indirect(lists[d][:, part.start // PER_COLUMN : part.stop // PER_COLUMN])

        def gather(h, part, which=range(4)):
            for d in which:
                nc.scalar.activation(fetched[h][:, d, part], looked_up(h, d, part), COPY)

        def gather_on_vector(h, d, part=everything):
            nc.vector.tensor_copy(fetched[h][:, d, part], looked_up(h, d, part))

        def pair(h, part):
            nc.vector.tensor_tensor(paired[h][:, :, part], fetched[h][:, :2, part], fetched[h][:, 2:, part], ALU.max)

        def larger(target, one, other, part):
            nc.vector.tensor_tensor(target[:, part], one[:, part], other[:, part], ALU.max)

        def join(h, part):
            larger(top[h], paired[h][:, 0, :], paired[h][:, 1, :], part)

        def add(h, part):
            nc.vector.tensor_tensor(sums[h][:, part], top[h][:, part], banks["y", h][:, part], ALU.add)

        def weave(part, on_scalar=False):
            source = slots[:, :, part].rearrange("p t (c i) -> p c t i", i=PACK)
            target = z_grouped[:, part, :].rearrange("p (c i) t -> p c t i", i=PACK)
            if on_scalar:
                nc.scalar.activation(target, source, RELU)
            else:
                nc.vector.tensor_scalar_max(target, source, 0.0)

        def project(part, copy=nc.scalar.copy):
            width = part.stop - part.start
            codes, plane = quantize(f"z_{part.start}", z_grouped[:, part, :].rearrange("p v t -> p (v t)"), width)
            projected = psum_out.tile([P, width], F32, name="acc_out")
            nc.tensor.matmul_mx(
                out=projected[:],
                lhsT=w3_codes[:].bitcast(FP8X4),
                lhsT_scale=w3_plane[:, 0, :],
                rhs=codes[:].bitcast(FP8X4),
                rhs_scale=plane[:],
                start=True,
                stop=True,
            )
            result = keep.tile([P, width], F32, name=f"result_{part.start}")
            copy(out=result[:], in_=projected[:])
            nc.sync.dma_start(out=out[:, part], in_=result[:])

        def unload(h):
            nc.scalar.copy(out=windows[h][:, :T], in_=banks["e", h][:])

        first = [psum_out.tile([P, HALF], F32, name="acc_out"), psum_y.tile([P, HALF], F32, name="acc_y")]
        for z in range(PASSES):
            cast_w2(0, z)
            quantize_tiles("e", z, 0, 1)
            for acc, points in zip(first, halves):
                one_pass(acc[:], "e", 0, z, points)
        for acc, points, copy in zip(first, halves, (nc.scalar.copy, nc.vector.tensor_copy)):
            copy(out=windows[0][:, points], in_=acc[:])
        gather(0, everything, (0, 1, 2))
        for z in range(PASSES):
            cast_w2(1, z)
            quantize_tiles("e", z, 1, 2)
            quantize_tiles("e", z, 2, TILES)
            multiply("e", (1, 3), z)
        gather_on_vector(0, 3)
        unload(1)
        gather(1, everything, (0, 1, 2))

        def prepare_y(z):
            cast_w1(z)
            quantize_tiles("y", z, 0, 2)
            quantize_tiles("y", z, 2, TILES)
            multiply("y", range(TILES), z)

        prepare_y(0)
        pair(0, everything)
        gather_on_vector(1, 3)
        join(0, everything)
        prepare_y(1)

        for z in range(PASSES):
            multiply("e", (2,), z)
        unload(2)
        gather(2, everything, (0, 1, 2))
        gather(2, slice(0, P), (3,))
        unload(3)
        gather(3, halves[0])
        gather(3, halves[1], (0, 1, 2))
        gather(3, pieces[1], (3,))
        gather(3, pieces[2], (3,))

        low, high = ([paired[h][:, i, :] for h in range(TILES)] for i in range(2))
        pair(1, everything)
        add(0, everything)
        deal(0)
        join(1, everything)
        gather_on_vector(2, 3, slice(P, T))
        add(1, everything)
        deal(1)
        pair(2, everything)
        larger(low[3], fetched[3][:, 0, :], fetched[3][:, 1, :], halves[0])
        join(2, everything)
        larger(high[3], low[3], fetched[3][:, 2, :], halves[0])
        add(2, everything)
        larger(top[3], high[3], fetched[3][:, 3, :], halves[0])
        larger(low[3], fetched[3][:, 0, :], fetched[3][:, 1, :], halves[1])
        add(3, halves[0])
        weave(pieces[0], on_scalar=True)
        larger(high[3], low[3], fetched[3][:, 2, :], halves[1])
        larger(top[3], high[3], fetched[3][:, 3, :], pieces[1])
        larger(top[3], high[3], fetched[3][:, 3, :], pieces[2])
        add(3, pieces[1])
        add(3, pieces[2])
        weave(pieces[1], on_scalar=True)
        project(pieces[0])
        weave(pieces[2])
        project(pieces[1])
        project(pieces[2], nc.vector.tensor_copy)
